import numpy as np, ml_dtypes
CORES = [5,29,101,125,133,157,229,253]
N = 8
BF = ml_dtypes.bfloat16
def gentries(a):
    return np.ascontiguousarray(a.reshape(8, 16, -1).transpose(0, 2, 1)).reshape(8, -1)
def gtable(e):
    e = np.asarray(e); return np.ascontiguousarray(e.reshape(8, -1, 16).transpose(0, 2, 1)).reshape(128, -1).astype(np.int32)
C, NV, LN, RO, LV = 2048, 512, 128, 3, 2
H, L, B, S = NV // 2, 2 * LN, C - LN * RO, LN // N
def parts(rng):
    o = np.argsort(rng.random((N, 8, C)), axis=-1); h = np.zeros((N, 8, C), np.int64)
    np.put_along_axis(h, o, np.broadcast_to(np.arange(C) * 256 // C, (N, 8, C)), 2)
    x = np.clip(h[:, :, None] + rng.integers(-60, 61, (N, 8, 16, C)), 0, 255)
    cen = rng.random((N, 8, NV, 1)); wd = rng.choice(np.array([0.02, 0.1, 0.3, 1.0]), (N, 8, NV, 1))
    pos = np.clip(((cen + wd * (rng.random((N, 8, NV, 16)) - 0.5)) * C).astype(np.int64), 0, C - 1)
    ring = np.take_along_axis(o, pos.reshape(N, 8, -1), 2).reshape(N, 8, NV, 16)
    ring = np.where(rng.random(ring.shape) < 0.04, C, ring)
    kid = rng.integers(0, NV, (N, 8, 2, NV)); rt = rng.integers(0, NV, (N, 8, L)); fn = rng.integers(0, C, (N, 8, LN))
    xl = np.clip(rng.integers(0, 256, (N, 8, 1, LN)) + rng.integers(-60, 61, (N, 8, 16, LN)), 0, 255)
    snd = np.argsort(rng.random((N, 8, LN)), axis=-1)
    return x, ring, kid, rt, xl, fn, snd
def plant(rng, ring, rt, fn):
    n, g, i = np.indices((N, 8, LN)); v = rt[..., LN:]; k = rng.integers(0, 16, (N, 8, LN))
    m = rng.random((N, 8, LN)) < 0.7; ring[n[m], g[m], v[m], k[m]] = fn[m]
    m = rng.random((N, 8, LN)) < 0.4; ring[n[m], g[m], v[m] ^ H, 15 - k[m]] = fn[m]
def pack(x, ring, kid, rt, xl, fn, snd):
    return {"x": np.ascontiguousarray(np.reshape(x, (N, 128, C))).astype(np.float32).astype(BF), "ring": np.ascontiguousarray(ring.transpose(0, 1, 3, 2)).reshape(N, 128, NV).astype(np.int32),
            "kid": np.ascontiguousarray(kid).reshape(N, 16, NV).astype(np.int32), "rt": np.stack([gtable(a) for a in rt]), "xl": np.reshape(xl, (N, 128, LN)).astype(np.float32).astype(BF),
            "fn": np.stack([gtable(a) for a in fn]), "snd": np.stack([gtable(a) for a in snd])}
def edge(rng, shape, top, share):
    r = rng.random(shape)
    return np.where(r < share * 0.5, 0, np.where(r < share, top, rng.integers(0, top + 1, shape)))
def halves(rng, *shape):
    k = shape[:-2] + (1, shape[-1])
    return 255 * np.where(rng.random(k) < 0.5, rng.integers(0, 2, k), rng.integers(0, 2, shape))
def swaps(rng, n, g, x, ring, rt, xl, fn, but):
    p = np.concatenate([np.array([0]), rng.permutation(np.arange(1, H - 1))[:L - 2], np.array([H - 1])])
    r = p + H * rng.integers(0, 2, L); r[0] = 0; r[L - 1] = NV - 1; rt[n, g] = r
    x[n, g, :, 0] = 255; x[n, g, :, C - 1] = 0
    hi = rng.integers(0, 2, L); xl[n, g] = 255 * hi[:LN]; fn[n, g] = np.where(hi[LN:] == 1, 0, C - 1)
    ring[n, g, r] = np.where(hi == 1, C, 0)[:, None]; ring[n, g, r ^ H] = np.where(hi == 1, 0, C)[:, None]
    if but: ring[n, g, r[L // 2] ^ H] = ring[n, g, r[L // 2]].copy()
def again(rng, n, g, x, ring, kid, rt, xl, fn, snd):
    o = rng.permutation(H); r = o[:L] + H * rng.integers(0, 2, L); rt[n, g] = r; i = np.arange(LN); h = LN // 2
    gap = np.array([2, L - 2, L, L, L + 2, 2 * L])
    x[n, g, :, 0] = 255; x[n, g, :, 1:7] = (2040 + gap[None, :] // 2 + np.arange(16)[:, None]) // 16
    xl[n, g] = 255; fn[n, g] = np.where(i < h, 0, 1 + i % 6); snd[n, g, :S] = h + np.arange(S)
    good = np.concatenate([np.zeros(LN, np.int64), fn[n, g]])[:, None]
    ring[n, g, r] = C; ring[n, g, r ^ H] = good
    if LV == 2: kid[n, g][:, r] = r ^ H
    else:
        q = o[L:2 * L] + H * rng.integers(0, 2, L); ring[n, g, q] = C; ring[n, g, q ^ H] = good
        kid[n, g][:, r] = q; kid[n, g][:, q] = r ^ H
def setup_inputs(rng):
    x, ring, kid, rt, xl, fn, snd = parts(rng); plant(rng, ring, rt, fn)
    return pack(x, ring, kid, rt, xl, fn, snd)
def setup_inputs_spread(rng):
    x, ring, kid, rt, xl, fn, snd = parts(rng)
    x = np.minimum(np.exp2(8 * rng.random((N, 8, 1, C))) * rng.random((N, 8, 16, C)), 255).astype(np.int64)
    xl = np.minimum(np.exp2(8 * rng.random((N, 8, 1, LN))) * rng.random((N, 8, 16, LN)), 255).astype(np.int64)
    ring = rng.integers(0, C + 1, ring.shape); plant(rng, ring, rt, fn)
    return pack(x, ring, kid, rt, xl, fn, snd)
def setup_inputs_ends(rng):
    x, ring, kid, rt, xl, fn, snd = parts(rng)
    x = halves(rng, N, 8, 16, C); xl = halves(rng, N, 8, 16, LN); x[:, ::2, :, 0] = 255
    ring = edge(rng, ring.shape, C, 0.64); ring[:, :, 5::16, :15] = C; ring[:, :, 5::16, 15] = 0; ring[:, :, 10::16, :15] = 0; ring[:, :, 10::16, 15] = C
    kid = edge(rng, kid.shape, NV - 1, 0.66); rt = edge(rng, rt.shape, NV - 1, 0.9); snd = edge(rng, snd.shape, LN - 1, 0.7)
    fn = (C - 1) * rng.integers(0, 2, fn.shape)
    for n in range(N):
        for g in (3, 7): swaps(rng, n, g, x, ring, rt, xl, fn, False)
    return pack(x, ring, kid, rt, xl, fn, snd)
def setup_inputs_corners(rng):
    x, ring, kid, rt, xl, fn, snd = parts(rng); plant(rng, ring, rt, fn); node = np.arange(NV)
    for n in range(N):
        s = int(rng.integers(0, 8))
        for g in range(8):
            m = (g + s) % 8
            if m == 0: ring[n, g] = C
            if m == 1: ring[n, g] = ring[n, g, :, :1].copy(); ring[n, g, rt[n, g, LN:]] = fn[n, g][:, None]
            if m == 2: kid[n, g] = node; rt[n, g] = rng.permutation(H)[:L] + H * rng.integers(0, 2, L); ring[n, g, rt[n, g]] = rng.permutation(C)[:L, None]
            if m == 3: kid[n, g] = node ^ H
            if m == 4: kid[n, g, 0] = (node + 1) % NV; kid[n, g, 1] = NV - 1; rt[n, g, ::4] = NV - 1; rt[n, g, 1::4] = 0
            if m == 5: ring[n, g] = rng.integers(B, C, (NV, 16)); fn[n, g] = rng.integers(B, B + LN, LN)
            if m == 6: rt[n, g] = rng.choice(np.array([0, H - 1, H, NV - 1]), L); kid[n, g] = (NV - 1) * rng.integers(0, 2, (2, NV))
            if m == 7: snd[n, g] = (LN - 1) * (n % 2); fn[n, g] = rng.integers(0, C)
    return pack(x, ring, kid, rt, xl, fn, snd)
def setup_inputs_crowd(rng):
    x, ring, kid, rt, xl, fn, snd = parts(rng); plant(rng, ring, rt, fn)
    for n in range(N):
        s = int(rng.integers(0, 8))
        for g in range(8):
            m = (g + s) % 8; v = int(rng.integers(0, NV)); c = int(rng.integers(0, C))
            if m == 0: again(rng, n, g, x, ring, kid, rt, xl, fn, snd)
            if m == 1: swaps(rng, n, g, x, ring, rt, xl, fn, True)
            if m == 2: rt[n, g] = v
            if m == 3: rt[n, g] = v; rt[n, g, L - 1] = (v + 1) % NV
            if m == 4: rt[n, g] = v ^ (H * rng.integers(0, 2, L))
            if m == 5: ring[n, g] = c
            if m == 6: ring[n, g] = c; rt[n, g, 0] = v; ring[n, g, v] = (c + 1) % C; rt[n, g, 1:] = np.where(rt[n, g, 1:] == v, (v + 1) % NV, rt[n, g, 1:])
            if m == 7: rt[n, g] = v; kid[n, g] = rng.integers(0, NV); fn[n, g] = c; ring[n, g, v, ::2] = c; snd[n, g] = rng.integers(0, LN)
    return pack(x, ring, kid, rt, xl, fn, snd)
def setup_inputs_ties(rng):
    x, ring, kid, rt, xl, fn, snd = parts(rng)
    b = rng.choice(np.array([0, 100, 252]), (N, 8, 1, 1)); s = rng.choice(np.array([1, 2, 3]), (N, 8, 1, 1))
    x = b + s * rng.integers(0, 2, x.shape); xl = b + s * rng.integers(0, 2, xl.shape)
    q = rng.choice(np.array([1, 2, 3, 16]), (N, 8, NV, 1)); ring = np.take_along_axis(ring, rng.integers(0, 16, ring.shape) % q, 3)
    pool = rng.integers(0, NV, (N, 4, 12)); rt[:, ::2] = np.take_along_axis(pool, rng.integers(0, 12, (N, 4, L)), 2)
    plant(rng, ring, rt, fn)
    return pack(x, ring, kid, rt, xl, fn, snd)
def check_inputs(d):
    bad = []
    for k, lo, hi in (("x", 0, 255), ("ring", 0, C), ("kid", 0, NV - 1), ("rt", 0, NV - 1), ("xl", 0, 255), ("fn", 0, C - 1), ("snd", 0, LN - 1)):
        a = np.asarray(d[k]).astype(np.float64)
        if not (np.min(a) >= lo and np.max(a) <= hi): bad.append("range of " + k)
        elif np.any(a != np.floor(a)): bad.append("whole numbers in " + k)
    return bad
def first(key, on):
    low = np.arange(L)[:, None] > np.arange(L)[None, :]
    return on & ~np.any((key[..., :, None] == key[..., None, :]) & on[..., None, :] & low, axis=-1)
def reference(x, ring, kid, rt, xl, fn, snd):
    X = np.zeros((N, 8, 16, C + 1), np.int32); X[..., :C] = x.astype(np.float32).astype(np.int32).reshape(N, 8, 16, C)
    R = ring.astype(np.int32).reshape(N, 8, 16, NV); K = kid.astype(np.int32).reshape(N, 8, 2, NV)
    st = np.stack([gentries(a) for a in rt]).astype(np.int64).reshape(N, 8, 2, LN); to = np.stack([gentries(a) for a in snd]).astype(np.int64)
    fname = np.stack([gentries(a) for a in fn]).astype(np.int64); come = xl.astype(np.float32).astype(np.int32).reshape(N, 8, 16, LN)
    A = np.zeros((N, 8, 1), np.int64)
    for t in range(RO):
        p0 = B + LN * t; X[..., p0:p0 + LN] = come
        lname = np.broadcast_to(p0 + np.arange(LN), (N, 8, LN)); name = np.concatenate([lname, fname], axis=2)
        w = np.take_along_axis(X, name[:, :, None, :], 3)
        v = np.concatenate([st[:, :, t & 1], st[:, :, (t + 1) & 1]], axis=2); new = np.zeros((N, 8, NV), bool)
        for l in range(LV):
            u = v ^ H
            rv = np.take_along_axis(R, v[:, :, None, :], 3); ru = np.take_along_axis(R, u[:, :, None, :], 3)
            z = np.take_along_axis(X, rv.reshape(N, 8, 1, 16 * L), 3).reshape(N, 8, 16, 16, L)
            zu = np.take_along_axis(X, ru.reshape(N, 8, 1, 16 * L), 3).reshape(N, 8, 16, 16, L)
            m = (np.max(z, axis=3) + np.min(z, axis=3)) >> 1; mu = (np.max(zu, axis=3) + np.min(zu, axis=3)) >> 1
            near = np.argmin(np.add.reduce(np.abs(z - w[:, :, :, None, :]), axis=2), axis=2)
            c = np.take_along_axis(rv, near[:, :, None, :], 2)[:, :, 0]
            dv = np.add.reduce(np.abs(w - m), axis=2); du = np.add.reduce(np.abs(w - mu), axis=2)
            b = np.count_nonzero(w >= m, axis=2) >= 9
            act = first(v & (H - 1), np.ones((N, 8, L), bool)); ex = act & (du + A < dv)
            kv = np.take_along_axis(K, v[:, :, None, :], 3); nxt = np.where(b, kv[:, :, 1], kv[:, :, 0]).astype(np.int64)
            n, g, j = np.nonzero(first(c, c < C)); a = c[n, g, j]
            X[n, g, :, a] = (X[n, g, :, a] + w[n, g, :, j]) >> 1
            n, g, j = np.nonzero(ex); a = v[n, g, j]; e = u[n, g, j]
            R[n, g, :, a] = ru[n, g, :, j]; R[n, g, :, e] = rv[n, g, :, j]
            ka = K[n, g, :, a].copy(); ke = K[n, g, :, e].copy(); K[n, g, :, a] = ke; K[n, g, :, e] = ka
            new[n, g, a] = True; new[n, g, e] = True
            n, g, j = np.nonzero(act[..., :LN]); R[n, g, (j + t) & 15, v[n, g, j]] = p0 + j
            n, g, j = np.nonzero(act[..., LN:]); j = j + LN; a = v[n, g, j]; col = R[n, g, :, a]
            R[n, g, :, a] = np.where((col == name[n, g, j][:, None]) & ~new[n, g, a][:, None], C, col)
            A = np.count_nonzero(ex, axis=2)[..., None]
            if l < LV - 1: v = nxt
        if t < RO - 1:
            gone = np.take_along_axis(X, fname[:, :, None, :], 3); come = np.zeros((N, 8, 16, LN), np.int32)
            for q in range(N):
                for d in range(N): come[(q + d) % N, :, :, d * S:d * S + S] = np.take_along_axis(gone[q], to[q][:, None, d * S:d * S + S], 2)
            fname = lname
    return {"yx": X[..., :C].astype(np.float32).astype(BF).reshape(N, 128, C), "yr": R.reshape(N, 128, NV).astype(np.float32), "yk": K.reshape(N, 16, NV).astype(np.float32)}

@@ -1,0 +1,708 @@
+from concourse.bass import DstId, RemoteDMATransfer
+from concourse.mybir import AluOpType as OP, AxisListType as AX, ActivationFunctionType as AF
+
+C, NV, LN, RO, N = 2048, 512, 128, 3, 8
+B0 = C - LN * RO
+MAGIC = 12582912.0
+XD, XN = 2064, 2320
+BF, F32, I32, U16, F16 = "bfloat16", "float32", "int32", "uint16", "float16"
+SB = {
+    "X0": (XN, BF), "X1": (XN, BF), "RI": (512, I32), "RW": (768, F32), "SW": (512, F32), "NT": (256, F32), "KI": (512, I32), "KF": (512, F32),
+    "NI": (2048, F32), "RT": (16, I32), "FNi": (8, I32), "SNi": (8, I32), "FNu": (8, U16), "SNu": (8, U16),
+    "CM0": (128, BF), "CM1": (128, BF), "CM2": (128, BF), "GO0": (128, BF), "GO1": (128, BF), "G1": (128, BF), "HL0": (128, BF), "HL1": (128, BF),
+    "IOT": (128, BF), "X16": (256, BF), "PI": (8, I32), "PJ": (16, I32), "CF": (32, F32), "ID": (128, BF), "H5": (128, BF), "NG": (128, BF),
+    "QI": (128, BF), "MI": (128, BF), "BO": (128, BF), "G16": (128, BF), "I16": (16, F32), "I16b": (16, BF), "ONE": (256, BF), "KC": (256, BF),
+    "RB": (512, BF), "MK": (512, BF), "SEL": (2048, BF), "BC": (2048, BF), "SELW": (512, BF), "JQ": (16, F32), "WT": (16, BF), "THR": (16, F32),
+    "IC": (16, I32), "CIu": (16, U16), "PMu": (16, U16), "ADG": (32, F32), "DUM": (48, F32), "DMX": (16, F32),
+    "Z": (4096, BF), "ZU": (4096, BF), "MXV": (4096, BF), "MNV": (4096, BF), "MXU": (4096, BF), "MNU": (4096, BF), "AB": (4096, BF),
+    "RU": (512, U16), "WJ": (256, BF), "WN": (256, BF), "WTT": (256, BF), "KS": (256, F32), "K1": (32, I32), "KB": (16, BF), "OH": (256, BF),
+    "PRD": (256, F16), "CI": (48, I32), "CU": (48, U16), "CD": (32, BF), "OAc": (2048, BF), "OBc": (2048, BF), "TWc": (144, BF), "HMc": (256, BF),
+    "RDc": (256, BF), "DL": (48, F32), "XU": (16, U16), "XC": (256, BF), "NW": (256, BF),
+    "QI2": (32, I32), "QU": (32, U16), "QD": (32, BF), "OAp": (2048, BF), "OBp": (256, BF), "TWp": (16, BF), "HMp": (256, BF), "RDp": (256, BF),
+    "EV": (256, BF), "EU": (256, BF), "LE": (256, BF), "SB_": (256, BF), "KP": (256, F16), "NS": (256, BF), "NP": (256, BF), "SP": (16, F32),
+    "TT": (32, F32), "LF": (64, F32), "LP": (32, U16), "LQ": (32, U16), "AC": (8, F32), "AP_": (16, F32), "TH": (16, F32), "OK": (16, F32),
+    "BS": (32, F32), "DT": (32, F32), "EX": (32, BF), "LT": (64, F32), "LU": (32, U16), "RD": (256, F32), "AD": (256, F32), "KE": (144, F32),
+    "EQ": (144, F32), "JK2": (144, F32), "NF": (128, F32), "N0": (128, F32), "N1": (128, F32), "N2": (128, F32), "JK": (16, F32), "U32": (64, F32), "VV": (64, F32), "RO_": (512, F32), "KO": (512, F32), "FU": (32, U16),
+}
+for _s in "EON":
+    SB.update({"vi" + _s: (64, I32), "pr" + _s: (32, F32), "sg" + _s: (32, F32), "pu" + _s: (16, U16), "ac" + _s: (16, F32)})
+PS = ["PD0", "PD1", "PK", "PM", "PN", "PA", "PB", "PC"]
+OWN = ("X0", "X1", "RI", "KI", "RT", "FNi", "SNi", "SNu", "CM0", "CM1", "CM2", "GO0", "GO1", "HL0", "HL1", "RO_", "KO", "U32", "AC")
+SCRATCH = {k: ("sbuf", [128, SB[k][0]], SB[k][1]) for k in OWN}
+AT = {k: (k, 0) for k in list(OWN) + PS}
+_fill = {}
+for _k, (_w, _d) in SB.items():
+    if _k not in OWN:
+        AT[_k] = ("all_" + _d, _fill.get(_d, 0)); _fill[_d] = _fill.get(_d, 0) + (_w + 15) // 16 * 16
+SCRATCH.update({"all_" + d: ("sbuf", [128, w], d) for d, w in _fill.items()})
+SCRATCH.update({k: ("psum", [128, 512], F32) for k in PS})
+DMAS = ["dx0", "dx1", "dring", "dkid", "drt", "dfn", "dsn", "dxl", "ox0", "ox1", "oyr", "oyk"] + ["dc%d" % k for k in range(2 * RO)]
+SEMAPHORES = ["ev", "es", "et", "ep", "arr0", "arr1", "hin0", "hin1", "loc"] + DMAS
+TUNE = {"z": [[(e, 1) for e in "svsvsvsv"]] * 2, "u": [[("s", 2, int(k >= 6)) for k in range(8)]] * 2,
+        "others": [(1.15, 2.0), (2.0, 5.5)], "seed": 1, "tries": 3000, "G": 1.56, "S": 3.8, "same": 70, "cross": 140, "far": 5000,
+        "look": 40, "rest": 4, "head": "PJ CF VV U32 viE sgE prE TT LF LP RW X0 CM0 FNi FNu",
+        "early": "PMu KI BO I16 BC JQ WT SW NT ID SELW",
+        "late": "QI2 QD QU OBp OAp RDp HMp TWp acE viO sgO prO puO SNu KF DUM BS DMX LQ puE TWc THR ADG CIu I16b AC KE EQ JK2",
+        "first": ["EX LU SW NS RW LP CM1 CM2 X0 X1 WJ WN WTT G1 GO0 GO1", "KS K1 KB OH PRD CI CD CU OAc OBc TWc RDc DL XU HMc XC NW", "RU AB Z", "MXV MNV EV", "",
+                  "EU ZU MXU MNU"]}
+
+
+def V(name, lo=0, hi=None, step=1):
+    return (name, lo, (512 if name in PS else SB[name][0]) if hi is None else hi, step)
+
+
+def IND(win, off):
+    return ("@", win, off)
+
+
+def cols(v):
+    return 16 * cols(v[2]) if v[0] == "@" else (v[2] - v[1] + v[3] - 1) // v[3]
+
+
+def ap(T, v):
+    if not isinstance(v, tuple):
+        return v
+    if v[0] == "@":
+        return ap(T, v[1]).indirect(ap(T, v[2]))
+    b, o = AT[v[0]]; p = slice(*v[4]) if len(v) > 4 else slice(None)
+    return T[b][p, o + v[1]:o + v[2]:v[3]] if v[3] != 1 else T[b][p, o + v[1]:o + v[2]]
+
+
+def build():
+    ops = []; lv = [-1]
+
+    def add(eng, fn, outs, ins, cost, grp=None, sem=None, n=1, lat=0, pre=None):
+        R, W = [], []
+        for v in ins:
+            if isinstance(v, tuple):
+                R += [v[1], v[2]] if v[0] == "@" else [v]
+        for v in outs:
+            if v[0] == "@":
+                W.append(v[1]); R.append(v[2])
+            else:
+                W.append(v)
+        ops.append({"e": eng, "f": fn, "R": R, "W": W, "c": cost, "g": grp, "sem": sem, "n": n, "lat": lat, "pre": pre, "x": [], "lv": lv[0]})
+        return len(ops) - 1
+
+    def two(*vs):
+        return all(v[0] in SB and SB[v[0]][1] in (BF, U16, F16) for v in vs)
+
+    def vc(o, a, f):
+        if o[0] == "@":
+            return 50 + TUNE["S"] * cols(o)
+        if a[0] == "@":
+            return 50 + TUNE["G"] * cols(a)
+        return max(64, f * cols(a))
+
+    def cp(o, a, pre=None):
+        return add("v", lambda q, T, x: q.tensor_copy(ap(T, o), ap(T, a)), [o], [a], vc(o, a, 0.5 if "@" not in (o[0], a[0]) and two(o, a) else 1), pre=pre)
+
+    def tt(o, a, b, op):
+        add("v", lambda q, T, x: q.tensor_tensor(ap(T, o), ap(T, a), ap(T, b), op), [o], [a, b], vc(o, a, 1 if a[0] in PS or b[0] in PS else 2))
+
+    def ts(o, a, s1, op0, s2=None, op1=None):
+        def f(q, T, x):
+            if op1 is None:
+                return q.tensor_scalar(ap(T, o), ap(T, a), ap(T, s1), None, op0)
+            return q.tensor_scalar(ap(T, o), ap(T, a), ap(T, s1), ap(T, s2), op0, op1)
+        add("v", f, [o], [a, s1, s2], vc(o, a, 0.5 if two(o, a) else 1))
+
+    def ms(o, c):
+        add("v", lambda q, T, x: q.memset(ap(T, o), c), [o], [], max(64, cols(o) * (0.5 if two(o) else 1)))
+
+    def scan(o, d0, d1, op0, op1):
+        add("v", lambda q, T, x: q.tensor_tensor_scan(ap(T, o), ap(T, d0), ap(T, d1), 0.0, op0, op1), [o], [d0, d1], max(64, cols(o) * (0.5 if two(o, d0, d1) else 1)))
+
+    def act(o, a, fn, bias=0.0, scale=1.0, total=None):
+        add("s", lambda q, T, x: q.activation(ap(T, o), ap(T, a), fn) if o[0] == "@" else
+            q.activation(ap(T, o), ap(T, a), fn, bias=ap(T, bias), scale=ap(T, scale), accum_out=ap(T, total)),
+            [o] + ([total] if total else []), [a, bias, scale],
+            (65 + TUNE["G"] * cols(a) if a[0] == "@" else 65 + TUNE["S"] * cols(a) if o[0] == "@" else max(64, 30 + cols(a))) + (1300 if fn == AF.Exp else 0))
+
+    def mm(ms_, grp=None):
+        def f(q, T, x):
+            for o, l, r, s0, s1 in ms_:
+                i = q.matmul(ap(T, o), ap(T, l), ap(T, r), s0, s1)
+            return i
+        add("t", f, [m[0] for m in ms_], [m[1] for m in ms_] + [m[2] for m in ms_], 60 + sum(0.45 * max(64, cols(m[2])) for m in ms_), grp)
+
+    def acc(o, pairs):
+        mm([(o, l, r, k == 0, k == len(pairs) - 1) for k, (l, r) in enumerate(pairs)])
+
+    def sel(a):
+        return V("SEL", 128 * a, 128 * a + 128)
+
+    def blocks(o, f, lo=0):
+        acc(o, [(sel(a), V(f, lo + 16 * a, lo + 16 * a + 16)) for a in range(16)])
+
+    def comb(o, f):
+        acc(o, [(sel(a), V(f, a, 256, 16)) for a in range(16)])
+
+    def iota(o, pat, base, cm):
+        small = SB[o[0]][1] != I32
+        add("p", lambda q, T, x: q.iota(ap(T, o), pat, base, cm, allow_small_or_imprecise_dtypes=True) if small else q.iota(ap(T, o), pat, base, cm),
+            [o], [], 130 + 2 * cols(o))
+
+    def dma(eng, sem, pairs, outs, ins, lat):
+        def f(q, T, x):
+            for o, a in pairs(T):
+                q.dma_start(o, a).then_inc(T.sem[sem], 16)
+        add(eng, f, outs, ins, 60, sem=sem, n=0, lat=lat)
+        return ops[-1]
+
+    def col(k):
+        return V("CF", k, k + 1)
+
+    dma("y", "drt", lambda T: [(T.RT[:, :], T.rt[:, :])], [V("RT")], [], 2000)["n"] = 16
+    dma("y", "dring", lambda T: [(T.RI[:, :], T.ring[:, :])], [V("RI")], [], 2600)["n"] = 16
+    dma("s", "dx0", lambda T: [(T.X0[:, 0:1024], T.x[:, 0:1024])], [V("X0", 0, 1024)], [], 3500)["n"] = 16
+    dma("y", "dx1", lambda T: [(T.X0[:, 1024:2048], T.x[:, 1024:2048])], [V("X0", 1024, 2048)], [], 3700)["n"] = 16
+    dma("s", "dxl", lambda T: [(T.CM0[:, :], T.xl[:, :])], [V("CM0")], [], 2500)["n"] = 16
+    dma("s", "dfn", lambda T: [(T.FNi[:, :], T.fn[:, :])], [V("FNi")], [], 2500)["n"] = 16
+    dma("y", "dsn", lambda T: [(T.SNi[:, :], T.snd[:, :])], [V("SNi")], [], 2500)["n"] = 16
+    ms(V("KI"), 0)
+    dma("y", "dkid", lambda T: [(T.KI[r:128:16, :], T.kid[r:16:2, :]) for r in range(2)], [V("KI")], [], 3000)["n"] = 32
+    iota(V("PI", 0, 4), [[-1, 4]], 16, 1)
+    iota(V("PI", 4, 6), [[0, 2]], 0, 1)
+    iota(V("IOT"), [[1, 128]], 0, 0)
+    iota(V("IC"), [[1, 16]], 0, 0)
+    iota(V("G16"), [[16, 8], [0, 16]], 0, 0)
+    iota(V("X16"), [[0, 16], [1, 16]], 0, 0)
+    iota(V("JQ"), [[16, 16]], 0, 1)
+    iota(V("SELW"), [[1, 32], [0, 16]], 0, 0)
+    iota(V("SEL"), [[-1, 16], [32, 8], [1, 16]], 0, 0)
+    iota(V("NI"), [[1, 2048]], 0, 0)
+    ts(V("PJ", 0, 3), V("PI", 0, 3), 15, OP.bitwise_and)
+    ts(V("PJ", 3, 4), V("PI", 0, 1), 16, OP.bitwise_and)
+    ts(V("PJ", 4, 5), V("PI", 0, 1), 1, OP.bitwise_and)
+    ts(V("PJ", 5, 6), V("PI", 4, 5), 31, OP.bitwise_and)
+    cp(V("CF", 0, 3), V("PJ", 0, 3))
+    ts(col(3), V("PI", 0, 1), -16.0, OP.add)
+    tt(col(4), col(3), col(0), OP.subtract)
+    ts(col(5), V("PJ", 3, 4), 1.0 / 16, OP.mult)
+    ts(col(6), col(5), -1.0, OP.mult, 1.0, OP.add)
+    cp(col(7), V("PJ", 5, 6))
+    ts(col(8), col(4), 2.0, OP.mult)
+    ts(col(9), V("PJ", 4, 5), 2.0, OP.mult, -1.0, OP.add)
+    ts(col(10), col(9), 8.5, OP.mult)
+    ts(col(11), col(0), 16.0, OP.mult)
+    ms(col(12), -MAGIC)
+    ms(col(13), 64.0)
+    for nm, c in (("ID", 1.0), ("H5", 0.5), ("NG", -1.0), ("QI", -0.25), ("MI", MAGIC)):
+        ts(V(nm), V("IOT"), col(3), OP.is_equal, c, OP.mult)
+    ts(V("BO"), V("G16"), col(4), OP.is_equal)
+    ts(V("I16"), V("IOT", 0, 16), col(0), OP.is_equal)
+    cp(V("I16b"), V("I16"))
+    ms(V("ONE"), 1.0)
+    ts(V("KC"), V("X16"), 1.0 / 16, OP.mult)
+    ms(V("RB"), 0.0); ms(V("RB", 0, 512, 16), 8192.0)
+    ms(V("MK"), 1.0); ms(V("MK", 0, 512, 16), 0.0)
+    ts(V("SEL"), V("SEL"), col(8), OP.is_equal)
+    for a in range(16):
+        act(V("BC", 128 * a, 128 * a + 128), V("BO"), AF.Copy, scale=V("I16", a, a + 1))
+    ts(V("SELW"), V("SELW"), col(7), OP.is_equal, -1.0, OP.mult)
+    ts(V("JQ"), V("JQ"), col(4), OP.subtract)
+    act(V("WT"), V("JQ"), AF.Exp, bias=col(13), scale=-0.5596)
+    ts(V("THR"), V("WT"), 2.54, OP.mult)
+    cp(V("CIu"), V("IC"))
+    ts(V("PMu"), V("IC"), col(11), OP.add)
+    ts(V("ADG", 0, 16), V("IC"), 0.0, OP.mult, col(4), OP.add); ms(V("ADG", 16, 32), 0.0)
+    ts(V("DUM", 0, 16), V("JQ"), 256.0, OP.add); ts(V("DUM", 16, 32), V("JQ"), 512.0, OP.add)
+    cp(V("BS", 0, 16), V("DUM", 0, 16))
+    ts(V("DMX"), V("JQ"), float(XD), OP.add)
+    ms(V("TWc", 128, 144), 5e29)
+    ts(V("DUM", 32, 48), V("JQ"), 384.0, OP.add)
+    ms(V("X0", 2048, XD), 0.0)
+    ms(V("RW", 512, 768), 0.0)
+    ms(V("NT"), -16.0); ms(V("NS"), -16.0)
+    act(V("SW", 0, 256), V("NT"), AF.Tanh, scale=-1.0)
+    ops[-1]["c"] += 1500; ops[-1]["R"].append(V("WT"))
+    ts(V("RW", 0, 512), V("RI"), 1.0 / C, OP.mult)
+    ms(col(14), -512.0)
+    for t in range(RO):
+        ms(col(15 + t), (B0 + LN * t - t) / C)
+    ts(V("KE"), V("X16", 0, 144), col(0), OP.not_equal)
+    act(V("JK2"), V("KE"), AF.Identity, scale=-8192.0)
+    tt(V("EQ"), V("JK2"), V("NI", 0, 144), OP.add)
+    cp(V("FNu"), V("FNi"))
+    for d in range(N):
+        add("v", lambda q, T, x, d=d: q.tensor_copy(T.SNu[:, d:d + 1], T.SNi[:, x["order"][d]:x["order"][d] + 1]), [V("SNu", d, d + 1)], [V("SNi")], 64)
+    cp(V("KF"), V("KI"))
+
+    def lowest(key, s, wide, bank):
+        ci, cu, cd, o = (("CI", "CU", "CD", 16) if wide else ("QI2", "QU", "QD", 0))
+        ts(V(ci, o, o + 16), key, 15, OP.bitwise_and)
+        ts(V(ci, o + 16, o + 32), key, 4, OP.arith_shift_right)
+        tt(V(cd), V(ci, o, o + 32), V("ADG"), OP.add)
+        cp(V(cu), V(ci))
+        w = 128 if wide else 16
+        if not wide:
+            tt(V("OBp"), IND(V(cd, 16, 32), V("CIu")), V("X16"), OP.is_equal)
+        gid = ("T", len(ops))
+        for i in range(16):
+            ts(V("OA" + s, 128 * i, 128 * i + 128), V("IOT"), V(cd, i, i + 1), OP.is_equal, V("WT", i, i + 1), OP.mult)
+            if wide:
+                ts(V("OBc", 128 * i, 128 * i + 128), V("IOT"), V(cd, 16 + i, 17 + i), OP.is_equal)
+            if i % 4 == 3:
+                mm([(V(bank, 128, 128 + w), V("OA" + s, 128 * k, 128 * k + 128), V("OB" + s, w * k, w * k + w), k == 0, k == 15) for k in range(i - 3, i + 1)], gid)
+        act(V("HM" + s), IND(V("I16b"), V(cu, o, o + 16)), AF.Identity)
+        act(V("TW" + s, 0, w), V(bank, 128, 128 + w), AF.Identity)
+        tt(V("RD" + s), IND(V("TW" + s), V(cu, o + 16, o + 32)), V("HM" + s), OP.mult)
+        comb(V(bank, 0, 16), "RD" + s)
+
+    def nodes(s, v):
+        cp(V("vi" + s, 0, 32), v)
+        ts(V("sg" + s), v, 256.0, OP.is_ge, -0.5, OP.add)
+        ts(V("vi" + s, 32, 64), V("vi" + s, 0, 32), 255, OP.bitwise_and)
+        cp(V("pu" + s), V("vi" + s, 48, 64))
+        ts(V("pr" + s), V("vi" + s, 32, 64), 128.0, OP.add)
+
+    def acting(s, bank):
+        lowest(V("vi" + s, 48, 64), "p", False, bank)
+        tt(V("ac" + s), V(bank, 0, 16), V("THR"), OP.is_lt)
+
+    def places(s, first):
+        for h, L in ((0, "LP"), (1, "LQ")):
+            t = V("TT", 16 * h, 16 * h + 16); sg = V("sg" + s, 16 * h, 16 * h + 16); pr = V("pr" + s, 16 * h, 16 * h + 16)
+            if first:
+                ts(t, sg, -256.0, OP.mult)
+            else:
+                if h == 0:
+                    blocks(V("PA", 0, 16), "NS")
+                else:
+                    comb(V("PB", 16, 32), "NS")
+                tt(t, V("PB" if h else "PA", 16 * h, 16 * h + 16), sg, OP.mult)
+            tt(V("LF", 32 * h, 32 * h + 16), pr, t, OP.subtract)
+            if h == 0:
+                tt(V("LF", 16, 32), pr, t, OP.add)
+                cp(V("LP"), V("LF", 0, 32))
+            else:
+                cp(V("LQ", 0, 8), V("LF", 40, 48))
+            if h == 1 and s == "N":
+                tt(V("OK", 8, 16), V("PB", 24, 32), V("SP", 8, 16), OP.is_equal)
+
+    for s, o in (("E", 0), ("O", 8)):
+        cp(V("VV", 16, 24), V("RT", o, o + 8)); cp(V("VV", 24, 32), V("RT", 8 - o, 16 - o))
+        ts(V("U32", 0, 16), V("VV", 16, 32), col(5), OP.mult); ts(V("U32", 16, 32), V("VV", 16, 32), col(6), OP.mult)
+        add("v", lambda q, T, x: q.transpose(T.U32[:, 32:64], T.U32[:, 0:32]), [V("U32", 32, 64)], [V("U32", 0, 32)], 64)
+        tt(V("VV", 0, 16), V("U32", 32, 48), V("U32", 48, 64), OP.add)
+        nodes(s, V("VV", 0, 32))
+        if s == "E":
+            places("E", True)
+    ms(V("AC", 0, 1), -8192.0)
+    acting("E", "PB")
+
+    def gather(eng, o, a):
+        if eng == "v":
+            cp(o, a)
+        else:
+            act(o, a, AF.Identity)
+
+    def middle(mx, mn, lo, hi, bank):
+        o = V(bank, lo, hi)
+        acc(o, [(V("H5"), V(mx, 16 * lo + 15, 16 * hi, 16)), (V("H5"), V(mn, 16 * lo + 15, 16 * hi, 16)), (V("NG"), V("WN", lo, hi)),
+                (V("QI"), V("ONE", lo, hi)), (V("MI"), V("ONE", lo, hi))])
+
+    send = None
+    for t in range(RO):
+        p0 = B0 + LN * t
+        cm = "CM%d" % t
+        for l in range(2):
+            s = "N" if l else "EO"[t & 1]
+            last = t == RO - 1 and l == 1
+            lv[0] = 2 * t + l
+            xa, xb = "X%d" % l, "X%d" % (1 - l)
+            XA, XB, RA = V(xa, 0, XD), V(xb), V("RW")
+            ts(V("RU", 0, 256), IND(RA, V("LP", 0, 16)), float(C), OP.mult)
+            ts(V("RU", 256, 512), IND(RA, V("LP", 16, 32)), float(C), OP.mult)
+            if l == 0:
+                k = cp(V(xa, p0, p0 + LN), V(cm), pre=("arr%d" % (t - 1) if t else None))
+                if t:
+                    ops[k]["x"].append(send)
+                k = cp(V("WJ", 0, 128), V(cm), pre=("arr%d" % (t - 1) if t else None))
+                if t:
+                    ops[k]["x"].append(send)
+                    add("v", lambda q, T, x, t=t, cm=cm: q.tensor_copy(T[cm][:, 0:16], T["GO%d" % (t - 1)][:, 0:16]), [V(cm, 0, 16)], [V("GO%d" % (t - 1), 0, 16)], 64)
+                    ops.insert(k - 1, ops.pop())
+                    cp(V("WJ", 128, 256), V(xa, p0 - LN, p0))
+                else:
+                    cp(V("WJ", 128, 256), IND(XA, V("FNu")))
+                act(V("WN"), IND(V("WJ"), V("PMu")), AF.Identity)
+                mm([(V("PN", 128 * h, 128 * h + 128), V("WN", 128 * h, 128 * h + 128), V("ID"), True, True) for h in range(2)])
+                act(V("WTT"), V("PN", 0, 256), AF.Identity)
+            dma("y", "dc%d" % (2 * t + l), lambda T, xa=xa, xb=xb: [(T[xb][:, 0:XD], T[xa][:, 0:XD])], [V(xb, 0, XD)], [V(xa, 0, XD)], 5000)["n"] = 16
+            kid = ("K", t, l)
+            mm([(V("PK", 0, 256), V("ID"), V("KC"), True, False)], kid)
+            c0 = 0
+            for eng, w in TUNE["z"][l]:
+                lo, hi = 512 * c0, 512 * (c0 + w)
+                gather(eng, V("Z", lo, hi), IND(XA, V("RU", lo // 16, hi // 16)))
+                for e in range(c0, c0 + w):
+                    pd = V(("PD0", "PD1", "PC")[e % 3]); pp = ((32 * (e % 4), 32 * (e % 4) + 32),)
+                    acc(pd, [(V("ID"), V("Z", 512 * e, 512 * e + 512)), (V("WTT", 128 * (e // 4), 128 * (e // 4) + 128) + pp, V("SELW") + pp)])
+                    act(V("AB", 512 * e, 512 * e + 512), pd, AF.Abs)
+                    mm([(V("PK", 0, 256), sel(q), V("AB", 256 * q, 256 * q + 256), False, q == 15) for q in (2 * e, 2 * e + 1)], kid)
+                scan(V("MXV", lo, hi), V("MK", 0, hi - lo), V("Z", lo, hi), OP.mult, OP.max)
+                scan(V("MNV", lo, hi), V("RB", 0, hi - lo), V("Z", lo, hi), OP.add, OP.min)
+                c0 += w
+            if l == 1 or t == 1:
+                acting(s, "PB")
+            if l == 1:
+                tt(V("OK", 8, 16), V("OK", 8, 16), V("acN", 8, 16), OP.mult)
+                act(V("OK", 0, 8), V("acN", 0, 8), AF.Identity)
+            if l == 0:
+                if t < RO - 1:
+                    act(V("N%d" % t), V("NI", p0, p0 + LN), AF.Identity, scale=1.0 / C)
+                act(V("AD", 0, 128), V("EQ", t, t + 128), AF.Identity, bias=col(15 + t), scale=1.0 / C)
+                if t == 0:
+                    act(V("NF"), IND(V("NI"), V("FNu")), AF.Identity, scale=1.0 / C)
+                nf = V("N%d" % (t - 1)) if t else V("NF")
+            middle("MXV", "MNV", 0, 256, "PM")
+            act(V("EV"), V("PM", 0, 256), AF.Abs, bias=col(12))
+            if l == 0:
+                ts(V("LE"), V("PM", 0, 256), MAGIC, OP.is_le)
+            scan(V("KS"), V("RB", 0, 256), V("PK", 0, 256), OP.add, OP.min)
+            ts(V("K1", 0, 16), V("KS", 15, 256, 16), 16.0, OP.mult)
+            ts(V("K1", 16, 32), V("K1", 0, 16), 15, OP.bitwise_and)
+            cp(V("KB"), V("K1", 16, 32))
+            mm([(V("PN", 16 * q, 16 * q + 16), V("BC", 128 * q, 128 * q + 128), V("KB"), True, True) for q in range(16)])
+            ts(V("OH"), V("PN", 0, 256), col(0), OP.is_equal)
+            tt(V("PRD"), IND(RA, V("LP", 0, 16)), V("OH"), OP.mult)
+            blocks(V("PA", 0, 16), "PRD")
+            ts(V("CI", 0, 16), V("PA", 0, 16), float(C), OP.mult)
+            blocks(V("PB", 0, 16), "EV")
+            ok = V("ac" + s)
+            act(V("AP_"), ok, AF.Identity, bias=V("AC", 0, 1), scale=8192.0)
+            tt(V("TH"), V("PB", 0, 16), V("AP_"), OP.add)
+            if l == 0:
+                mm([(V("PM", 256, 512), V("BO"), V("LE"), True, True)])
+                ts(V("SB_"), V("PM", 256, 512), col(9), OP.mult, col(10), OP.is_ge)
+                tt(V("KP"), IND(V("KF"), V("LP", 0, 16)), V("SB_"), OP.mult)
+                comb(V("PB", 0, 16), "KP"); blocks(V("PB", 16, 32), "KP")
+                nodes("N", V("PB", 0, 32))
+            tt(V("DL", 0, 16), V("CI", 0, 16), V("DMX"), OP.subtract)
+            lowest(V("CI", 0, 16), "c", True, "PA")
+            act(V("XC"), IND(XA, V("CU", 0, 16)), AF.Identity)
+            acc(V("PN", 0, 256), [(V("H5"), V("XC")), (V("H5"), V("WJ")), (V("QI"), V("ONE")), (V("MI"), V("ONE"))])
+            act(V("NW"), V("PN", 0, 256), AF.Identity, bias=col(12))
+            tt(V("DL", 16, 32), V("PA", 0, 16), V("THR"), OP.is_lt)
+            tt(V("DL", 32, 48), V("DL", 16, 32), V("DL", 0, 16), OP.mult)
+            tt(V("DL", 16, 32), V("DL", 32, 48), V("DMX"), OP.add)
+            cp(V("XU"), V("DL", 16, 32))
+            act(V("NT"), V("NS"), AF.Identity)
+            act(V("RD", 128, 256), IND(RA, V("LQ", 0, 8)), AF.Identity)
+            tt(V("AD", 128, 256), IND(RA, V("LQ", 0, 8)), nf, OP.is_equal)
+            if l == 1:
+                ok = V("OK")
+            tt(V("LT", 0, 16), V("LF", 32, 48), V("DUM", 16, 32), OP.subtract)
+            tt(V("LT", 16, 32), V("LT", 0, 16), ok, OP.mult)
+            tt(V("BS", 16, 32), V("LT", 16, 32), V("DUM", 16, 32), OP.add)
+            act(V("DT", 24, 32), V("LT", 24, 32), AF.Identity, scale=-1.0)
+            tt(V("DT", 0, 16), V("pr" + s, 16, 32), V("DUM", 32, 48), OP.subtract)
+            act(V("DT", 16, 24), V("TT", 16, 24), AF.Identity, scale=2.0)
+            if l == 0:
+                act(V("NP"), IND(V("SW", 0, 256), V("puN")), AF.Identity, scale=-16.0)
+                comb(V("PB", 0, 16), "NP")
+                act(V("SP"), V("PB", 0, 16), AF.Identity)
+            did = ("D", t, l)
+            c0 = 0; m0 = 0
+            for eng, w, mid in TUNE["u"][l]:
+                lo, hi = 256 * c0, 256 * (c0 + w)
+                gather(eng, V("ZU", lo, hi), IND(XA, V("RU", 256 + lo // 16, 256 + hi // 16)))
+                scan(V("MXU", lo, hi), V("MK", 0, hi - lo), V("ZU", lo, hi), OP.mult, OP.max)
+                scan(V("MNU", lo, hi), V("RB", 0, hi - lo), V("ZU", lo, hi), OP.add, OP.min)
+                c0 += w
+                if mid:
+                    lo, hi = 16 * m0, 16 * c0
+                    middle("MXU", "MNU", lo, hi, "PM")
+                    act(V("EU", lo, hi), V("PM", lo, hi), AF.Abs, bias=col(12))
+                    mm([(V("PK", 0, 16), sel(a), V("EU", 16 * a, 16 * a + 16), a == 0, a == 15) for a in range(m0, c0)], did)
+                    m0 = c0
+            cp(IND(XB, V("XU")), V("NW"))
+            if l == 1 and not last:
+                go = "GO%d" % t
+                if t == 0:
+                    act(V("G1"), IND(V(xb, 0, XD), V("FNu")), AF.Identity)
+                    act(V(go), IND(V("G1"), V("SNu")), AF.Identity)
+                else:
+                    act(V(go), IND(V(xb, p0 - LN, p0), V("SNu")), AF.Identity)
+                send = ops[add("p", lambda q, T, x, t=t: x["send"](t), [], [V(go)], 1500, sem="loc", n=0, lat=TUNE["far"])]
+            if last:
+                dma("y", "ox0", lambda T: [(T.yx[:, 0:1024], T.X0[:, 0:1024])], [], [V("X0", 0, 1024)], 3000)["n"] = 16
+                dma("y", "ox1", lambda T: [(T.yx[:, 1024:2048], T.X0[:, 1024:2048])], [], [V("X0", 1024, 2048)], 3000)["n"] = 16
+            for r, w in ((0, 16), (16, 16)):
+                tt(V("EX", r, r + w), V("PK", 0, w), V("TH", 0, w), OP.is_lt)
+            tt(V("LT", 0, 32), V("EX"), V("DT"), OP.mult)
+            tt(V("LT", 32, 64), V("LT", 0, 32), V("BS"), OP.add)
+            cp(V("LU"), V("LT", 32, 64))
+            act(IND(V("SW"), V("LU", 0, 16)), V("NT"), AF.Tanh)
+            nx = "N" if l == 0 else "EO"[(t + 1) & 1]
+            if not last:
+                act(V("NS"), IND(V("SW", 0, 256), V("pu" + nx)), AF.Identity, scale=-16.0)
+            tt(V("RD", 0, 128), IND(RA, V("LU", 16, 24)), V("KE", t, t + 128), OP.mult)
+            tt(IND(RA, V("LU", 16, 32)), V("RD"), V("AD"), OP.max)
+            if not last:
+                lv[0] += 1
+                places(nx, False)
+                mm([(V("PN", 0, 16), V("BO"), V("EX", 0, 16), True, True)])
+                act(V("JK"), V("PN", 0, 16), AF.Identity, bias=col(14), scale=-1.0, total=V("AC", 0, 1))
+    act(V("NS"), V("SW", 0, 256), AF.Identity, scale=16.0)
+    comb(V("PA", 0, 16), "NS")
+    ts(V("TT", 0, 16), V("PA", 0, 16), 0.5, OP.mult, -128.0, OP.add)
+    ts(V("TT", 16, 32), V("PA", 0, 16), 0.5, OP.mult, 128.0, OP.add)
+    tt(V("LF", 0, 16), V("JQ"), V("TT", 0, 16), OP.subtract)
+    tt(V("LF", 16, 32), V("JQ"), V("TT", 16, 32), OP.add)
+    cp(V("FU"), V("LF", 0, 32))
+    ts(V("RO_"), IND(V("RW"), V("FU")), float(C), OP.mult)
+    act(V("KO"), IND(V("KF"), V("FU")), AF.Identity)
+    dma("y", "oyr", lambda T: [(T.yr[:, :], T.RO_[:, :])], [], [V("RO_")], 2500)["n"] = 16
+    dma("s", "oyk", lambda T: [(T.yk[r:16:2, :], T.KO[r:128:16, :]) for r in range(2)], [], [V("KO")], 2500)["n"] = 32
+    return ops
+
+
+TURN = {}
+PLAN = {}
+
+
+def kind(o):
+    w = o["W"][0] if o["W"] else ("", 0)
+    return w[0] + ("b" if w[0] in ("RU", "TT", "LF", "LT", "AD", "RD", "DT", "DL", "Z", "EU") and (w[1] > 0 and w[0] != "Z" or w[0] == "Z" and o["e"] == "v") else "") + \
+        ("s" if o["lv"] < 0 else str(o["lv"] % 2))
+
+
+def schedule(ops):
+    n = len(ops); others = []; mid = (TUNE["G"], TUNE["S"])
+    for rates in TUNE["others"] + [mid]:
+        TUNE["G"], TUNE["S"] = rates
+        others.append([o["c"] for o in build()])
+    others.pop()
+    for k, o in enumerate(ops):
+        o["k"] = k
+    pred = [set() for _ in range(n)]; soft = [set() for _ in range(n)]
+    hist = {}
+    for k, o in enumerate(ops):
+        for x in o["x"]:
+            soft[k].add(x["k"])
+        for w, vs in ((False, o["R"]), (True, o["W"])):
+            for v in vs:
+                h = hist.setdefault(v[0], [])
+                for (j, lo, hi, wj) in h:
+                    if j == k:
+                        continue
+                    clash = lo < v[2] and v[1] < hi and (w or wj)
+                    if v[0] in PS:
+                        if ops[j]["e"] != o["e"]:
+                            clash = True
+                        elif o["e"] == "t":
+                            soft[k].add(j)
+                            clash = clash and not (o["g"] is not None and o["g"] == ops[j]["g"])
+                    if clash:
+                        pred[k].add(j)
+        for w, vs in ((False, o["R"]), (True, o["W"])):
+            for v in vs:
+                h = hist[v[0]]
+                if w and v[3] == 1 and v[0] not in PS:
+                    h[:] = [e for e in h if not (v[1] <= e[1] and e[2] <= v[2])]
+                if v[0] in PS and o["e"] == "t":
+                    h[:] = [e for e in h if ops[e[0]]["e"] == "t"][-40:]
+                if (k, v[1], v[2], w) not in h[-20:]:
+                    h.append((k, v[1], v[2], w))
+    allp = [pred[k] | soft[k] for k in range(n)]
+    succ = [[] for _ in range(n)]
+    for k in range(n):
+        for j in allp[k]:
+            succ[j].append(k)
+
+    def gap(j, k):
+        return ops[j]["lat"] + (TUNE["same"] if ops[j]["e"] == ops[k]["e"] else TUNE["cross"]) * (0 if j not in pred[k] and not ops[j]["lat"] else 1)
+    fw = [[(j, gap(k, j)) for j in succ[k]] for k in range(n)]
+    bw = [[(j, gap(j, k)) for j in allp[k]] for k in range(n)]
+
+    def run(nxt, prv, pri, back, look):
+        left = [len(p) for p in prv]; ready = [ops[k]["lat"] if back else 0.0 for k in range(n)]; free = {e: 0.0 for e in "vstpy"}
+        pool = {e: [] for e in "vstpy"}; seq = []; at = [0.0] * n; end = 0.0
+        for k in range(n):
+            if not left[k]:
+                pool[ops[k]["e"]].append(k)
+        for _ in range(n):
+            t0, e = min((max(free[e], min(ready[k] for k in pool[e])), e) for e in pool if pool[e])
+            k = max((k for k in pool[e] if ready[k] <= t0 + look), key=lambda k: pri[k])
+            pool[e].remove(k); at[k] = max(t0, ready[k])
+            free[e] = at[k] + ops[k]["c"]; end = max(end, free[e] + (0 if back else ops[k]["lat"])); seq.append(k)
+            for j, d in nxt[k]:
+                ready[j] = max(ready[j], free[e] + d); left[j] -= 1
+                if not left[j]:
+                    pool[ops[j]["e"]].append(j)
+        return end, seq, at
+    rank = {nm: r for r, names in enumerate(TUNE["first"]) for nm in names.split()}
+    keys = [kind(o) for o in ops]
+    off = {}
+    for key, o in zip(keys, ops):
+        if o["e"] in "vs" and o["W"]:
+            nm = o["W"][0][0]
+            if o["lv"] < 0:
+                off[key] = -1e6 if nm in TUNE["head"].split() else -8000 if nm in TUNE["early"].split() else 9000 if nm in TUNE["late"].split() else 2000
+            else:
+                off[key] = 0 if key[:3] in ("RU0", "RU1") else 3000 * rank.get(nm, TUNE["rest"])
+    off.update(TURN)
+
+    def again(seq, cost):
+        ready = [0.0] * n; free = {e: 0.0 for e in "vstpy"}; end = 0.0
+        for k in seq:
+            e = ops[k]["e"]; f = max(ready[k], free[e]) + cost[k]; free[e] = f; end = max(end, f + ops[k]["lat"])
+            for j, d in fw[k]:
+                if f + d > ready[j]:
+                    ready[j] = f + d
+        return end
+
+    def tried(off):
+        p = [0.0] * n
+        for k in range(n - 1, -1, -1):
+            o = ops[k]
+            if o["e"] in "vs":
+                p[k] = -25000.0 * max(o["lv"], 0) - off.get(keys[k], 0) - 0.01 * k
+            else:
+                p[k] = max([p[j] for j in succ[k]] + [-1e9])
+        r = run(fw, bw, p, False, TUNE["look"])
+        return (r[0] + sum(again(r[1], c) for c in others),) + r
+    best = tried(off); names = sorted(k for k in off if off[k] > -1e5); z = [TUNE["seed"]]
+
+    def pick(xs):
+        z[0] = (z[0] * 6364136223846793005 + 1442695040888963407) % 2 ** 64
+        return xs[(z[0] >> 33) % len(xs)]
+    for _ in range(TUNE["tries"]):
+        o = dict(off)
+        for _ in range(pick([1, 1, 2, 3])):
+            o[pick(names)] += pick([-1, 1]) * pick([500, 1500, 3000, 6000, 12000])
+        r = tried(o)
+        if r[0] <= best[0]:
+            best, off = r, o
+    PLAN["off"] = off; PLAN["all"] = [best[1]] + [again(best[2], c) for c in others]
+    end, seq, at = best[1:]
+    seq.sort(key=lambda k: at[k])
+    for k in range(n):
+        ops[k]["t"] = at[k]
+    need = set()
+    for k in range(n):
+        need |= pred[k]
+    cnt = {e: 0 for e in "vstpy"}
+    for k in seq:
+        o = ops[k]
+        if o["sem"] is None and k in need:
+            cnt[o["e"]] += 1; o["mark"] = ("e" + o["e"], cnt[o["e"]])
+        elif o["sem"] in DMAS:
+            o["mark"] = (o["sem"], o["n"])
+        else:
+            o["mark"] = None
+    known = {e: {} for e in "vstpy"}; clock = {}
+    for k in seq:
+        o = ops[k]; kn = known[o["e"]]; waits = []
+        for j in sorted(pred[k], key=lambda j: -ops[j]["t"]):
+            m = ops[j]["mark"]
+            if m is not None and kn.get(m[0], 0) < m[1]:
+                waits.append(m)
+                for s, c in clock[j].items():
+                    kn[s] = max(kn.get(s, 0), c)
+        o["waits"] = waits
+        clock[k] = dict(kn)
+        if o["mark"]:
+            clock[k][o["mark"][0]] = o["mark"][1]
+    return seq, cnt, end
+
+
+def bits(es):
+    return sum(1 << e for e in es)
+
+
+def routes(T, topo, r):
+    me = T.cores[r]
+    near = [d for d in range(1, N) if topo.may_write(me, T.cores[(r + d) % N])]
+    far = [d for d in range(1, N) if d not in near]
+    able = [c for c in topo.cores_of(me) if c not in T.cores and all(topo.may_write(c, T.cores[(r + d) % N]) for d in far)]
+    able.sort(key=lambda c: topo.die(c) != topo.die(me))
+    h = (len(far) + 1) // 2
+    return near, [(able[0], far[:h]), (able[1], far[h:])]
+
+
+def shares(es, k):
+    out = [es]
+    while len(out) < k:
+        out.sort(key=len); a = out.pop()
+        out += [a[:len(a) // 2], a[len(a) // 2:]]
+    return out
+
+
+def arrivals(T, topo, r):
+    tot = 0
+    for q in range(N):
+        near, helpers = routes(T, topo, q)
+        for src, ds in [(T.cores[q], near)] + helpers:
+            sh = shares(topo.engines(src, T.cores[(q + ds[0]) % N]), len(ds))
+            tot += sum(len(e) for d, e in zip(ds, sh) if (q + d) % N == r)
+    return tot
+
+
+def on_chip(T, topo, r):
+    me = T.cores[r]; near, helpers = routes(T, topo, r)
+    off = topo.engines(me, T.cores[(r + near[0]) % N])
+    return shares([e for e in topo.engines(me, helpers[0][0]) if e not in off], len(helpers))
+
+
+def forward(g, T, topo, src, r, ds, buf, lo, t):
+    sh = shares(topo.engines(src, T.cores[(r + ds[0]) % N]), len(ds)); trs = []
+    for k, d in enumerate(ds):
+        rid, pid = topo.addr(T.cores[(r + d) % N], src)
+        trs.append(RemoteDMATransfer(dst_ids=[DstId(rid=rid, pnc=pid)], dma_engine_mask=bits(sh[k]), remote_sem=T.sem["arr%d" % t],
+                                     src=buf[:, lo + 16 * k:lo + 16 * k + 16], dst=T["CM%d" % (t + 1)][:, 16 * d:16 * d + 16]))
+    g.remote_dma_fused(trs, local_sem=T.sem["loc"])
+    return sum(len(e) for e in sh)
+
+
+def rank_program(g, core, T, topo):
+    rank = T.rank_of(core)
+    if rank is None:
+        for r in range(N):
+            for k, (h, ds) in enumerate(routes(T, topo, r)[1]):
+                if h == core:
+                    tot = 0
+                    for t in range(RO - 1):
+                        g.wait_ge(T.sem["hin%d" % t], len(on_chip(T, topo, r)[k]))
+                        tot += forward(g, T, topo, core, r, ds, T["HL%d" % t], 0, t)
+                    g.wait_ge(T.sem["loc"], tot)
+        return
+    if "ops" not in PLAN:
+        ops = build()
+        PLAN["ops"] = ops; PLAN["s"] = schedule(ops)
+    ops = PLAN["ops"]; seq, cnt, end = PLAN["s"]
+    near, helpers = routes(T, topo, rank)
+    sent = [0]
+
+    def send(t):
+        go = T["GO%d" % t]; lo = 16 * (1 + len(near)); trs = []
+        for (h, ds), es in zip(helpers, on_chip(T, topo, rank)):
+            rid, pid = topo.addr(h, core); w = 16 * len(ds)
+            trs.append(RemoteDMATransfer(dst_ids=[DstId(rid=rid, pnc=pid)], dma_engine_mask=bits(es), remote_sem=T.sem["hin%d" % t],
+                                         src=go[:, lo:lo + w], dst=T["HL%d" % t][:, 0:w]))
+            lo += w; sent[0] += len(es)
+        g.remote_dma_fused(trs, local_sem=T.sem["loc"])
+        sent[0] += forward(g, T, topo, core, rank, near, go, 16, t)
+
+    x = {"order": [0] + near + [d for h, ds in helpers for d in ds], "send": send}
+    qs = {"v": g.vector, "s": g.scalar, "t": g.tensor, "p": g, "y": g.sync}
+    come = arrivals(T, topo, rank); seen = set()
+    for k in seq:
+        o = ops[k]; q = qs[o["e"]]
+        if o["pre"] and o["pre"] not in seen:
+            seen.add(o["pre"]); q.wait_ge(T.sem[o["pre"]], come)
+        for s, c in o["waits"]:
+            q.wait_ge(T.sem[s], c)
+        i = o["f"](q, T, x)
+        if o["sem"] is None and o["mark"]:
+            i.then_inc(T.sem[o["mark"][0]], 1)
+    for e in "vstp":
+        if cnt[e]:
+            g.sync.wait_ge(T.sem["e" + e], cnt[e])
+    for o in ops:
+        if o["sem"] in DMAS:
+            g.sync.wait_ge(T.sem[o["sem"]], o["n"])
+    g.wait_ge(T.sem["loc"], sent[0])

@@ -1,5 +1,5 @@
 from concourse.bass import DstId, RemoteDMATransfer
-from concourse.mybir import AluOpType as OP, AxisListType as AX, ActivationFunctionType as AF
+from concourse.mybir import AluOpType as OP, ActivationFunctionType as AF
 
 C, NV, LN, RO, N = 2048, 512, 128, 3, 8
 B0 = C - LN * RO
@@ -8,26 +8,27 @@ XD, XN = 2064, 2320
 BF, F32, I32, U16, F16 = "bfloat16", "float32", "int32", "uint16", "float16"
 SB = {
     "X0": (XN, BF), "X1": (XN, BF), "RI": (512, I32), "RW": (768, F32), "SW": (512, F32), "NT": (256, F32), "KI": (512, I32), "KF": (512, F32),
-    "NI": (2048, F32), "RT": (16, I32), "FNi": (8, I32), "SNi": (8, I32), "FNu": (8, U16), "SNu": (8, U16),
-    "CM0": (128, BF), "CM1": (128, BF), "CM2": (128, BF), "GO0": (128, BF), "GO1": (128, BF), "G1": (128, BF), "HL0": (128, BF), "HL1": (128, BF),
-    "IOT": (128, BF), "X16": (256, BF), "PI": (8, I32), "PJ": (16, I32), "CF": (32, F32), "ID": (128, BF), "H5": (128, BF), "NG": (128, BF),
-    "QI": (128, BF), "MI": (128, BF), "BO": (128, BF), "G16": (128, BF), "I16": (16, F32), "I16b": (16, BF), "ONE": (256, BF), "KC": (256, BF),
-    "RB": (512, BF), "MK": (512, BF), "SEL": (2048, BF), "BC": (2048, BF), "SELW": (512, BF), "JQ": (16, F32), "WT": (16, BF), "THR": (16, F32),
-    "IC": (16, I32), "CIu": (16, U16), "PMu": (16, U16), "ADG": (32, F32), "DUM": (48, F32), "DMX": (16, F32),
-    "Z": (4096, BF), "ZU": (4096, BF), "MXV": (4096, BF), "MNV": (4096, BF), "MXU": (4096, BF), "MNU": (4096, BF), "AB": (4096, BF),
-    "RU": (512, U16), "WJ": (256, BF), "WN": (256, BF), "WTT": (256, BF), "KS": (256, F32), "K1": (32, I32), "KB": (16, BF), "OH": (256, BF),
-    "PRD": (256, F16), "CI": (48, I32), "CU": (48, U16), "CD": (32, BF), "OAc": (2048, BF), "OBc": (2048, BF), "TWc": (144, BF), "HMc": (256, BF),
-    "RDc": (256, BF), "DL": (48, F32), "XU": (16, U16), "XC": (256, BF), "NW": (256, BF),
-    "QI2": (32, I32), "QU": (32, U16), "QD": (32, BF), "OAp": (2048, BF), "OBp": (256, BF), "TWp": (16, BF), "HMp": (256, BF), "RDp": (256, BF),
-    "EV": (256, BF), "EU": (256, BF), "LE": (256, BF), "SB_": (256, BF), "KP": (256, F16), "NS": (256, BF), "NP": (256, BF), "SP": (16, F32),
-    "TT": (32, F32), "LF": (64, F32), "LP": (32, U16), "LQ": (32, U16), "AC": (8, F32), "AP_": (16, F32), "TH": (16, F32), "OK": (16, F32),
+    "NI": (2048, F32), "RT": (16, I32), "FNi": (8, I32), "SNi": (8, I32), "FNu": (8, U16), "SNu": (8, U16), "FSu": (8, U16), "FSw": (128, F16),
+    "CM0": (256, BF), "CM1": (256, BF), "CM2": (256, BF), "GO0": (128, BF), "GO1": (128, BF), "HL0": (128, BF), "HL1": (128, BF),
+    "IOT": (144, BF), "X16": (256, BF), "PI": (8, I32), "PJ": (16, I32), "CF": (32, F32), "ID": (128, BF), "H5": (128, BF), "NG": (128, BF),
+    "QI": (128, BF), "MI": (128, BF), "DP": (128, BF), "ID32": (128, F32), "BO": (128, BF), "G16": (128, BF), "S0": (144, BF), "S0N": (144, BF),
+    "ONE": (512, BF), "BIG": (512, BF), "KC": (256, BF), "RB": (512, BF), "MK": (512, BF), "BC": (2048, BF), "SELW": (512, BF), "ZOFF": (512, BF),
+    "RC": (256, BF), "JQ": (16, F32), "WT": (16, F32), "THW": (256, BF), "RR": (256, BF), "M1K": (16, BF), "DUM": (64, F32), "DMX": (16, F32),
+    "ZV": (4096, BF), "HV": (4096, F16), "ZU": (4096, BF), "HU": (4096, F16),
+    "MXV": (4096, F16), "MNV": (4096, F16), "MXU": (4096, F16), "MNU": (4096, F16), "AB": (4096, BF),
+    "RU": (512, U16), "WTT": (256, F16), "KS": (256, F32), "K1": (16, F32), "KB": (32, BF), "PRD": (256, F16), "CW": (256, F16), "CN": (32, F32),
+    "CU": (16, U16), "DA": (16, F16), "DB": (16, BF), "Ec": (2176, BF), "SGc": (256, BF), "DL": (16, F32), "XU": (16, U16), "XC": (256, BF), "NW": (256, BF),
+    "PW": (256, F16), "Ep": (2176, BF), "SGp": (256, BF),
+    "EV": (256, BF), "EU": (256, BF), "LE": (256, BF), "SB_": (256, BF), "KP": (256, F16), "NS": (256, BF), "NP": (128, BF), "SP": (8, F32),
+    "TT": (16, F32), "LF": (32, F32), "LP": (32, U16), "AC": (8, F32), "AP_": (16, F32), "OK": (8, F32),
     "BS": (32, F32), "DT": (32, F32), "EX": (32, BF), "LT": (64, F32), "LU": (32, U16), "RD": (256, F32), "AD": (256, F32), "KE": (144, F32),
-    "EQ": (144, F32), "JK2": (144, F32), "NF": (128, F32), "N0": (128, F32), "N1": (128, F32), "N2": (128, F32), "JK": (16, F32), "U32": (64, F32), "VV": (64, F32), "RO_": (512, F32), "KO": (512, F32), "FU": (32, U16),
+    "EQ": (144, F32), "JK2": (144, F32), "NF": (128, F32), "N0": (128, F32), "N1": (128, F32), "JK": (16, F32), "VV": (32, F32),
+    "RO_": (512, F32), "KO": (512, F32), "FU": (32, U16),
 }
 for _s in "EON":
-    SB.update({"vi" + _s: (64, I32), "pr" + _s: (32, F32), "sg" + _s: (32, F32), "pu" + _s: (16, U16), "ac" + _s: (16, F32)})
-PS = ["PD0", "PD1", "PK", "PM", "PN", "PA", "PB", "PC"]
-OWN = ("X0", "X1", "RI", "KI", "RT", "FNi", "SNi", "SNu", "CM0", "CM1", "CM2", "GO0", "GO1", "HL0", "HL1", "RO_", "KO", "U32", "AC")
+    SB.update({"pr" + _s: (16, F32), "sg" + _s: (16, F32), "pu" + _s: (16, U16), "ac" + _s: (16, F32)})
+PS = ["PD0", "PD1", "PK", "PV", "PM", "PX", "PA", "PB"]
+OWN = ("X0", "X1", "RI", "KI", "RT", "FNi", "SNi", "SNu", "CM0", "CM1", "CM2", "GO0", "GO1", "HL0", "HL1", "RO_", "KO", "AC")
 SCRATCH = {k: ("sbuf", [128, SB[k][0]], SB[k][1]) for k in OWN}
 AT = {k: (k, 0) for k in list(OWN) + PS}
 _fill = {}
@@ -38,13 +39,9 @@ SCRATCH.update({"all_" + d: ("sbuf", [128, w], d) for d, w in _fill.items()})
 SCRATCH.update({k: ("psum", [128, 512], F32) for k in PS})
 DMAS = ["dx0", "dx1", "dring", "dkid", "drt", "dfn", "dsn", "dxl", "ox0", "ox1", "oyr", "oyk"] + ["dc%d" % k for k in range(2 * RO)]
 SEMAPHORES = ["ev", "es", "et", "ep", "arr0", "arr1", "hin0", "hin1", "loc"] + DMAS
-TUNE = {"z": [[(e, 1) for e in "svsvsvsv"]] * 2, "u": [[("s", 2, int(k >= 6)) for k in range(8)]] * 2,
-        "others": [(1.15, 2.0), (2.0, 5.5)], "seed": 1, "tries": 3000, "G": 1.56, "S": 3.8, "same": 70, "cross": 140, "far": 5000,
-        "look": 40, "rest": 4, "head": "PJ CF VV U32 viE sgE prE TT LF LP RW X0 CM0 FNi FNu",
-        "early": "PMu KI BO I16 BC JQ WT SW NT ID SELW",
-        "late": "QI2 QD QU OBp OAp RDp HMp TWp acE viO sgO prO puO SNu KF DUM BS DMX LQ puE TWc THR ADG CIu I16b AC KE EQ JK2",
-        "first": ["EX LU SW NS RW LP CM1 CM2 X0 X1 WJ WN WTT G1 GO0 GO1", "KS K1 KB OH PRD CI CD CU OAc OBc TWc RDc DL XU HMc XC NW", "RU AB Z", "MXV MNV EV", "",
-                  "EU ZU MXU MNU"]}
+TUNE = {"z": "vvsvvvsv", "u": ["ssssssss", "ssssssss"], "cut": [8, 8], "zo": [[4, 5, 6, 7, 0, 1, 2, 3], [0, 1, 2, 3, 4, 5, 6, 7]],
+        "others": [(1.15, 2.0, 0.45), (2.0, 5.5, 0.45), (1.56, 3.8, 0.6)], "seed": 1, "tries": 1500, "G": 1.56, "S": 3.8, "PE": 0.45,
+        "same": 70, "cross": 140, "far": 5000, "look": 40}
 
 
 def V(name, lo=0, hi=None, step=1):
@@ -56,7 +53,7 @@ def IND(win, off):
 
 
 def cols(v):
-    return 16 * cols(v[2]) if v[0] == "@" else (v[2] - v[1] + v[3] - 1) // v[3]
+    return 16 * cols(v[2]) if v[0] == "@" else (v[2] - v[1] + abs(v[3]) - 1) // abs(v[3])
 
 
 def ap(T, v):
@@ -65,6 +62,8 @@ def ap(T, v):
     if v[0] == "@":
         return ap(T, v[1]).indirect(ap(T, v[2]))
     b, o = AT[v[0]]; p = slice(*v[4]) if len(v) > 4 else slice(None)
+    if v[3] < 0:
+        return T[b][p, o + v[2] - 1:(o + v[1] - 1 if o + v[1] else None):v[3]]
     return T[b][p, o + v[1]:o + v[2]:v[3]] if v[3] != 1 else T[b][p, o + v[1]:o + v[2]]
 
 
@@ -110,198 +109,200 @@ def build():
     def ms(o, c):
         add("v", lambda q, T, x: q.memset(ap(T, o), c), [o], [], max(64, cols(o) * (0.5 if two(o) else 1)))
 
-    def scan(o, d0, d1, op0, op1):
-        add("v", lambda q, T, x: q.tensor_tensor_scan(ap(T, o), ap(T, d0), ap(T, d1), 0.0, op0, op1), [o], [d0, d1], max(64, cols(o) * (0.5 if two(o, d0, d1) else 1)))
+    def scan(o, d0, d1, op0, op1, first=0.0):
+        add("v", lambda q, T, x: q.tensor_tensor_scan(ap(T, o), ap(T, d0), ap(T, d1), first, op0, op1), [o], [d0, d1], max(64, cols(o) * (0.5 if two(o, d0, d1) else 1)))
 
-    def act(o, a, fn, bias=0.0, scale=1.0, total=None):
+    def act(o, a, fn=AF.Identity, bias=0.0, scale=1.0, total=None):
         add("s", lambda q, T, x: q.activation(ap(T, o), ap(T, a), fn) if o[0] == "@" else
             q.activation(ap(T, o), ap(T, a), fn, bias=ap(T, bias), scale=ap(T, scale), accum_out=ap(T, total)),
             [o] + ([total] if total else []), [a, bias, scale],
-            (65 + TUNE["G"] * cols(a) if a[0] == "@" else 65 + TUNE["S"] * cols(a) if o[0] == "@" else max(64, 30 + cols(a))) + (1300 if fn == AF.Exp else 0))
+            (65 + TUNE["G"] * cols(a) if a[0] == "@" else 65 + TUNE["S"] * cols(a) if o[0] == "@" else max(64, 30 + cols(a))) + (140 if total else 0))
 
     def mm(ms_, grp=None):
         def f(q, T, x):
             for o, l, r, s0, s1 in ms_:
                 i = q.matmul(ap(T, o), ap(T, l), ap(T, r), s0, s1)
             return i
-        add("t", f, [m[0] for m in ms_], [m[1] for m in ms_] + [m[2] for m in ms_], 60 + sum(0.45 * max(64, cols(m[2])) for m in ms_), grp)
+        add("t", f, [m[0] for m in ms_], [m[1] for m in ms_] + [m[2] for m in ms_],
+            60 + sum(TUNE["PE"] * max(64, cols(m[2])) * (4 if SB[m[1][0]][1] == F32 else 1) for m in ms_), grp)
 
-    def acc(o, pairs):
-        mm([(o, l, r, k == 0, k == len(pairs) - 1) for k, (l, r) in enumerate(pairs)])
+    def acc(o, pairs, start=True, stop=True, grp=None):
+        mm([(o, l, r, start and k == 0, stop and k == len(pairs) - 1) for k, (l, r) in enumerate(pairs)], grp)
 
-    def sel(a):
-        return V("SEL", 128 * a, 128 * a + 128)
+    def sel(a, s="S0"):
+        return V(s, 15 - a, 143 - a)
 
-    def blocks(o, f, lo=0):
-        acc(o, [(sel(a), V(f, lo + 16 * a, lo + 16 * a + 16)) for a in range(16)])
+    def comb(f, lo=0, hi=256, s="S0"):
+        return [(sel(a, s), V(f, lo + a, hi, 16)) for a in range(16)]
 
-    def comb(o, f):
-        acc(o, [(sel(a), V(f, a, 256, 16)) for a in range(16)])
+    def spread(bank, k, start, stop):
+        return [(V(bank, 16 * q, 16 * q + 16), V("BC", 128 * q, 128 * q + 128), k, start and q == 0, stop and q == 15) for q in range(16)]
 
     def iota(o, pat, base, cm):
         small = SB[o[0]][1] != I32
         add("p", lambda q, T, x: q.iota(ap(T, o), pat, base, cm, allow_small_or_imprecise_dtypes=True) if small else q.iota(ap(T, o), pat, base, cm),
             [o], [], 130 + 2 * cols(o))
 
-    def dma(eng, sem, pairs, outs, ins, lat):
+    def pick_(o, a, pat, op, base, cm):
+        add("p", lambda q, T, x: q.affine_select(ap(T, o), ap(T, a), pat, op, 0.0, base, cm), [o], [a], 170 + 2 * cols(o))
+
+    def dma(eng, sem, pairs, outs, ins, lat, n=16):
         def f(q, T, x):
             for o, a in pairs(T):
                 q.dma_start(o, a).then_inc(T.sem[sem], 16)
-        add(eng, f, outs, ins, 60, sem=sem, n=0, lat=lat)
-        return ops[-1]
+        add(eng, f, outs, ins, 60 * n // 16, sem=sem, n=n, lat=lat)
 
     def col(k):
         return V("CF", k, k + 1)
 
-    dma("y", "drt", lambda T: [(T.RT[:, :], T.rt[:, :])], [V("RT")], [], 2000)["n"] = 16
-    dma("y", "dring", lambda T: [(T.RI[:, :], T.ring[:, :])], [V("RI")], [], 2600)["n"] = 16
-    dma("s", "dx0", lambda T: [(T.X0[:, 0:1024], T.x[:, 0:1024])], [V("X0", 0, 1024)], [], 3500)["n"] = 16
-    dma("y", "dx1", lambda T: [(T.X0[:, 1024:2048], T.x[:, 1024:2048])], [V("X0", 1024, 2048)], [], 3700)["n"] = 16
-    dma("s", "dxl", lambda T: [(T.CM0[:, :], T.xl[:, :])], [V("CM0")], [], 2500)["n"] = 16
-    dma("s", "dfn", lambda T: [(T.FNi[:, :], T.fn[:, :])], [V("FNi")], [], 2500)["n"] = 16
-    dma("y", "dsn", lambda T: [(T.SNi[:, :], T.snd[:, :])], [V("SNi")], [], 2500)["n"] = 16
-    ms(V("KI"), 0)
-    dma("y", "dkid", lambda T: [(T.KI[r:128:16, :], T.kid[r:16:2, :]) for r in range(2)], [V("KI")], [], 3000)["n"] = 32
-    iota(V("PI", 0, 4), [[-1, 4]], 16, 1)
-    iota(V("PI", 4, 6), [[0, 2]], 0, 1)
-    iota(V("IOT"), [[1, 128]], 0, 0)
-    iota(V("IC"), [[1, 16]], 0, 0)
+    dma("y", "drt", lambda T: [(T.RT[:, :], T.rt[:, :])], [V("RT")], [], 2000)
+    dma("y", "dring", lambda T: [(T.RI[:, :], T.ring[:, :])], [V("RI")], [], 2600)
+    dma("s", "dx0", lambda T: [(T.X0[:, 0:1024], T.x[:, 0:1024])], [V("X0", 0, 1024)], [], 3500)
+    dma("y", "dx1", lambda T: [(T.X0[:, 1024:2048], T.x[:, 1024:2048])], [V("X0", 1024, 2048)], [], 3700)
+    dma("s", "dxl", lambda T: [(T.CM0[:, 0:128], T.xl[:, :])], [V("CM0", 0, 128)], [], 2500)
+    dma("s", "dfn", lambda T: [(T.FNi[:, :], T.fn[:, :])], [V("FNi")], [], 2500)
+    dma("y", "dsn", lambda T: [(T.SNi[:, :], T.snd[:, :])], [V("SNi")], [], 2500)
+    iota(V("KI"), [[0, 512]], 0, 0)
+    dma("y", "dkid", lambda T: [(T.KI[r:128:16, :], T.kid[r % 2:16:2, :]) for r in range(4)], [V("KI")], [], 3000, 64)
+    iota(V("PI", 0, 2), [[0, 2]], 0, 1)
+    iota(V("IOT"), [[1, 144]], 0, 0)
     iota(V("G16"), [[16, 8], [0, 16]], 0, 0)
     iota(V("X16"), [[0, 16], [1, 16]], 0, 0)
     iota(V("JQ"), [[16, 16]], 0, 1)
     iota(V("SELW"), [[1, 32], [0, 16]], 0, 0)
-    iota(V("SEL"), [[-1, 16], [32, 8], [1, 16]], 0, 0)
-    iota(V("NI"), [[1, 2048]], 0, 0)
-    ts(V("PJ", 0, 3), V("PI", 0, 3), 15, OP.bitwise_and)
-    ts(V("PJ", 3, 4), V("PI", 0, 1), 16, OP.bitwise_and)
-    ts(V("PJ", 4, 5), V("PI", 0, 1), 1, OP.bitwise_and)
-    ts(V("PJ", 5, 6), V("PI", 4, 5), 31, OP.bitwise_and)
-    cp(V("CF", 0, 3), V("PJ", 0, 3))
-    ts(col(3), V("PI", 0, 1), -16.0, OP.add)
+    iota(V("ZOFF"), [[0, 2], [256, 16], [0, 16]], -2048, 0)
+    iota(V("NI", 0, 256), [[1, 256]], 0, 0)
+    iota(V("NT"), [[0, 256]], -16, 0)
+    iota(V("RW", 512, 768), [[0, 256]], 0, 0)
+    ms(V("ONE"), 1.0); ms(V("BIG"), 131072.0)
+    pick_(V("MK"), V("ONE"), [[0, 32], [1, 16]], OP.not_equal, 0, 0)
+    pick_(V("RB"), V("BIG"), [[0, 32], [1, 16]], OP.is_equal, 0, 0)
+    for m in range(4):
+        pick_(V("BC", 512 * m, 512 * m + 512), V("BIG"), [[-1, 4], [-16, 8], [0, 16]], OP.is_equal, -4 * m, 1)
+    iota(V("NI", 256, 2048), [[1, 1792]], 256, 0)
+    ts(V("PJ", 0, 1), V("PI", 0, 1), 15, OP.bitwise_and)
+    ts(V("PJ", 1, 2), V("PI", 0, 1), 31, OP.bitwise_and)
+    cp(V("CF", 0, 2), V("PJ", 0, 2))
+    cp(col(3), V("PI", 0, 1))
     tt(col(4), col(3), col(0), OP.subtract)
-    ts(col(5), V("PJ", 3, 4), 1.0 / 16, OP.mult)
-    ts(col(6), col(5), -1.0, OP.mult, 1.0, OP.add)
-    cp(col(7), V("PJ", 5, 6))
-    ts(col(8), col(4), 2.0, OP.mult)
-    ts(col(9), V("PJ", 4, 5), 2.0, OP.mult, -1.0, OP.add)
-    ts(col(10), col(9), 8.5, OP.mult)
-    ts(col(11), col(0), 16.0, OP.mult)
-    ms(col(12), -MAGIC)
-    ms(col(13), 64.0)
-    for nm, c in (("ID", 1.0), ("H5", 0.5), ("NG", -1.0), ("QI", -0.25), ("MI", MAGIC)):
-        ts(V(nm), V("IOT"), col(3), OP.is_equal, c, OP.mult)
+    ts(col(5), col(4), 15.0, OP.add)
+    ts(col(6), col(0), -8192.0, OP.mult, 61440.0, OP.add)
+    ts(V("CF", 8, 10), V("IOT", 0, 2), col(0), OP.is_equal)
+    tt(col(10), col(9), col(8), OP.subtract)
+    ts(col(12), col(8), 7.5, OP.mult, 1.0, OP.add)
+    ts(col(11), col(9), -9.5, OP.mult, col(12), OP.add)
+    ts(col(13), col(9), -256.0, OP.mult)
+    ts(col(15), col(8), -0.25, OP.mult)
+    ts(col(14), col(9), 2048.0, OP.mult, col(15), OP.add)
+    for h in range(2):
+        ts(col(16 + h), col(0), 256.0, OP.mult, -2048.0, OP.add)
+        for e in range(4):
+            if TUNE["z"][4 * h + e] == "s":
+                ms(col(16 + h) + ((32 * e, 32 * e + 32),), 0.0)
+    for nm, c in (("ID", 1.0), ("H5", 0.5), ("NG", -1.0), ("QI", -0.25), ("MI", MAGIC), ("DP", col(6)), ("ID32", float(C))):
+        ts(V(nm), V("IOT", 0, 128), col(3), OP.is_equal, c, OP.mult)
     ts(V("BO"), V("G16"), col(4), OP.is_equal)
-    ts(V("I16"), V("IOT", 0, 16), col(0), OP.is_equal)
-    cp(V("I16b"), V("I16"))
-    ms(V("ONE"), 1.0)
-    ts(V("KC"), V("X16"), 1.0 / 16, OP.mult)
-    ms(V("RB"), 0.0); ms(V("RB", 0, 512, 16), 8192.0)
-    ms(V("MK"), 1.0); ms(V("MK", 0, 512, 16), 0.0)
-    ts(V("SEL"), V("SEL"), col(8), OP.is_equal)
-    for a in range(16):
-        act(V("BC", 128 * a, 128 * a + 128), V("BO"), AF.Copy, scale=V("I16", a, a + 1))
-    ts(V("SELW"), V("SELW"), col(7), OP.is_equal, -1.0, OP.mult)
+    ts(V("S0"), V("IOT"), col(5), OP.is_equal)
+    ts(V("S0N"), V("IOT"), col(5), OP.is_equal, -1.0, OP.mult)
+    ts(V("KC"), V("X16"), 1.0 / 16, OP.mult, -15.0 / 32, OP.add)
+    ts(V("RC"), V("X16"), col(13), OP.mult, col(14), OP.add)
+    ts(V("SELW"), V("SELW"), col(1), OP.is_equal, -1.0, OP.mult)
     ts(V("JQ"), V("JQ"), col(4), OP.subtract)
-    act(V("WT"), V("JQ"), AF.Exp, bias=col(13), scale=-0.5596)
-    ts(V("THR"), V("WT"), 2.54, OP.mult)
-    cp(V("CIu"), V("IC"))
-    ts(V("PMu"), V("IC"), col(11), OP.add)
-    ts(V("ADG", 0, 16), V("IC"), 0.0, OP.mult, col(4), OP.add); ms(V("ADG", 16, 32), 0.0)
-    ts(V("DUM", 0, 16), V("JQ"), 256.0, OP.add); ts(V("DUM", 16, 32), V("JQ"), 512.0, OP.add)
+    ms(V("RR"), 0.5703125)
+    scan(V("THW"), V("RR"), V("ONE", 0, 256), OP.mult, OP.mult, 1.5e28)
+    acc(V("PA", 0, 16), comb("THW"))
+    ts(V("WT"), V("PA", 0, 16), 1.0 / (16 * 2.54), OP.mult)
+    ms(V("M1K"), -1024.0)
+    for k, c in enumerate((256, 512, 384, 128)):
+        ts(V("DUM", 16 * k, 16 * k + 16), V("JQ"), float(c), OP.add, 1.0 / 256, OP.mult)
     cp(V("BS", 0, 16), V("DUM", 0, 16))
-    ts(V("DMX"), V("JQ"), float(XD), OP.add)
-    ms(V("TWc", 128, 144), 5e29)
-    ts(V("DUM", 32, 48), V("JQ"), 384.0, OP.add)
+    ts(V("DMX"), V("JQ"), float(XD - C), OP.add, 1.0 / 128, OP.mult)
     ms(V("X0", 2048, XD), 0.0)
-    ms(V("RW", 512, 768), 0.0)
-    ms(V("NT"), -16.0); ms(V("NS"), -16.0)
     act(V("SW", 0, 256), V("NT"), AF.Tanh, scale=-1.0)
-    ops[-1]["c"] += 1500; ops[-1]["R"].append(V("WT"))
+    ops[-1]["c"] += 1300
     ts(V("RW", 0, 512), V("RI"), 1.0 / C, OP.mult)
-    ms(col(14), -512.0)
-    for t in range(RO):
-        ms(col(15 + t), (B0 + LN * t - t) / C)
-    ts(V("KE"), V("X16", 0, 144), col(0), OP.not_equal)
-    act(V("JK2"), V("KE"), AF.Identity, scale=-8192.0)
+    ts(V("KE", 0, 128), V("X16", 0, 128), col(0), OP.not_equal)
+    ts(V("KE", 128, 144), V("X16", 0, 16), col(0), OP.not_equal)
+    act(V("JK2"), V("KE"), scale=-8192.0)
     tt(V("EQ"), V("JK2"), V("NI", 0, 144), OP.add)
     cp(V("FNu"), V("FNi"))
-    for d in range(N):
-        add("v", lambda q, T, x, d=d: q.tensor_copy(T.SNu[:, d:d + 1], T.SNi[:, x["order"][d]:x["order"][d] + 1]), [V("SNu", d, d + 1)], [V("SNi")], 64)
-    cp(V("KF"), V("KI"))
+    for k in range(2):
+        add("v", lambda q, T, x, k=k: q.tensor_copy(T.SNu[:, x["runs"][k][0]], T.SNi[:, x["runs"][k][1]]), [V("SNu")], [V("SNi")], 64)
+    ts(V("KF"), V("KI"), 1.0 / 512, OP.mult)
+    act(V("NF"), IND(V("NI"), V("FNu")), scale=1.0 / C)
+    act(V("FSw"), IND(V("NF"), V("SNu")), scale=128.0)
+    acc(V("PB", 0, 8), comb("FSw", 0, 128))
+    cp(V("FSu"), V("PB", 0, 8))
 
-    def lowest(key, s, wide, bank):
-        ci, cu, cd, o = (("CI", "CU", "CD", 16) if wide else ("QI2", "QU", "QD", 0))
-        ts(V(ci, o, o + 16), key, 15, OP.bitwise_and)
-        ts(V(ci, o + 16, o + 32), key, 4, OP.arith_shift_right)
-        tt(V(cd), V(ci, o, o + 32), V("ADG"), OP.add)
-        cp(V(cu), V(ci))
-        w = 128 if wide else 16
-        if not wide:
-            tt(V("OBp"), IND(V(cd, 16, 32), V("CIu")), V("X16"), OP.is_equal)
-        gid = ("T", len(ops))
+    def lowest(wide, key, s, bank, lo):
+        gid = ("T", len(ops)); at = 0; part = [(V(bank, lo, lo + 256), V("NG"), V("THW"), True, False)]
         for i in range(16):
-            ts(V("OA" + s, 128 * i, 128 * i + 128), V("IOT"), V(cd, i, i + 1), OP.is_equal, V("WT", i, i + 1), OP.mult)
-            if wide:
-                ts(V("OBc", 128 * i, 128 * i + 128), V("IOT"), V(cd, 16 + i, 17 + i), OP.is_equal)
+            e = V("E" + s, at, at + 256 - 16 * i); at = e[2]
+            ts(e, V(wide, 16 * i, 256), V(key, i, i + 1), OP.is_equal, V("WT", i, i + 1), OP.mult)
+            part.append((V(bank, lo + 16 * i, lo + 256), V("BO"), e, False, i == 15))
             if i % 4 == 3:
-                mm([(V(bank, 128, 128 + w), V("OA" + s, 128 * k, 128 * k + 128), V("OB" + s, w * k, w * k + w), k == 0, k == 15) for k in range(i - 3, i + 1)], gid)
-        act(V("HM" + s), IND(V("I16b"), V(cu, o, o + 16)), AF.Identity)
-        act(V("TW" + s, 0, w), V(bank, 128, 128 + w), AF.Identity)
-        tt(V("RD" + s), IND(V("TW" + s), V(cu, o + 16, o + 32)), V("HM" + s), OP.mult)
-        comb(V(bank, 0, 16), "RD" + s)
+                mm(part, gid); part = []
+        act(V("SG" + s), V(bank, lo, lo + 256), AF.Sign)
 
     def nodes(s, v):
-        cp(V("vi" + s, 0, 32), v)
-        ts(V("sg" + s), v, 256.0, OP.is_ge, -0.5, OP.add)
-        ts(V("vi" + s, 32, 64), V("vi" + s, 0, 32), 255, OP.bitwise_and)
-        cp(V("pu" + s), V("vi" + s, 48, 64))
-        ts(V("pr" + s), V("vi" + s, 32, 64), 128.0, OP.add)
+        ts(V("sg" + s), v, 1.0, OP.is_ge, -0.5, OP.add)
+        tt(V("pr" + s), v, V("sg" + s), OP.subtract)
+        ts(V("pu" + s), V("pr" + s), 256.0, OP.mult, -128.0, OP.add)
 
-    def acting(s, bank):
-        lowest(V("vi" + s, 48, 64), "p", False, bank)
-        tt(V("ac" + s), V(bank, 0, 16), V("THR"), OP.is_lt)
+    def acting(s):
+        act(V("PW"), IND(V("NI", 0, 256), V("pu" + s)), bias=0.5, scale=1.0 / 256)
+        lowest("PW", "pr" + s, "p", "PA", 0)
+        acc(V("PA", 256, 272), comb("SGp"))
+        ts(V("ac" + s), V("PA", 256, 272), 0.0, OP.is_lt)
 
     def places(s, first):
-        for h, L in ((0, "LP"), (1, "LQ")):
-            t = V("TT", 16 * h, 16 * h + 16); sg = V("sg" + s, 16 * h, 16 * h + 16); pr = V("pr" + s, 16 * h, 16 * h + 16)
-            if first:
-                ts(t, sg, -256.0, OP.mult)
-            else:
-                if h == 0:
-                    blocks(V("PA", 0, 16), "NS")
-                else:
-                    comb(V("PB", 16, 32), "NS")
-                tt(t, V("PB" if h else "PA", 16 * h, 16 * h + 16), sg, OP.mult)
-            tt(V("LF", 32 * h, 32 * h + 16), pr, t, OP.subtract)
-            if h == 0:
-                tt(V("LF", 16, 32), pr, t, OP.add)
-                cp(V("LP"), V("LF", 0, 32))
-            else:
-                cp(V("LQ", 0, 8), V("LF", 40, 48))
-            if h == 1 and s == "N":
-                tt(V("OK", 8, 16), V("PB", 24, 32), V("SP", 8, 16), OP.is_equal)
-
-    for s, o in (("E", 0), ("O", 8)):
-        cp(V("VV", 16, 24), V("RT", o, o + 8)); cp(V("VV", 24, 32), V("RT", 8 - o, 16 - o))
-        ts(V("U32", 0, 16), V("VV", 16, 32), col(5), OP.mult); ts(V("U32", 16, 32), V("VV", 16, 32), col(6), OP.mult)
-        add("v", lambda q, T, x: q.transpose(T.U32[:, 32:64], T.U32[:, 0:32]), [V("U32", 32, 64)], [V("U32", 0, 32)], 64)
-        tt(V("VV", 0, 16), V("U32", 32, 48), V("U32", 48, 64), OP.add)
-        nodes(s, V("VV", 0, 32))
-        if s == "E":
-            places("E", True)
-    ms(V("AC", 0, 1), -8192.0)
-    acting("E", "PB")
-
-    def gather(eng, o, a):
-        if eng == "v":
-            cp(o, a)
+        if first:
+            ts(V("TT"), V("sg" + s), -1.0, OP.mult)
         else:
-            act(o, a, AF.Identity)
+            acc(V("PX", 16, 32), comb("NS"))
+            tt(V("TT"), V("PX", 16, 32), V("sg" + s), OP.mult)
+        tt(V("LF", 0, 16), V("pr" + s), V("TT"), OP.subtract)
+        tt(V("LF", 16, 32), V("pr" + s), V("TT"), OP.add)
+        ts(V("LP"), V("LF"), 256.0, OP.mult)
+        if s == "N":
+            tt(V("OK"), V("PX", 24, 32), V("SP"), OP.is_equal)
 
-    def middle(mx, mn, lo, hi, bank):
-        o = V(bank, lo, hi)
-        acc(o, [(V("H5"), V(mx, 16 * lo + 15, 16 * hi, 16)), (V("H5"), V(mn, 16 * lo + 15, 16 * hi, 16)), (V("NG"), V("WN", lo, hi)),
-                (V("QI"), V("ONE", lo, hi)), (V("MI"), V("ONE", lo, hi))])
+    ts(V("VV", 0, 16), V("RT"), 1.0 / 256, OP.mult)
+    nodes("E", V("VV", 0, 16)); places("E", True)
+    cp(V("VV", 16, 24), V("VV", 8, 16)); cp(V("VV", 24, 32), V("VV", 0, 8))
+    nodes("O", V("VV", 16, 32))
+    ms(V("AC", 0, 1), -8192.0)
+    acting("E")
+
+    def rings(r, e, eng, XA):
+        lo, hi = 512 * e, 512 * e + 512; u = 256 * (r == "U") + 32 * e
+        src = IND(XA, V("RU", u, u + 32))
+        if eng == "v":
+            z = "H" + r
+            tt(V(z, lo, hi), src, V("ZOFF"), OP.add)
+            for b in (lo, lo + 256):
+                scan(V("MX" + r, b + 1, b + 256, 2), V(z, b, b + 256, 2), V(z, b + 1, b + 256, 2), OP.max, OP.max, -4096.0)
+                scan(V("MN" + r, b, b + 255, -2), V(z, b, b + 255, -2), V(z, b + 1, b + 256, -2), OP.min, OP.min, 4096.0)
+        else:
+            z = "Z" + r
+            act(V(z, lo, hi), src)
+            scan(V("MX" + r, lo, hi), V("MK"), V(z, lo, hi), OP.mult, OP.max)
+            scan(V("MN" + r, lo, hi, -1), V("RB"), V(z, lo, hi, -1), OP.add, OP.min)
+        return V(z, lo, hi)
+
+    def middle(r, e0, e1, bank, engs, cm):
+        lo, hi = 32 * e0, 32 * e1; o = V(bank, lo, hi)
+        part = [(o, V("NG"), V(cm, lo, hi), True, False)]; e = e0
+        while e < e1:
+            f = e
+            while f < e1 and engs[f] == engs[e]:
+                f += 1
+            part.append((V(bank, 32 * e, 32 * f), V("BO"), V("RC", 32 * e, 32 * f), False, False) if engs[e] == "v" else
+                        (V(bank, 32 * e, 32 * f), V("QI"), V("ONE", 32 * e, 32 * f), False, False))
+            e = f
+        gid = ("M", len(ops)); mm(part, gid)
+        mm([(o, V("H5"), V("MX" + r, 16 * lo + 15, 16 * hi, 16), False, False), (o, V("H5"), V("MN" + r, 16 * lo, 16 * hi, 16), False, False),
+            (o, V("MI"), V("ONE", lo, hi), False, True)], gid)
 
     send = None
     for t in range(RO):
@@ -313,167 +314,148 @@ def build():
             lv[0] = 2 * t + l
             xa, xb = "X%d" % l, "X%d" % (1 - l)
             XA, XB, RA = V(xa, 0, XD), V(xb), V("RW")
-            ts(V("RU", 0, 256), IND(RA, V("LP", 0, 16)), float(C), OP.mult)
-            ts(V("RU", 256, 512), IND(RA, V("LP", 16, 32)), float(C), OP.mult)
-            if l == 0:
-                k = cp(V(xa, p0, p0 + LN), V(cm), pre=("arr%d" % (t - 1) if t else None))
-                if t:
-                    ops[k]["x"].append(send)
-                k = cp(V("WJ", 0, 128), V(cm), pre=("arr%d" % (t - 1) if t else None))
-                if t:
-                    ops[k]["x"].append(send)
-                    add("v", lambda q, T, x, t=t, cm=cm: q.tensor_copy(T[cm][:, 0:16], T["GO%d" % (t - 1)][:, 0:16]), [V(cm, 0, 16)], [V("GO%d" % (t - 1), 0, 16)], 64)
-                    ops.insert(k - 1, ops.pop())
-                    cp(V("WJ", 128, 256), V(xa, p0 - LN, p0))
+            for lo, hi in ((8, 16), (0, 8), (16, 32)) if TUNE["zo"][l][0] >= 4 else ((0, 8), (8, 16), (16, 32)):
+                if lv[0]:
+                    ts(V("RU", 16 * lo, 16 * hi), IND(RA, V("LP", lo, hi)), float(C), OP.mult)
                 else:
-                    cp(V("WJ", 128, 256), IND(XA, V("FNu")))
-                act(V("WN"), IND(V("WJ"), V("PMu")), AF.Identity)
-                mm([(V("PN", 128 * h, 128 * h + 128), V("WN", 128 * h, 128 * h + 128), V("ID"), True, True) for h in range(2)])
-                act(V("WTT"), V("PN", 0, 256), AF.Identity)
-            dma("y", "dc%d" % (2 * t + l), lambda T, xa=xa, xb=xb: [(T[xb][:, 0:XD], T[xa][:, 0:XD])], [V(xb, 0, XD)], [V(xa, 0, XD)], 5000)["n"] = 16
+                    cp(V("RU", 16 * lo, 16 * hi), IND(V("RI"), V("LP", lo, hi)))
+            if l == 0:
+                k = cp(V(xa, p0, p0 + LN), V(cm, 0, LN), pre=("arr%d" % (t - 1) if t else None))
+                if t:
+                    ops[k]["x"].append(send); ops[k]["W"].append(V(cm, 16, LN))
+                else:
+                    cp(V(cm, 128, 256), IND(XA, V("FNu")))
+                for h in (1, 0):
+                    acc(V("PB", 128 * h, 128 * h + 128), [(V(cm, 128 * h, 128 * h + 128), V("ID"))])
+                    act(V("WTT", 128 * h, 128 * h + 128), V("PB", 128 * h, 128 * h + 128), bias=col(16 + h))
+            dma("y", "dc%d" % (2 * t + l), lambda T, xa=xa, xb=xb: [(T[xb][:, 0:XD], T[xa][:, 0:XD])], [V(xb, 0, XD)], [V(xa, 0, XD)], 5000)
+            act(V("RD"), IND(RA, V("LP", 0, 16)))
+            vid = ("V", t, l)
+            mm([(V("PV", 0, 256), V("ID32"), V("RD"), True, False), (V("PV", 0, 256), V("DP"), V("ONE", 0, 256), False, False)], vid)
             kid = ("K", t, l)
             mm([(V("PK", 0, 256), V("ID"), V("KC"), True, False)], kid)
-            c0 = 0
-            for eng, w in TUNE["z"][l]:
-                lo, hi = 512 * c0, 512 * (c0 + w)
-                gather(eng, V("Z", lo, hi), IND(XA, V("RU", lo // 16, hi // 16)))
-                for e in range(c0, c0 + w):
-                    pd = V(("PD0", "PD1", "PC")[e % 3]); pp = ((32 * (e % 4), 32 * (e % 4) + 32),)
-                    acc(pd, [(V("ID"), V("Z", 512 * e, 512 * e + 512)), (V("WTT", 128 * (e // 4), 128 * (e // 4) + 128) + pp, V("SELW") + pp)])
-                    act(V("AB", 512 * e, 512 * e + 512), pd, AF.Abs)
-                    mm([(V("PK", 0, 256), sel(q), V("AB", 256 * q, 256 * q + 256), False, q == 15) for q in (2 * e, 2 * e + 1)], kid)
-                scan(V("MXV", lo, hi), V("MK", 0, hi - lo), V("Z", lo, hi), OP.mult, OP.max)
-                scan(V("MNV", lo, hi), V("RB", 0, hi - lo), V("Z", lo, hi), OP.add, OP.min)
-                c0 += w
-            if l == 1 or t == 1:
-                acting(s, "PB")
-            if l == 1:
-                tt(V("OK", 8, 16), V("OK", 8, 16), V("acN", 8, 16), OP.mult)
-                act(V("OK", 0, 8), V("acN", 0, 8), AF.Identity)
+            for n_, e in enumerate(TUNE["zo"][l]):
+                z = rings("V", e, TUNE["z"][e], XA)
+                pd = V("PD%d" % (n_ % 2)); pp = ((32 * (e % 4), 32 * (e % 4) + 32),)
+                acc(pd, [(V("ID"), z), (V("WTT", 128 * (e // 4), 128 * (e // 4) + 128) + pp, V("SELW") + pp)])
+                act(V("AB", 512 * e, 512 * e + 512), pd, AF.Abs)
+                mm([(V("PK", 0, 256), sel(q), V("AB", 256 * q, 256 * q + 256), False, n_ == 7 and q % 2 == 1) for q in (2 * e, 2 * e + 1)], kid)
             if l == 0:
                 if t < RO - 1:
-                    act(V("N%d" % t), V("NI", p0, p0 + LN), AF.Identity, scale=1.0 / C)
-                act(V("AD", 0, 128), V("EQ", t, t + 128), AF.Identity, bias=col(15 + t), scale=1.0 / C)
-                if t == 0:
-                    act(V("NF"), IND(V("NI"), V("FNu")), AF.Identity, scale=1.0 / C)
+                    act(V("N%d" % t), V("NI", p0, p0 + LN), scale=1.0 / C)
+                act(V("AD", 0, 128), V("EQ", t, t + 128), bias=(p0 - t) / C, scale=1.0 / C)
                 nf = V("N%d" % (t - 1)) if t else V("NF")
-            middle("MXV", "MNV", 0, 256, "PM")
-            act(V("EV"), V("PM", 0, 256), AF.Abs, bias=col(12))
+            middle("V", 0, 8, "PM", TUNE["z"], cm)
+            act(V("EV"), V("PM", 0, 256), AF.Abs, bias=-MAGIC)
+            did = ("D", t, l)
+            acc(V("PX", 0, 16), comb("EV", s="S0N"), True, False, did)
             if l == 0:
                 ts(V("LE"), V("PM", 0, 256), MAGIC, OP.is_le)
-            scan(V("KS"), V("RB", 0, 256), V("PK", 0, 256), OP.add, OP.min)
-            ts(V("K1", 0, 16), V("KS", 15, 256, 16), 16.0, OP.mult)
-            ts(V("K1", 16, 32), V("K1", 0, 16), 15, OP.bitwise_and)
-            cp(V("KB"), V("K1", 16, 32))
-            mm([(V("PN", 16 * q, 16 * q + 16), V("BC", 128 * q, 128 * q + 128), V("KB"), True, True) for q in range(16)])
-            ts(V("OH"), V("PN", 0, 256), col(0), OP.is_equal)
-            tt(V("PRD"), IND(RA, V("LP", 0, 16)), V("OH"), OP.mult)
-            blocks(V("PA", 0, 16), "PRD")
-            ts(V("CI", 0, 16), V("PA", 0, 16), float(C), OP.mult)
-            blocks(V("PB", 0, 16), "EV")
-            ok = V("ac" + s)
-            act(V("AP_"), ok, AF.Identity, bias=V("AC", 0, 1), scale=8192.0)
-            tt(V("TH"), V("PB", 0, 16), V("AP_"), OP.add)
-            if l == 0:
-                mm([(V("PM", 256, 512), V("BO"), V("LE"), True, True)])
-                ts(V("SB_"), V("PM", 256, 512), col(9), OP.mult, col(10), OP.is_ge)
+                acc(V("PM", 256, 512), [(V("BO"), V("LE"))])
+                act(V("SB_"), V("PM", 256, 512), AF.Sign, bias=col(11), scale=col(10))
                 tt(V("KP"), IND(V("KF"), V("LP", 0, 16)), V("SB_"), OP.mult)
-                comb(V("PB", 0, 16), "KP"); blocks(V("PB", 16, 32), "KP")
-                nodes("N", V("PB", 0, 32))
-            tt(V("DL", 0, 16), V("CI", 0, 16), V("DMX"), OP.subtract)
-            lowest(V("CI", 0, 16), "c", True, "PA")
-            act(V("XC"), IND(XA, V("CU", 0, 16)), AF.Identity)
-            acc(V("PN", 0, 256), [(V("H5"), V("XC")), (V("H5"), V("WJ")), (V("QI"), V("ONE")), (V("MI"), V("ONE"))])
-            act(V("NW"), V("PN", 0, 256), AF.Identity, bias=col(12))
-            tt(V("DL", 16, 32), V("PA", 0, 16), V("THR"), OP.is_lt)
-            tt(V("DL", 32, 48), V("DL", 16, 32), V("DL", 0, 16), OP.mult)
-            tt(V("DL", 16, 32), V("DL", 32, 48), V("DMX"), OP.add)
-            cp(V("XU"), V("DL", 16, 32))
-            act(V("NT"), V("NS"), AF.Identity)
-            act(V("RD", 128, 256), IND(RA, V("LQ", 0, 8)), AF.Identity)
-            tt(V("AD", 128, 256), IND(RA, V("LQ", 0, 8)), nf, OP.is_equal)
+                acc(V("PM", 0, 16), comb("KP"))
+                nodes("N", V("PM", 0, 16))
+                act(V("NP"), IND(V("SW", 0, 256), V("puN", 8, 16)), scale=-1.0 / 16)
+                acc(V("PM", 16, 24), comb("NP", 0, 128))
+                act(V("SP"), V("PM", 16, 24))
+            scan(V("KS"), V("RB", 0, 256), V("PK", 0, 256), OP.add, OP.min)
+            ts(V("K1"), V("KS", 15, 256, 16), MAGIC, OP.add, MAGIC, OP.subtract)
+            tt(V("KB", 0, 16), V("KS", 15, 256, 16), V("K1"), OP.subtract)
+            ts(V("KB", 16, 32), V("KB", 0, 16), -0.5, OP.mult)
+            mm(spread("PV", V("KB", 0, 16), False, True), vid)
+            cid = ("C", t, l)
+            mm(spread("PK", V("KB", 16, 32), True, False), cid)
+            ts(V("PRD"), V("PV", 0, 256), 0.0, OP.max, 4096.0, OP.min)
+            acc(V("PK", 0, 256), [(V("BO"), V("PRD"))], False, True, cid)
+            acc(V("PV", 256, 272), [(V("ID"), V("M1K"))] + comb("PRD"))
+            act(V("CW"), V("PK", 0, 256), bias=-31744.0)
+            ts(V("CN", 16, 32), V("PV", 256, 272), 4096 * MAGIC, OP.add, 4096 * MAGIC, OP.subtract)
+            tt(V("CN", 0, 16), V("PV", 256, 272), V("CN", 16, 32), OP.subtract)
+            ts(V("CU"), V("CN", 0, 16), 1024.0, OP.add)
+            ts(V("DA"), V("CN", 0, 16), 1.0 / 128, OP.mult, 8.0, OP.add)
+            ts(V("DB"), V("CN", 0, 16), 1023.5, OP.is_ge, 16.0, OP.mult)
+            lowest("CW", "CN", "c", "PK", 256)
+            act(V("XC"), IND(XA, V("CU")))
+            acc(V("PD0", 0, 256), [(V("H5"), V(cm)), (V("QI"), V("ONE", 0, 256)), (V("H5"), V("XC")), (V("MI"), V("ONE", 0, 256))])
+            act(V("NW"), V("PD0", 0, 256), bias=-MAGIC)
+            acc(V("PV", 272, 288), [(V("ID"), V("DA")), (V("ID"), V("DB"))] + comb("SGc"))
+            tt(V("DL"), V("PV", 272, 288), V("DMX"), OP.min)
+            ts(V("XU"), V("DL"), 128.0, OP.mult, float(C), OP.add)
+            ac = V("ac" + s)
+            act(V("AP_"), ac, bias=V("AC", 0, 1), scale=8192.0)
+            if lv[0]:
+                act(V("NT"), V("NS"), scale=256.0)
+            tt(V("AD", 128, 256), V("RD", 128, 256), nf, OP.is_equal)
+            tt(V("LT", 0, 16), V("LF", 0, 16), V("DUM", 16, 32), OP.subtract)
+            tt(V("LT", 16, 32), V("LT", 0, 16), ac, OP.mult)
             if l == 1:
-                ok = V("OK")
-            tt(V("LT", 0, 16), V("LF", 32, 48), V("DUM", 16, 32), OP.subtract)
-            tt(V("LT", 16, 32), V("LT", 0, 16), ok, OP.mult)
+                tt(V("LT", 24, 32), V("LT", 24, 32), V("OK"), OP.mult)
             tt(V("BS", 16, 32), V("LT", 16, 32), V("DUM", 16, 32), OP.add)
-            act(V("DT", 24, 32), V("LT", 24, 32), AF.Identity, scale=-1.0)
-            tt(V("DT", 0, 16), V("pr" + s, 16, 32), V("DUM", 32, 48), OP.subtract)
-            act(V("DT", 16, 24), V("TT", 16, 24), AF.Identity, scale=2.0)
-            if l == 0:
-                act(V("NP"), IND(V("SW", 0, 256), V("puN")), AF.Identity, scale=-16.0)
-                comb(V("PB", 0, 16), "NP")
-                act(V("SP"), V("PB", 0, 16), AF.Identity)
-            did = ("D", t, l)
-            c0 = 0; m0 = 0
-            for eng, w, mid in TUNE["u"][l]:
-                lo, hi = 256 * c0, 256 * (c0 + w)
-                gather(eng, V("ZU", lo, hi), IND(XA, V("RU", 256 + lo // 16, 256 + hi // 16)))
-                scan(V("MXU", lo, hi), V("MK", 0, hi - lo), V("ZU", lo, hi), OP.mult, OP.max)
-                scan(V("MNU", lo, hi), V("RB", 0, hi - lo), V("ZU", lo, hi), OP.add, OP.min)
-                c0 += w
-                if mid:
-                    lo, hi = 16 * m0, 16 * c0
-                    middle("MXU", "MNU", lo, hi, "PM")
-                    act(V("EU", lo, hi), V("PM", lo, hi), AF.Abs, bias=col(12))
-                    mm([(V("PK", 0, 16), sel(a), V("EU", 16 * a, 16 * a + 16), a == 0, a == 15) for a in range(m0, c0)], did)
-                    m0 = c0
+            act(V("DT", 24, 32), V("LT", 24, 32), scale=-1.0)
+            tt(V("DT", 0, 16), V("pr" + s), V("DUM", 32, 48), OP.subtract)
+            act(V("DT", 16, 24), V("TT", 0, 8), scale=2.0)
+            m0 = 0
+            for e in range(8):
+                rings("U", e, TUNE["u"][l][e], XA)
+                if e + 1 in (TUNE["cut"][l], 8):
+                    lo, hi = 32 * m0, 32 * e + 32
+                    middle("U", m0, e + 1, "PB", TUNE["u"][l], cm)
+                    act(V("EU", lo, hi), V("PB", lo, hi), AF.Abs, bias=-MAGIC)
+                    acc(V("PX", lo // 16, hi // 16), comb("EU", lo, hi), False, e == 7, did)
+                    m0 = e + 1
             cp(IND(XB, V("XU")), V("NW"))
             if l == 1 and not last:
-                go = "GO%d" % t
-                if t == 0:
-                    act(V("G1"), IND(V(xb, 0, XD), V("FNu")), AF.Identity)
-                    act(V(go), IND(V("G1"), V("SNu")), AF.Identity)
-                else:
-                    act(V(go), IND(V(xb, p0 - LN, p0), V("SNu")), AF.Identity)
+                go = "GO%d" % t; nm = "CM%d" % (t + 1)
+                act(V(go), IND(V(xb, p0 - LN, p0), V("SNu")) if t else IND(V(xb, 0, XD), V("FSu")))
                 send = ops[add("p", lambda q, T, x, t=t: x["send"](t), [], [V(go)], 1500, sem="loc", n=0, lat=TUNE["far"])]
+                cp(V(nm, 0, 16), V(go, 0, 16))
+                cp(V(nm, 128, 256), V(xb, p0, p0 + LN))
             if last:
-                dma("y", "ox0", lambda T: [(T.yx[:, 0:1024], T.X0[:, 0:1024])], [], [V("X0", 0, 1024)], 3000)["n"] = 16
-                dma("y", "ox1", lambda T: [(T.yx[:, 1024:2048], T.X0[:, 1024:2048])], [], [V("X0", 1024, 2048)], 3000)["n"] = 16
-            for r, w in ((0, 16), (16, 16)):
-                tt(V("EX", r, r + w), V("PK", 0, w), V("TH", 0, w), OP.is_lt)
+                dma("y", "ox0", lambda T: [(T.yx[:, 0:1024], T.X0[:, 0:1024])], [], [V("X0", 0, 1024)], 3000)
+                dma("y", "ox1", lambda T: [(T.yx[:, 1024:2048], T.X0[:, 1024:2048])], [], [V("X0", 1024, 2048)], 3000)
+            for r in (0, 16):
+                tt(V("EX", r, r + 16), V("PX", 0, 16), V("AP_"), OP.is_lt)
             tt(V("LT", 0, 32), V("EX"), V("DT"), OP.mult)
             tt(V("LT", 32, 64), V("LT", 0, 32), V("BS"), OP.add)
-            cp(V("LU"), V("LT", 32, 64))
+            ts(V("LU"), V("LT", 32, 64), 256.0, OP.mult)
             act(IND(V("SW"), V("LU", 0, 16)), V("NT"), AF.Tanh)
             nx = "N" if l == 0 else "EO"[(t + 1) & 1]
             if not last:
-                act(V("NS"), IND(V("SW", 0, 256), V("pu" + nx)), AF.Identity, scale=-16.0)
+                act(V("NS"), IND(V("SW", 0, 256), V("pu" + nx)), scale=-1.0 / 16)
             tt(V("RD", 0, 128), IND(RA, V("LU", 16, 24)), V("KE", t, t + 128), OP.mult)
             tt(IND(RA, V("LU", 16, 32)), V("RD"), V("AD"), OP.max)
             if not last:
                 lv[0] += 1
+                if l == 0 or t == 0:
+                    acting(nx)
                 places(nx, False)
-                mm([(V("PN", 0, 16), V("BO"), V("EX", 0, 16), True, True)])
-                act(V("JK"), V("PN", 0, 16), AF.Identity, bias=col(14), scale=-1.0, total=V("AC", 0, 1))
-    act(V("NS"), V("SW", 0, 256), AF.Identity, scale=16.0)
-    comb(V("PA", 0, 16), "NS")
-    ts(V("TT", 0, 16), V("PA", 0, 16), 0.5, OP.mult, -128.0, OP.add)
-    ts(V("TT", 16, 32), V("PA", 0, 16), 0.5, OP.mult, 128.0, OP.add)
-    tt(V("LF", 0, 16), V("JQ"), V("TT", 0, 16), OP.subtract)
-    tt(V("LF", 16, 32), V("JQ"), V("TT", 16, 32), OP.add)
-    cp(V("FU"), V("LF", 0, 32))
+                acc(V("PM", 32, 48), [(V("BO"), V("EX", 0, 16))])
+                act(V("JK"), V("PM", 32, 48), bias=-512.0, scale=-1.0, total=V("AC", 0, 1))
+    act(V("NS"), V("SW", 0, 256), scale=-1.0 / 32)
+    acc(V("PX", 16, 32), comb("NS"))
+    tt(V("LF", 0, 16), V("PX", 16, 32), V("DUM", 48, 64), OP.add)
+    tt(V("LF", 16, 32), V("DUM", 48, 64), V("PX", 16, 32), OP.subtract)
+    ts(V("FU"), V("LF"), 256.0, OP.mult)
     ts(V("RO_"), IND(V("RW"), V("FU")), float(C), OP.mult)
-    act(V("KO"), IND(V("KF"), V("FU")), AF.Identity)
-    dma("y", "oyr", lambda T: [(T.yr[:, :], T.RO_[:, :])], [], [V("RO_")], 2500)["n"] = 16
-    dma("s", "oyk", lambda T: [(T.yk[r:16:2, :], T.KO[r:128:16, :]) for r in range(2)], [], [V("KO")], 2500)["n"] = 32
+    act(V("KO"), IND(V("KF"), V("FU")), scale=512.0)
+    dma("y", "oyr", lambda T: [(T.yr[:, :], T.RO_[:, :])], [], [V("RO_")], 2500)
+    dma("s", "oyk", lambda T: [(T.yk[r:16:2, :], T.KO[r:128:16, :]) for r in range(2)], [], [V("KO")], 2500, 32)
     return ops
 
 
-TURN = {}
 PLAN = {}
 
 
 def kind(o):
     w = o["W"][0] if o["W"] else ("", 0)
-    return w[0] + ("b" if w[0] in ("RU", "TT", "LF", "LT", "AD", "RD", "DT", "DL", "Z", "EU") and (w[1] > 0 and w[0] != "Z" or w[0] == "Z" and o["e"] == "v") else "") + \
-        ("s" if o["lv"] < 0 else str(o["lv"] % 2))
+    return w[0] + ("b" if w[0] in ("RU", "LF", "LT", "AD", "RD", "DT", "EU", "KB", "CN", "WTT") and w[1] > 0 else "") + str(o["lv"])
 
 
 def schedule(ops):
-    n = len(ops); others = []; mid = (TUNE["G"], TUNE["S"])
+    n = len(ops); others = []; mid = (TUNE["G"], TUNE["S"], TUNE["PE"])
     for rates in TUNE["others"] + [mid]:
-        TUNE["G"], TUNE["S"] = rates
+        TUNE["G"], TUNE["S"], TUNE["PE"] = rates
         others.append([o["c"] for o in build()])
     others.pop()
     for k, o in enumerate(ops):
@@ -501,7 +483,7 @@ def schedule(ops):
         for w, vs in ((False, o["R"]), (True, o["W"])):
             for v in vs:
                 h = hist[v[0]]
-                if w and v[3] == 1 and v[0] not in PS:
+                if w and abs(v[3]) == 1 and len(v) == 4 and v[0] not in PS:
                     h[:] = [e for e in h if not (v[1] <= e[1] and e[2] <= v[2])]
                 if v[0] in PS and o["e"] == "t":
                     h[:] = [e for e in h if ops[e[0]]["e"] == "t"][-40:]
@@ -516,64 +498,56 @@ def schedule(ops):
     def gap(j, k):
         return ops[j]["lat"] + (TUNE["same"] if ops[j]["e"] == ops[k]["e"] else TUNE["cross"]) * (0 if j not in pred[k] and not ops[j]["lat"] else 1)
     fw = [[(j, gap(k, j)) for j in succ[k]] for k in range(n)]
-    bw = [[(j, gap(j, k)) for j in allp[k]] for k in range(n)]
+    eng = [o["e"] for o in ops]; cost0 = [o["c"] for o in ops]; lat = [o["lat"] for o in ops]; npred = [len(p) for p in allp]; look = TUNE["look"]
 
-    def run(nxt, prv, pri, back, look):
-        left = [len(p) for p in prv]; ready = [ops[k]["lat"] if back else 0.0 for k in range(n)]; free = {e: 0.0 for e in "vstpy"}
+    def run(pri):
+        left = list(npred); ready = [0.0] * n; free = {e: 0.0 for e in "vstpy"}
         pool = {e: [] for e in "vstpy"}; seq = []; at = [0.0] * n; end = 0.0
         for k in range(n):
             if not left[k]:
-                pool[ops[k]["e"]].append(k)
+                pool[eng[k]].append(k)
         for _ in range(n):
             t0, e = min((max(free[e], min(ready[k] for k in pool[e])), e) for e in pool if pool[e])
             k = max((k for k in pool[e] if ready[k] <= t0 + look), key=lambda k: pri[k])
             pool[e].remove(k); at[k] = max(t0, ready[k])
-            free[e] = at[k] + ops[k]["c"]; end = max(end, free[e] + (0 if back else ops[k]["lat"])); seq.append(k)
-            for j, d in nxt[k]:
-                ready[j] = max(ready[j], free[e] + d); left[j] -= 1
+            f = free[e] = at[k] + cost0[k]; end = max(end, f + lat[k]); seq.append(k)
+            for j, d in fw[k]:
+                if f + d > ready[j]:
+                    ready[j] = f + d
+                left[j] -= 1
                 if not left[j]:
-                    pool[ops[j]["e"]].append(j)
+                    pool[eng[j]].append(j)
         return end, seq, at
-    rank = {nm: r for r, names in enumerate(TUNE["first"]) for nm in names.split()}
-    keys = [kind(o) for o in ops]
-    off = {}
-    for key, o in zip(keys, ops):
-        if o["e"] in "vs" and o["W"]:
-            nm = o["W"][0][0]
-            if o["lv"] < 0:
-                off[key] = -1e6 if nm in TUNE["head"].split() else -8000 if nm in TUNE["early"].split() else 9000 if nm in TUNE["late"].split() else 2000
-            else:
-                off[key] = 0 if key[:3] in ("RU0", "RU1") else 3000 * rank.get(nm, TUNE["rest"])
-    off.update(TURN)
 
     def again(seq, cost):
         ready = [0.0] * n; free = {e: 0.0 for e in "vstpy"}; end = 0.0
         for k in seq:
-            e = ops[k]["e"]; f = max(ready[k], free[e]) + cost[k]; free[e] = f; end = max(end, f + ops[k]["lat"])
+            e = eng[k]; f = max(ready[k], free[e]) + cost[k]; free[e] = f; end = max(end, f + lat[k])
             for j, d in fw[k]:
                 if f + d > ready[j]:
                     ready[j] = f + d
         return end
+    keys = [kind(o) for o in ops]
+    tail = [0.0] * n
+    for k in range(n - 1, -1, -1):
+        tail[k] = cost0[k] + max([d + tail[j] for j, d in fw[k]] + [lat[k]])
 
     def tried(off):
         p = [0.0] * n
         for k in range(n - 1, -1, -1):
-            o = ops[k]
-            if o["e"] in "vs":
-                p[k] = -25000.0 * max(o["lv"], 0) - off.get(keys[k], 0) - 0.01 * k
-            else:
-                p[k] = max([p[j] for j in succ[k]] + [-1e9])
-        r = run(fw, bw, p, False, TUNE["look"])
+            p[k] = tail[k] + off[keys[k]] if eng[k] in "vsp" else max([p[j] + 1 for j in succ[k]] + [-1e9])
+        r = run(p)
         return (r[0] + sum(again(r[1], c) for c in others),) + r
-    best = tried(off); names = sorted(k for k in off if off[k] > -1e5); z = [TUNE["seed"]]
+    off = {k: 0.0 for k in keys}
+    best = tried(off); names = sorted({keys[k] for k in range(n) if eng[k] in "vsp"}); z = [TUNE["seed"]]
 
     def pick(xs):
         z[0] = (z[0] * 6364136223846793005 + 1442695040888963407) % 2 ** 64
         return xs[(z[0] >> 33) % len(xs)]
     for _ in range(TUNE["tries"]):
         o = dict(off)
-        for _ in range(pick([1, 1, 2, 3])):
-            o[pick(names)] += pick([-1, 1]) * pick([500, 1500, 3000, 6000, 12000])
+        for _ in range(pick([1, 2, 3, 5])):
+            o[pick(names)] += pick([-1, 1]) * pick([300, 1000, 2000, 4000, 8000])
         r = tried(o)
         if r[0] <= best[0]:
             best, off = r, o
@@ -658,6 +632,12 @@ def forward(g, T, topo, src, r, ds, buf, lo, t):
     return sum(len(e) for e in sh)
 
 
+def even_run(ds):
+    step = ds[1] - ds[0]
+    assert all(b - a == step for a, b in zip(ds, ds[1:]))
+    return slice(ds[0], ds[-1] + 1, step)
+
+
 def rank_program(g, core, T, topo):
     rank = T.rank_of(core)
     if rank is None:
@@ -687,7 +667,8 @@ def rank_program(g, core, T, topo):
         g.remote_dma_fused(trs, local_sem=T.sem["loc"])
         sent[0] += forward(g, T, topo, core, rank, near, go, 16, t)
 
-    x = {"order": [0] + near + [d for h, ds in helpers for d in ds], "send": send}
+    k0 = 1 + len(near)
+    x = {"runs": [(slice(0, k0), even_run([0] + near)), (slice(k0, N), even_run([d for h, ds in helpers for d in ds]))], "send": send}
     qs = {"v": g.vector, "s": g.scalar, "t": g.tensor, "p": g, "y": g.sync}
     come = arrivals(T, topo, rank); seen = set()
     for k in seq:

@@ -8,21 +8,21 @@ XD, XN = 2064, 2320
 BF, F32, I32, U16, F16 = "bfloat16", "float32", "int32", "uint16", "float16"
 SB = {
     "X0": (XN, BF), "X1": (XN, BF), "RI": (512, I32), "RW": (768, F32), "SW": (512, F32), "NT": (256, F32), "KI": (512, I32), "KF": (512, F32),
-    "NI": (2048, F32), "RT": (16, I32), "FNi": (8, I32), "SNi": (8, I32), "FNu": (8, U16), "SNu": (8, U16), "FSu": (8, U16), "FSw": (128, F16),
+    "NI": (256, F32), "FNh": (8, F16), "RT": (16, I32), "FNi": (8, I32), "SNi": (8, I32), "FNu": (8, U16), "SNu": (8, U16), "FSu": (8, U16), "FSw": (128, F16),
     "CM0": (256, BF), "CM1": (256, BF), "CM2": (256, BF), "GO0": (128, BF), "GO1": (128, BF), "HL0": (128, BF), "HL1": (128, BF),
     "IOT": (144, BF), "X16": (256, BF), "PI": (8, I32), "PJ": (16, I32), "CF": (32, F32), "ID": (128, BF), "H5": (128, BF), "NG": (128, BF),
     "QI": (128, BF), "MI": (128, BF), "DP": (128, BF), "ID32": (128, F32), "BO": (128, BF), "G16": (128, BF), "S0": (144, BF), "S0N": (144, BF),
-    "ONE": (512, BF), "BIG": (512, BF), "KC": (256, BF), "RB": (512, BF), "MK": (512, BF), "BC": (2048, BF), "SELW": (512, BF), "ZOFF": (512, BF),
-    "RC": (256, BF), "JQ": (16, F32), "WT": (16, F32), "THW": (256, BF), "RR": (256, BF), "M1K": (16, BF), "DUM": (64, F32), "DMX": (16, F32),
+    "ONE": (512, BF), "BIG": (512, BF), "KC": (256, BF), "RB": (2048, BF), "MK": (2048, BF), "BC": (2048, BF), "SELW": (512, BF), "ZOFF": (512, BF),
+    "RC": (256, BF), "WT": (32, F32), "Fc": (576, F16), "Fp": (576, F16), "THW": (256, BF), "RR": (256, BF), "M1K": (16, BF), "DUM": (64, F32), "DMX": (16, F32),
     "ZV": (4096, BF), "HV": (4096, F16), "ZU": (4096, BF), "HU": (4096, F16),
     "MXV": (4096, F16), "MNV": (4096, F16), "MXU": (4096, F16), "MNU": (4096, F16), "AB": (4096, BF),
     "RU": (512, U16), "WTT": (256, F16), "KS": (256, F32), "K1": (16, F32), "KB": (32, BF), "PRD": (256, F16), "CW": (256, F16), "CN": (32, F32),
     "CU": (16, U16), "DA": (16, F16), "DB": (16, BF), "Ec": (2176, BF), "SGc": (256, BF), "DL": (16, F32), "XU": (16, U16), "XC": (256, BF), "NW": (256, BF),
-    "PW": (256, F16), "Ep": (2176, BF), "SGp": (256, BF),
+    "SV": (256, F32), "AW": (256, F16), "BON": (128, BF), "PW": (256, F16), "Ep": (2176, BF), "SGp": (256, BF),
     "EV": (256, BF), "EU": (256, BF), "LE": (256, BF), "SB_": (256, BF), "KP": (256, F16), "NS": (256, BF), "NP": (128, BF), "SP": (8, F32),
     "TT": (16, F32), "LF": (32, F32), "LP": (32, U16), "AC": (8, F32), "AP_": (16, F32), "OK": (8, F32),
-    "BS": (32, F32), "DT": (32, F32), "EX": (32, BF), "LT": (64, F32), "LU": (32, U16), "RD": (256, F32), "AD": (256, F32), "KE": (144, F32),
-    "EQ": (144, F32), "JK2": (144, F32), "NF": (128, F32), "N0": (128, F32), "N1": (128, F32), "JK": (16, F32), "VV": (32, F32),
+    "BS": (32, F32), "DT": (32, F32), "EX": (32, BF), "LT": (64, F32), "LU": (32, U16), "RD": (256, F32), "AD": (256, F32), "KE": (144, BF),
+    "S0Q": (144, BF), "NF": (128, F32), "N0": (128, F32), "N1": (128, F32), "JK": (16, F32), "VV": (32, F32),
     "RO_": (512, F32), "KO": (512, F32), "FU": (32, U16),
 }
 for _s in "EON":
@@ -37,11 +37,14 @@ for _k, (_w, _d) in SB.items():
         AT[_k] = ("all_" + _d, _fill.get(_d, 0)); _fill[_d] = _fill.get(_d, 0) + (_w + 15) // 16 * 16
 SCRATCH.update({"all_" + d: ("sbuf", [128, w], d) for d, w in _fill.items()})
 SCRATCH.update({k: ("psum", [128, 512], F32) for k in PS})
-DMAS = ["dx0", "dx1", "dring", "dkid", "drt", "dfn", "dsn", "dxl", "ox0", "ox1", "oyr", "oyk"] + ["dc%d" % k for k in range(2 * RO)]
+DMAS = ["dx0", "dx1", "dring", "dkid", "drt", "dfn", "dsn", "dxl", "ox0", "ox1", "oyr0", "oyr1", "oyk", "dMK", "dRB"] + ["dc%d" % k for k in range(2 * RO)]
 SEMAPHORES = ["ev", "es", "et", "ep", "arr0", "arr1", "hin0", "hin1", "loc"] + DMAS
-TUNE = {"z": "vvsvvvsv", "u": ["ssssssss", "ssssssss"], "cut": [8, 8], "zo": [[4, 5, 6, 7, 0, 1, 2, 3], [0, 1, 2, 3, 4, 5, 6, 7]],
-        "others": [(1.15, 2.0, 0.45), (2.0, 5.5, 0.45), (1.56, 3.8, 0.6)], "seed": 1, "tries": 1500, "G": 1.56, "S": 3.8, "PE": 0.45,
-        "same": 70, "cross": 140, "far": 5000, "look": 40}
+TUNE = {
+    "z": "vSsvvsvv", "u": ["SSsSsSsv", "SSsSssSs"], "zo": [[4, 5, 6, 7, 0, 1, 2, 3], [0, 1, 2, 3, 4, 5, 6, 7]], "cut": [8, 6], "wide": [0, 1],
+    "span": 128, "share": {"c": [0, 32], "p": [0, 0, 128]}, "on_s": "KB DA DT CM1 CM2 KC RC WT DMX BON S0Q QI MI DP S0N H5 NG".split(),
+    "F": 1.0, "G": 1.56, "S": 3.8, "PE": 0.45, "far": 4500, "same": 70, "cross": 140,
+    "others": [(1.1, 1.15, 2.0, 0.5, 7000), (1.1, 2.0, 5.5, 0.45, 3500), (1.4, 1.6, 3.0, 0.6, 5500)],
+    "seed": 1, "first": 40, "turns": 30, "tries": 200, "width": 200, "slack": 250, "ways": [0, 1, 1]}
 
 
 def V(name, lo=0, hi=None, step=1):
@@ -86,12 +89,8 @@ def build():
     def two(*vs):
         return all(v[0] in SB and SB[v[0]][1] in (BF, U16, F16) for v in vs)
 
-    def vc(o, a, f):
-        if o[0] == "@":
-            return 50 + TUNE["S"] * cols(o)
-        if a[0] == "@":
-            return 50 + TUNE["G"] * cols(a)
-        return max(64, f * cols(a))
+    def vc(o, a, f, fixed=50):
+        return TUNE["F"] * (fixed + 0.83 * (TUNE["S"] * cols(o) if o[0] == "@" else TUNE["G"] * cols(a) if a[0] == "@" else f * cols(a)))
 
     def cp(o, a, pre=None):
         return add("v", lambda q, T, x: q.tensor_copy(ap(T, o), ap(T, a)), [o], [a], vc(o, a, 0.5 if "@" not in (o[0], a[0]) and two(o, a) else 1), pre=pre)
@@ -107,16 +106,22 @@ def build():
         add("v", f, [o], [a, s1, s2], vc(o, a, 0.5 if two(o, a) else 1))
 
     def ms(o, c):
-        add("v", lambda q, T, x: q.memset(ap(T, o), c), [o], [], max(64, cols(o) * (0.5 if two(o) else 1)))
+        add("v", lambda q, T, x: q.memset(ap(T, o), c), [o], [], vc(o, o, 0.5 if two(o) else 1))
 
     def scan(o, d0, d1, op0, op1, first=0.0):
-        add("v", lambda q, T, x: q.tensor_tensor_scan(ap(T, o), ap(T, d0), ap(T, d1), first, op0, op1), [o], [d0, d1], max(64, cols(o) * (0.5 if two(o, d0, d1) else 1)))
+        add("v", lambda q, T, x: q.tensor_tensor_scan(ap(T, o), ap(T, d0), ap(T, d1), first, op0, op1), [o], [d0, d1], vc(o, o, 0.5 if two(o, d0, d1) else 1))
 
     def act(o, a, fn=AF.Identity, bias=0.0, scale=1.0, total=None):
         add("s", lambda q, T, x: q.activation(ap(T, o), ap(T, a), fn) if o[0] == "@" else
             q.activation(ap(T, o), ap(T, a), fn, bias=ap(T, bias), scale=ap(T, scale), accum_out=ap(T, total)),
             [o] + ([total] if total else []), [a, bias, scale],
-            (65 + TUNE["G"] * cols(a) if a[0] == "@" else 65 + TUNE["S"] * cols(a) if o[0] == "@" else max(64, 30 + cols(a))) + (140 if total else 0))
+            vc(o, a, 1, 65) + (140 if total else 0))
+
+    def lin(o, a, mul=1.0, plus=0.0):
+        if o[0] in TUNE["on_s"]:
+            act(o, a, bias=plus, scale=mul)
+        else:
+            ts(o, a, mul, OP.mult, plus, OP.add)
 
     def mm(ms_, grp=None):
         def f(q, T, x):
@@ -168,18 +173,21 @@ def build():
     iota(V("IOT"), [[1, 144]], 0, 0)
     iota(V("G16"), [[16, 8], [0, 16]], 0, 0)
     iota(V("X16"), [[0, 16], [1, 16]], 0, 0)
-    iota(V("JQ"), [[16, 16]], 0, 1)
+    iota(V("DUM"), [[128, 2], [256, 2], [16, 16]], 128, 1)
     iota(V("SELW"), [[1, 32], [0, 16]], 0, 0)
     iota(V("ZOFF"), [[0, 2], [256, 16], [0, 16]], -2048, 0)
     iota(V("NI", 0, 256), [[1, 256]], 0, 0)
-    iota(V("NT"), [[0, 256]], -16, 0)
-    iota(V("RW", 512, 768), [[0, 256]], 0, 0)
     ms(V("ONE"), 1.0); ms(V("BIG"), 131072.0)
-    pick_(V("MK"), V("ONE"), [[0, 32], [1, 16]], OP.not_equal, 0, 0)
-    pick_(V("RB"), V("BIG"), [[0, 32], [1, 16]], OP.is_equal, 0, 0)
+    act(V("SW", 0, 256), V("ONE", 0, 256), AF.Tanh, scale=16.0)
+    ops[-1]["c"] += 1300
+    act(V("NT"), V("ONE", 0, 256), scale=32.0 if TUNE["wide"][0] else -16.0)
+    act(V("RW", 512, 768), V("ONE", 0, 256), scale=0.0)
+    pick_(V("MK", 0, 512), V("ONE"), [[0, 32], [1, 16]], OP.not_equal, 0, 0)
+    pick_(V("RB", 0, 512), V("BIG"), [[0, 32], [1, 16]], OP.is_equal, 0, 0)
+    for nm in ("MK", "RB"):
+        dma("y", "d" + nm, lambda T, nm=nm: [(ap(T, V(nm, b, b + 512)), ap(T, V(nm, 0, 512))) for b in (512, 1024, 1536)], [V(nm, 512, 2048)], [V(nm, 0, 512)], 2500, 48)
     for m in range(4):
         pick_(V("BC", 512 * m, 512 * m + 512), V("BIG"), [[-1, 4], [-16, 8], [0, 16]], OP.is_equal, -4 * m, 1)
-    iota(V("NI", 256, 2048), [[1, 1792]], 256, 0)
     ts(V("PJ", 0, 1), V("PI", 0, 1), 15, OP.bitwise_and)
     ts(V("PJ", 1, 2), V("PI", 0, 1), 31, OP.bitwise_and)
     cp(V("CF", 0, 2), V("PJ", 0, 2))
@@ -197,49 +205,47 @@ def build():
     for h in range(2):
         ts(col(16 + h), col(0), 256.0, OP.mult, -2048.0, OP.add)
         for e in range(4):
-            if TUNE["z"][4 * h + e] == "s":
+            if TUNE["z"][4 * h + e] != "v":
                 ms(col(16 + h) + ((32 * e, 32 * e + 32),), 0.0)
-    for nm, c in (("ID", 1.0), ("H5", 0.5), ("NG", -1.0), ("QI", -0.25), ("MI", MAGIC), ("DP", col(6)), ("ID32", float(C))):
-        ts(V(nm), V("IOT", 0, 128), col(3), OP.is_equal, c, OP.mult)
+    ts(V("ID"), V("IOT", 0, 128), col(3), OP.is_equal)
+    for nm, c in (("H5", 0.5), ("NG", -1.0), ("QI", -0.25), ("MI", MAGIC), ("DP", col(6)), ("ID32", float(C))):
+        lin(V(nm), V("ID"), c)
     ts(V("BO"), V("G16"), col(4), OP.is_equal)
+    lin(V("BON"), V("BO"), -1.0)
     ts(V("S0"), V("IOT"), col(5), OP.is_equal)
-    ts(V("S0N"), V("IOT"), col(5), OP.is_equal, -1.0, OP.mult)
-    ts(V("KC"), V("X16"), 1.0 / 16, OP.mult, -15.0 / 32, OP.add)
-    ts(V("RC"), V("X16"), col(13), OP.mult, col(14), OP.add)
+    lin(V("S0N"), V("S0"), -1.0)
+    lin(V("KC"), V("X16"), 1.0 / 16, -15.0 / 32)
+    lin(V("RC"), V("X16"), col(13), col(14))
     ts(V("SELW"), V("SELW"), col(1), OP.is_equal, -1.0, OP.mult)
-    ts(V("JQ"), V("JQ"), col(4), OP.subtract)
+    ts(V("DUM"), V("DUM"), col(4), OP.subtract, 1.0 / 256, OP.mult)
     ms(V("RR"), 0.5703125)
     scan(V("THW"), V("RR"), V("ONE", 0, 256), OP.mult, OP.mult, 1.5e28)
     acc(V("PA", 0, 16), comb("THW"))
-    ts(V("WT"), V("PA", 0, 16), 1.0 / (16 * 2.54), OP.mult)
+    lin(V("WT", 0, 16), V("PA", 0, 16), 1.0 / (16 * 2.54)); lin(V("WT", 16, 32), V("PA", 0, 16), -16.0 / 2.54)
     ms(V("M1K"), -1024.0)
-    for k, c in enumerate((256, 512, 384, 128)):
-        ts(V("DUM", 16 * k, 16 * k + 16), V("JQ"), float(c), OP.add, 1.0 / 256, OP.mult)
-    cp(V("BS", 0, 16), V("DUM", 0, 16))
-    ts(V("DMX"), V("JQ"), float(XD - C), OP.add, 1.0 / 128, OP.mult)
+    lin(V("DMX"), V("DUM", 0, 16), 2.0, (XD - C - 128) / 128)
     ms(V("X0", 2048, XD), 0.0)
-    act(V("SW", 0, 256), V("NT"), AF.Tanh, scale=-1.0)
-    ops[-1]["c"] += 1300
     ts(V("RW", 0, 512), V("RI"), 1.0 / C, OP.mult)
-    ts(V("KE", 0, 128), V("X16", 0, 128), col(0), OP.not_equal)
-    ts(V("KE", 128, 144), V("X16", 0, 16), col(0), OP.not_equal)
-    act(V("JK2"), V("KE"), scale=-8192.0)
-    tt(V("EQ"), V("JK2"), V("NI", 0, 144), OP.add)
+    ts(V("KE"), V("X16", 0, 144), col(0), OP.not_equal)
     cp(V("FNu"), V("FNi"))
     for k in range(2):
         add("v", lambda q, T, x, k=k: q.tensor_copy(T.SNu[:, x["runs"][k][0]], T.SNi[:, x["runs"][k][1]]), [V("SNu")], [V("SNi")], 64)
-    ts(V("KF"), V("KI"), 1.0 / 512, OP.mult)
-    act(V("NF"), IND(V("NI"), V("FNu")), scale=1.0 / C)
-    act(V("FSw"), IND(V("NF"), V("SNu")), scale=128.0)
-    acc(V("PB", 0, 8), comb("FSw", 0, 128))
-    cp(V("FSu"), V("PB", 0, 8))
+    cp(V("KF"), V("KI"))
+    lin(V("S0Q"), V("S0"), 1.0 / 512)
+    cp(V("FNh"), V("FNi"))
 
-    def lowest(wide, key, s, bank, lo):
-        gid = ("T", len(ops)); at = 0; part = [(V(bank, lo, lo + 256), V("NG"), V("THW"), True, False)]
+    def lowest(wide, key, s, bank, lo, span=256):
+        gid = ("T", len(ops)); at = 0; ad = 0; part = [(V(bank, lo, lo + 256), V("NG"), V("THW"), True, False)]
         for i in range(16):
-            e = V("E" + s, at, at + 256 - 16 * i); at = e[2]
-            ts(e, V(wide, 16 * i, 256), V(key, i, i + 1), OP.is_equal, V("WT", i, i + 1), OP.mult)
-            part.append((V(bank, lo + 16 * i, lo + 256), V("BO"), e, False, i == 15))
+            end = (16 * i // span + 1) * span; w = end - 16 * i
+            e = V("E" + s, at, at + w); at += w
+            if w > TUNE["share"][s][2 if lv[0] < 0 else lv[0] % 2]:
+                ts(e, V(wide, 16 * i, end), V(key, i, i + 1), OP.is_equal, V("WT", i, i + 1), OP.mult)
+            else:
+                d = V("F" + s, ad, ad + w); ad += w
+                act(d, V(wide, 16 * i, end), AF.Abs, bias=V(key, i, i + 1), scale=-1.0)
+                act(e, d, AF.Relu, bias=V("WT", i, i + 1), scale=V("WT", 16 + i, 17 + i))
+            part.append((V(bank, lo + 16 * i, lo + end), V("BO"), e, False, i == 15))
             if i % 4 == 3:
                 mm(part, gid); part = []
         act(V("SG" + s), V(bank, lo, lo + 256), AF.Sign)
@@ -253,7 +259,7 @@ def build():
         act(V("PW"), IND(V("NI", 0, 256), V("pu" + s)), bias=0.5, scale=1.0 / 256)
         lowest("PW", "pr" + s, "p", "PA", 0)
         acc(V("PA", 256, 272), comb("SGp"))
-        ts(V("ac" + s), V("PA", 256, 272), 0.0, OP.is_lt)
+        act(V("ac" + s), V("PA", 256, 272), AF.Relu, scale=0.25)
 
     def places(s, first):
         if first:
@@ -265,41 +271,51 @@ def build():
         tt(V("LF", 16, 32), V("pr" + s), V("TT"), OP.add)
         ts(V("LP"), V("LF"), 256.0, OP.mult)
         if s == "N":
-            tt(V("OK"), V("PX", 24, 32), V("SP"), OP.is_equal)
+            tt(V("OK"), V("PX", 24, 32), V("SP"), OP.mult)
 
     ts(V("VV", 0, 16), V("RT"), 1.0 / 256, OP.mult)
     nodes("E", V("VV", 0, 16)); places("E", True)
     cp(V("VV", 16, 24), V("VV", 8, 16)); cp(V("VV", 24, 32), V("VV", 0, 8))
     nodes("O", V("VV", 16, 32))
-    ms(V("AC", 0, 1), -8192.0)
+    ms(V("AC", 0, 1), 0.0); lin(V("DT", 0, 16), V("ONE", 0, 16), -4.0); lin(V("DT", 24, 32), V("ONE", 0, 8), 4.0)
     acting("E")
+    mm([(V("PA", 272 + a, 400, 16), V("BC", 128 * a, 128 * a + 128), V("FNh"), a == 0, a == 15) for a in range(16)])
+    act(V("NF"), V("PA", 272, 400), scale=1.0 / (131072 * C))
+    act(V("FSw"), IND(V("NF"), V("SNu")), scale=128.0)
 
-    def rings(r, e, eng, XA):
-        lo, hi = 512 * e, 512 * e + 512; u = 256 * (r == "U") + 32 * e
+    def rings(r, e, engs, XA, use=None):
+        lo, hi = 512 * e, 512 * e + 512; u = 256 * (r == "U") + 32 * e; eng = engs[e]
         src = IND(XA, V("RU", u, u + 32))
+        z = ("H" if eng == "v" else "Z") + r
         if eng == "v":
-            z = "H" + r
             tt(V(z, lo, hi), src, V("ZOFF"), OP.add)
-            for b in (lo, lo + 256):
+        else:
+            act(V(z, lo, hi), src)
+        if use:
+            use(V(z, lo, hi))
+        if eng == "S":
+            return
+        if eng == "s":
+            lo -= 512 * (e - len(engs[:e].rstrip("S")))
+            scan(V("MX" + r, lo, hi), V("MK", 0, hi - lo), V(z, lo, hi), OP.mult, OP.max)
+            scan(V("MN" + r, lo, hi, -1), V("RB", 0, hi - lo), V(z, lo, hi, -1), OP.add, OP.min)
+        else:
+            for b in range(lo, hi, 256):
                 scan(V("MX" + r, b + 1, b + 256, 2), V(z, b, b + 256, 2), V(z, b + 1, b + 256, 2), OP.max, OP.max, -4096.0)
                 scan(V("MN" + r, b, b + 255, -2), V(z, b, b + 255, -2), V(z, b + 1, b + 256, -2), OP.min, OP.min, 4096.0)
-        else:
-            z = "Z" + r
-            act(V(z, lo, hi), src)
-            scan(V("MX" + r, lo, hi), V("MK"), V(z, lo, hi), OP.mult, OP.max)
-            scan(V("MN" + r, lo, hi, -1), V("RB"), V(z, lo, hi, -1), OP.add, OP.min)
-        return V(z, lo, hi)
 
     def middle(r, e0, e1, bank, engs, cm):
         lo, hi = 32 * e0, 32 * e1; o = V(bank, lo, hi)
-        part = [(o, V("NG"), V(cm, lo, hi), True, False)]; e = e0
-        while e < e1:
-            f = e
-            while f < e1 and engs[f] == engs[e]:
-                f += 1
-            part.append((V(bank, 32 * e, 32 * f), V("BO"), V("RC", 32 * e, 32 * f), False, False) if engs[e] == "v" else
-                        (V(bank, 32 * e, 32 * f), V("QI"), V("ONE", 32 * e, 32 * f), False, False))
-            e = f
+        part = []
+        for kinds_, lhs, rhs in (("sv", "NG", cm), ("s", "QI", "ONE"), ("v", "BO", "RC")):
+            e = e0
+            while e < e1:
+                f = e
+                while f < e1 and engs[f].lower() in kinds_:
+                    f += 1
+                if f > e:
+                    part.append((V(bank, 32 * e, 32 * f), V(lhs), V(rhs, 32 * e, 32 * f), not part, False))
+                e = f + 1
         gid = ("M", len(ops)); mm(part, gid)
         mm([(o, V("H5"), V("MX" + r, 16 * lo + 15, 16 * hi, 16), False, False), (o, V("H5"), V("MN" + r, 16 * lo, 16 * hi, 16), False, False),
             (o, V("MI"), V("ONE", lo, hi), False, True)], gid)
@@ -334,35 +350,39 @@ def build():
             mm([(V("PV", 0, 256), V("ID32"), V("RD"), True, False), (V("PV", 0, 256), V("DP"), V("ONE", 0, 256), False, False)], vid)
             kid = ("K", t, l)
             mm([(V("PK", 0, 256), V("ID"), V("KC"), True, False)], kid)
+            zs = TUNE["z"]
             for n_, e in enumerate(TUNE["zo"][l]):
-                z = rings("V", e, TUNE["z"][e], XA)
-                pd = V("PD%d" % (n_ % 2)); pp = ((32 * (e % 4), 32 * (e % 4) + 32),)
-                acc(pd, [(V("ID"), z), (V("WTT", 128 * (e // 4), 128 * (e // 4) + 128) + pp, V("SELW") + pp)])
+                pd = V(("PD0", "PD1", "PB")[n_ % 3]); pp = ((32 * (e % 4), 32 * (e % 4) + 32),); gid = ("P", t, l, e)
+                minus_w = (V("WTT", 128 * (e // 4), 128 * (e // 4) + 128) + pp, V("SELW") + pp)
+                if n_ < 3:
+                    acc(pd, [minus_w], True, False, gid)
+                    rings("V", e, zs, XA, lambda z: acc(pd, [(V("ID"), z)], False, True, gid))
+                else:
+                    rings("V", e, zs, XA, lambda z: acc(pd, [(V("ID"), z), minus_w]))
                 act(V("AB", 512 * e, 512 * e + 512), pd, AF.Abs)
                 mm([(V("PK", 0, 256), sel(q), V("AB", 256 * q, 256 * q + 256), False, n_ == 7 and q % 2 == 1) for q in (2 * e, 2 * e + 1)], kid)
             if l == 0:
                 if t < RO - 1:
-                    act(V("N%d" % t), V("NI", p0, p0 + LN), scale=1.0 / C)
-                act(V("AD", 0, 128), V("EQ", t, t + 128), bias=(p0 - t) / C, scale=1.0 / C)
+                    act(V("N%d" % t), V("NI", 0, LN), bias=p0 / C, scale=1.0 / C)
+                acc(V("PM", 0, 128), [(V("MI"), V("KE", t, t + 128)), (V("NG"), V("IOT", 0, 128))])
+                act(V("AD", 0, 128), V("PM", 0, 128), bias=p0 / C, scale=-1.0 / C)
                 nf = V("N%d" % (t - 1)) if t else V("NF")
-            middle("V", 0, 8, "PM", TUNE["z"], cm)
+            middle("V", 0, 8, "PM", zs, cm)
             act(V("EV"), V("PM", 0, 256), AF.Abs, bias=-MAGIC)
-            did = ("D", t, l)
-            acc(V("PX", 0, 16), comb("EV", s="S0N"), True, False, did)
             if l == 0:
                 ts(V("LE"), V("PM", 0, 256), MAGIC, OP.is_le)
                 acc(V("PM", 256, 512), [(V("BO"), V("LE"))])
                 act(V("SB_"), V("PM", 256, 512), AF.Sign, bias=col(11), scale=col(10))
-                tt(V("KP"), IND(V("KF"), V("LP", 0, 16)), V("SB_"), OP.mult)
-                acc(V("PM", 0, 16), comb("KP"))
+                tt(V("KP"), IND(V("KI"), V("LP", 0, 16)), V("SB_"), OP.mult)
+                acc(V("PM", 0, 16), comb("KP", s="S0Q"))
                 nodes("N", V("PM", 0, 16))
                 act(V("NP"), IND(V("SW", 0, 256), V("puN", 8, 16)), scale=-1.0 / 16)
                 acc(V("PM", 16, 24), comb("NP", 0, 128))
-                act(V("SP"), V("PM", 16, 24))
+                act(V("SP"), V("PM", 16, 24), scale=-4.0)
             scan(V("KS"), V("RB", 0, 256), V("PK", 0, 256), OP.add, OP.min)
             ts(V("K1"), V("KS", 15, 256, 16), MAGIC, OP.add, MAGIC, OP.subtract)
             tt(V("KB", 0, 16), V("KS", 15, 256, 16), V("K1"), OP.subtract)
-            ts(V("KB", 16, 32), V("KB", 0, 16), -0.5, OP.mult)
+            lin(V("KB", 16, 32), V("KB", 0, 16), -0.5)
             mm(spread("PV", V("KB", 0, 16), False, True), vid)
             cid = ("C", t, l)
             mm(spread("PK", V("KB", 16, 32), True, False), cid)
@@ -373,74 +393,101 @@ def build():
             ts(V("CN", 16, 32), V("PV", 256, 272), 4096 * MAGIC, OP.add, 4096 * MAGIC, OP.subtract)
             tt(V("CN", 0, 16), V("PV", 256, 272), V("CN", 16, 32), OP.subtract)
             ts(V("CU"), V("CN", 0, 16), 1024.0, OP.add)
-            ts(V("DA"), V("CN", 0, 16), 1.0 / 128, OP.mult, 8.0, OP.add)
-            ts(V("DB"), V("CN", 0, 16), 1023.5, OP.is_ge, 16.0, OP.mult)
-            lowest("CW", "CN", "c", "PK", 256)
+            lin(V("DA"), V("CN", 0, 16), 1.0 / 128, 8.0)
+            act(V("DB"), V("CN", 0, 16), AF.Relu, bias=-16.0 * 1023, scale=16.0)
+            lowest("CW", "CN", "c", "PK", 256, TUNE["span"])
             act(V("XC"), IND(XA, V("CU")))
             acc(V("PD0", 0, 256), [(V("H5"), V(cm)), (V("QI"), V("ONE", 0, 256)), (V("H5"), V("XC")), (V("MI"), V("ONE", 0, 256))])
             act(V("NW"), V("PD0", 0, 256), bias=-MAGIC)
             acc(V("PV", 272, 288), [(V("ID"), V("DA")), (V("ID"), V("DB"))] + comb("SGc"))
             tt(V("DL"), V("PV", 272, 288), V("DMX"), OP.min)
             ts(V("XU"), V("DL"), 128.0, OP.mult, float(C), OP.add)
-            ac = V("ac" + s)
-            act(V("AP_"), ac, bias=V("AC", 0, 1), scale=8192.0)
+            idle = V("ac" + s)
+            act(V("AP_"), idle, bias=V("AC", 0, 1), scale=-2048.0)
+            wide = TUNE["wide"][l]
             if lv[0]:
-                act(V("NT"), V("NS"), scale=256.0)
+                act(V("NT"), V("NS"), scale=-512.0 if wide else 256.0)
             tt(V("AD", 128, 256), V("RD", 128, 256), nf, OP.is_equal)
-            tt(V("LT", 0, 16), V("LF", 0, 16), V("DUM", 16, 32), OP.subtract)
-            tt(V("LT", 16, 32), V("LT", 0, 16), ac, OP.mult)
+            tt(V("BS", 16, 32), V("LF", 0, 16), idle, OP.add)
             if l == 1:
-                tt(V("LT", 24, 32), V("LT", 24, 32), V("OK"), OP.mult)
-            tt(V("BS", 16, 32), V("LT", 16, 32), V("DUM", 16, 32), OP.add)
-            act(V("DT", 24, 32), V("LT", 24, 32), scale=-1.0)
-            tt(V("DT", 0, 16), V("pr" + s), V("DUM", 32, 48), OP.subtract)
+                tt(V("BS", 24, 32), V("BS", 24, 32), V("OK"), OP.max)
             act(V("DT", 16, 24), V("TT", 0, 8), scale=2.0)
-            m0 = 0
+            if wide:
+                tt(V("LT", 32, 48), V("pr" + s), idle, OP.add)
+                tt(V("LT", 0, 16), V("LT", 32, 48), V("DUM", 16, 32), OP.min)
+                ts(V("LU", 0, 16), V("LT", 0, 16), 256.0, OP.mult, -128.0, OP.add)
+                act(V("AW"), V("ONE", 0, 256), bias=-0.5, scale=V("AC", 0, 1))
+            else:
+                act(V("BS", 0, 16), V("pr" + s), bias=3.5)
+
+            def signs(lo, hi):
+                wid = ("W", t, l, lo)
+                acc(V("PD1", lo, hi), [(V("BON"), V("EV", lo, hi)), (V("NG"), V("AW", lo, hi))], True, False, wid)
+                acc(V("PD1", lo, hi), [(V("BO"), V("EU", lo, hi))], False, True, wid)
+                tt(V("SV", lo, hi), V("PD1", lo, hi), V("NT", lo, hi), OP.mult)
+                act(IND(V("SW"), V("LU", lo // 16, hi // 16)), V("SV", lo, hi), AF.Tanh)
+
+            m0 = 0; did = ("D", t, l)
+            acc(V("PX", 0, 16), comb("EV", s="S0N"), True, False, did)
             for e in range(8):
-                rings("U", e, TUNE["u"][l][e], XA)
+                rings("U", e, TUNE["u"][l], XA)
                 if e + 1 in (TUNE["cut"][l], 8):
                     lo, hi = 32 * m0, 32 * e + 32
                     middle("U", m0, e + 1, "PB", TUNE["u"][l], cm)
                     act(V("EU", lo, hi), V("PB", lo, hi), AF.Abs, bias=-MAGIC)
-                    acc(V("PX", lo // 16, hi // 16), comb("EU", lo, hi), False, e == 7, did)
+                    if wide:
+                        signs(lo, hi)
                     m0 = e + 1
-            cp(IND(XB, V("XU")), V("NW"))
+            acc(V("PX", 0, 16), comb("EU"), False, True, did)
+            r0 = 16 * wide
+            for r in range(r0, 32, 16):
+                tt(V("EX", r, r + 16), V("PX", 0, 16), V("AP_"), OP.is_lt)
+            tt(V("LT", r0, 32), V("EX", r0, 32), V("DT", r0, 32), OP.mult)
+            tt(V("LT", 32 + r0, 64), V("LT", r0, 32), V("BS", r0, 32), OP.add)
+            tt(V("LT", r0, 32), V("LT", 32 + r0, 64), V("DUM", 32 + r0, 64), OP.min)
+            ts(V("LU", r0, 32), V("LT", r0, 32), 256.0, OP.mult)
+            if not wide:
+                act(IND(V("SW"), V("LU", 0, 16)), V("NT"), AF.Tanh)
+            tt(V("RD", 0, 128), IND(RA, V("LU", 16, 24)), V("KE", t, t + 128), OP.mult)
+            tt(IND(RA, V("LU", 16, 32)), V("RD"), V("AD"), OP.max)
+            for b in range(256, 0, -TUNE["span"]):
+                cp(IND(XB, V("XU", (b - TUNE["span"]) // 16, b // 16)), V("NW", b - TUNE["span"], b))
             if l == 1 and not last:
                 go = "GO%d" % t; nm = "CM%d" % (t + 1)
                 act(V(go), IND(V(xb, p0 - LN, p0), V("SNu")) if t else IND(V(xb, 0, XD), V("FSu")))
                 send = ops[add("p", lambda q, T, x, t=t: x["send"](t), [], [V(go)], 1500, sem="loc", n=0, lat=TUNE["far"])]
-                cp(V(nm, 0, 16), V(go, 0, 16))
-                cp(V(nm, 128, 256), V(xb, p0, p0 + LN))
+                lin(V(nm, 0, 16), V(go, 0, 16))
+                lin(V(nm, 128, 256), V(xb, p0, p0 + LN))
             if last:
                 dma("y", "ox0", lambda T: [(T.yx[:, 0:1024], T.X0[:, 0:1024])], [], [V("X0", 0, 1024)], 3000)
                 dma("y", "ox1", lambda T: [(T.yx[:, 1024:2048], T.X0[:, 1024:2048])], [], [V("X0", 1024, 2048)], 3000)
-            for r in (0, 16):
-                tt(V("EX", r, r + 16), V("PX", 0, 16), V("AP_"), OP.is_lt)
-            tt(V("LT", 0, 32), V("EX"), V("DT"), OP.mult)
-            tt(V("LT", 32, 64), V("LT", 0, 32), V("BS"), OP.add)
-            ts(V("LU"), V("LT", 32, 64), 256.0, OP.mult)
-            act(IND(V("SW"), V("LU", 0, 16)), V("NT"), AF.Tanh)
             nx = "N" if l == 0 else "EO"[(t + 1) & 1]
             if not last:
                 act(V("NS"), IND(V("SW", 0, 256), V("pu" + nx)), scale=-1.0 / 16)
-            tt(V("RD", 0, 128), IND(RA, V("LU", 16, 24)), V("KE", t, t + 128), OP.mult)
-            tt(IND(RA, V("LU", 16, 32)), V("RD"), V("AD"), OP.max)
-            if not last:
                 lv[0] += 1
                 if l == 0 or t == 0:
                     acting(nx)
                 places(nx, False)
-                acc(V("PM", 32, 48), [(V("BO"), V("EX", 0, 16))])
-                act(V("JK"), V("PM", 32, 48), bias=-512.0, scale=-1.0, total=V("AC", 0, 1))
+                acc(V("PM", 32, 48), [(V("BO"), V("EX", 16, 32))])
+                act(V("JK"), V("PM", 32, 48), scale=-1.0, total=V("AC", 0, 1))
+                if lv[0] == 1:
+                    acc(V("PM", 48, 56), comb("FSw", 0, 128))
+                    cp(V("FSu"), V("PM", 48, 56))
     act(V("NS"), V("SW", 0, 256), scale=-1.0 / 32)
     acc(V("PX", 16, 32), comb("NS"))
-    tt(V("LF", 0, 16), V("PX", 16, 32), V("DUM", 48, 64), OP.add)
-    tt(V("LF", 16, 32), V("DUM", 48, 64), V("PX", 16, 32), OP.subtract)
-    ts(V("FU"), V("LF"), 256.0, OP.mult)
-    ts(V("RO_"), IND(V("RW"), V("FU")), float(C), OP.mult)
-    act(V("KO"), IND(V("KF"), V("FU")), scale=512.0)
-    dma("y", "oyr", lambda T: [(T.yr[:, :], T.RO_[:, :])], [], [V("RO_")], 2500)
-    dma("s", "oyk", lambda T: [(T.yk[r:16:2, :], T.KO[r:128:16, :]) for r in range(2)], [], [V("KO")], 2500, 32)
+    tt(V("LF", 0, 16), V("PX", 16, 32), V("DUM", 0, 16), OP.add)
+    tt(V("LF", 16, 32), V("DUM", 0, 16), V("PX", 16, 32), OP.subtract)
+    for h in range(2):
+        ts(V("FU", 16 * h, 16 * h + 16), V("LF", 16 * h, 16 * h + 16), 256.0, OP.mult)
+        fu = V("FU", 16 * h, 16 * h + 16)
+        if h:
+            act(V("RO_", 256, 512), IND(V("RW"), fu), scale=float(C))
+            act(V("KO", 256, 512), IND(V("KF"), fu))
+        else:
+            ts(V("RO_", 0, 256), IND(V("RW"), fu), float(C), OP.mult)
+            cp(V("KO", 0, 256), IND(V("KF"), fu))
+        dma("y", "oyr%d" % h, lambda T, h=h: [(T.yr[:, 256 * h:256 * h + 256], T.RO_[:, 256 * h:256 * h + 256])], [], [V("RO_", 256 * h, 256 * h + 256)], 2300)
+    dma("y", "oyk", lambda T: [(T.yk[r:16:2, :], T.KO[r:128:16, :]) for r in range(2)], [], [V("KO")], 2500, 32)
     return ops
 
 
@@ -449,14 +496,14 @@ PLAN = {}
 
 def kind(o):
     w = o["W"][0] if o["W"] else ("", 0)
-    return w[0] + ("b" if w[0] in ("RU", "LF", "LT", "AD", "RD", "DT", "EU", "KB", "CN", "WTT") and w[1] > 0 else "") + str(o["lv"])
+    return w[0] + ("b" if w[0] in ("RU", "LF", "LT", "AD", "RD", "DT", "EU", "KB", "CN", "WTT") and w[1] > 0 else "") + ("s" if o["lv"] < 0 else str(o["lv"] % 2))
 
 
 def schedule(ops):
-    n = len(ops); others = []; mid = (TUNE["G"], TUNE["S"], TUNE["PE"])
+    n = len(ops); others = []; named = ("F", "G", "S", "PE", "far"); mid = [TUNE[k] for k in named]
     for rates in TUNE["others"] + [mid]:
-        TUNE["G"], TUNE["S"], TUNE["PE"] = rates
-        others.append([o["c"] for o in build()])
+        TUNE.update(zip(named, rates))
+        others.append([(o["c"], o["lat"]) for o in build()])
     others.pop()
     for k, o in enumerate(ops):
         o["k"] = k
@@ -498,60 +545,139 @@ def schedule(ops):
     def gap(j, k):
         return ops[j]["lat"] + (TUNE["same"] if ops[j]["e"] == ops[k]["e"] else TUNE["cross"]) * (0 if j not in pred[k] and not ops[j]["lat"] else 1)
     fw = [[(j, gap(k, j)) for j in succ[k]] for k in range(n)]
-    eng = [o["e"] for o in ops]; cost0 = [o["c"] for o in ops]; lat = [o["lat"] for o in ops]; npred = [len(p) for p in allp]; look = TUNE["look"]
-
-    def run(pri):
-        left = list(npred); ready = [0.0] * n; free = {e: 0.0 for e in "vstpy"}
-        pool = {e: [] for e in "vstpy"}; seq = []; at = [0.0] * n; end = 0.0
-        for k in range(n):
-            if not left[k]:
-                pool[eng[k]].append(k)
-        for _ in range(n):
-            t0, e = min((max(free[e], min(ready[k] for k in pool[e])), e) for e in pool if pool[e])
-            k = max((k for k in pool[e] if ready[k] <= t0 + look), key=lambda k: pri[k])
-            pool[e].remove(k); at[k] = max(t0, ready[k])
-            f = free[e] = at[k] + cost0[k]; end = max(end, f + lat[k]); seq.append(k)
-            for j, d in fw[k]:
-                if f + d > ready[j]:
-                    ready[j] = f + d
-                left[j] -= 1
-                if not left[j]:
-                    pool[eng[j]].append(j)
-        return end, seq, at
+    eng = [o["e"] for o in ops]; cost0 = [o["c"] for o in ops]; lat = [o["lat"] for o in ops]
 
     def again(seq, cost):
         ready = [0.0] * n; free = {e: 0.0 for e in "vstpy"}; end = 0.0
         for k in seq:
-            e = eng[k]; f = max(ready[k], free[e]) + cost[k]; free[e] = f; end = max(end, f + lat[k])
+            e = eng[k]; c, late = cost[k]; f = free[e] = max(ready[k], free[e]) + c; end = max(end, f + late); f += late - lat[k]
             for j, d in fw[k]:
                 if f + d > ready[j]:
                     ready[j] = f + d
         return end
-    keys = [kind(o) for o in ops]
-    tail = [0.0] * n
-    for k in range(n - 1, -1, -1):
-        tail[k] = cost0[k] + max([d + tail[j] for j, d in fw[k]] + [lat[k]])
-
-    def tried(off):
-        p = [0.0] * n
-        for k in range(n - 1, -1, -1):
-            p[k] = tail[k] + off[keys[k]] if eng[k] in "vsp" else max([p[j] + 1 for j in succ[k]] + [-1e9])
-        r = run(p)
-        return (r[0] + sum(again(r[1], c) for c in others),) + r
-    off = {k: 0.0 for k in keys}
-    best = tried(off); names = sorted({keys[k] for k in range(n) if eng[k] in "vsp"}); z = [TUNE["seed"]]
+    bw = [[(j, gap(j, k)) for j in allp[k]] for k in range(n)]
+    z = [TUNE["seed"]]
 
     def pick(xs):
         z[0] = (z[0] * 6364136223846793005 + 1442695040888963407) % 2 ** 64
         return xs[(z[0] >> 33) % len(xs)]
-    for _ in range(TUNE["tries"]):
-        o = dict(off)
-        for _ in range(pick([1, 2, 3, 5])):
-            o[pick(names)] += pick([-1, 1]) * pick([300, 1000, 2000, 4000, 8000])
-        r = tried(o)
-        if r[0] <= best[0]:
-            best, off = r, o
-    PLAN["off"] = off; PLAN["all"] = [best[1]] + [again(best[2], c) for c in others]
+
+    every = list(range(n)); worlds = [list(zip(cost0, lat))] + others; kinds = [kind(o) for o in ops]
+
+    def place(order, prv, first):
+        fin = {}; used = {e: ([], []) for e in "vstpy"}
+        for k in order:
+            t = first[k]
+            for j, d in prv[k]:
+                d += fin[j]
+                if d > t:
+                    t = d
+            s0, s1 = used[eng[k]]; c = cost0[k]; i = m = len(s0)
+            while i and s1[i - 1] > t:
+                i -= 1
+            while i < m and s0[i] < t + c:
+                t = s1[i]; i += 1
+            s0.insert(i, t); s1.insert(i, t + c); fin[k] = t + c
+        return fin
+
+    def improve(seq, a, b, tries):
+        win = seq[a:b]; inside = set(win); frames = []
+        prv = {k: [e for e in bw[k] if e[0] in inside] for k in win}; nxt = {k: [e for e in fw[k] if e[0] in inside] for k in win}
+        for w in worlds:
+            fin = {}; free = {}; rest = {}; head = {}; fixed = 0.0
+            for k in seq[:a]:
+                fin[k] = free[eng[k]] = max([free.get(eng[k], 0.0)] + [fin[j] + d + w[j][1] - lat[j] for j, d in bw[k]]) + w[k][0]
+            for k in reversed(seq[b:]):
+                rest[k] = head[eng[k]] = max([head.get(eng[k], 0.0), w[k][1]] + [rest[j] + d + w[k][1] - lat[k] for j, d in fw[k]]) + w[k][0]
+                fixed = max([fixed] + [fin[j] + d + w[j][1] - lat[j] + rest[k] for j, d in bw[k] if j in fin])
+            frames.append(({k: max([free.get(eng[k], 0.0)] + [fin[j] + d + w[j][1] - lat[j] for j, d in bw[k] if j in fin]) for k in win},
+                           {k: max([head.get(eng[k], 0.0), w[k][1]] + [rest[j] + d + w[k][1] - lat[k] for j, d in fw[k] if j in rest]) for k in win}, fixed))
+        first, after, fixed = frames[0]
+
+        def tried(order):
+            fin = place(order, prv, first)
+            fin = place(sorted(win, key=lambda k: -fin[k]), nxt, after)
+            fin = place(sorted(win, key=lambda k: -fin[k]), prv, first)
+            return max(fixed, max(fin[k] + after[k] for k in win)), fin
+
+        def whole(r):
+            fin = r[1]; order = sorted(win, key=lambda k: fin[k] - cost0[k]); total = r[0]
+            for w, (f0, a0, end) in zip(others, frames[1:]):
+                f = {}; free = {}
+                for k in order:
+                    t = max(f0[k], free.get(eng[k], 0.0))
+                    for j, d in prv[k]:
+                        d += f[j] + w[j][1] - lat[j]
+                        if d > t:
+                            t = d
+                    f[k] = free[eng[k]] = t = t + w[k][0]
+                    if t + a0[k] > end:
+                        end = t + a0[k]
+                total += end
+            before = {}; last = {}
+            for k in order:
+                before[k] = last.get(eng[k]); last[eng[k]] = k
+            k = max(win, key=lambda k: fin[k] + after[k]); held = []
+            while True:
+                j = before[k]; t = fin[k] - cost0[k] - 0.01
+                if j is not None and fin[j] >= t:
+                    held.append((j, k))
+                else:
+                    j = [j for j, d in prv[k] if fin[j] + d >= t]
+                    if not j:
+                        break
+                    j = j[0]
+                k = j
+            return total, r[0], order, fin, held
+        fin = place(win, prv, first)
+        best = now = whole((max(fixed, max(fin[k] + after[k] for k in win)), fin)); alike = {}
+        for k in win:
+            alike.setdefault(kinds[k], []).append(k)
+        names = sorted(alike); text = sorted(win)
+        for it in range(tries):
+            p = {k: now[3][k] - cost0[k] for k in win}; early = pick([0, 1])
+            if now[4] and pick(TUNE["ways"]):
+                x, y = pick(now[4]); k0 = y if early else x
+                d = (p[y] - p[x] + pick([10, 10, 300, 1000, 2000])) * (-1 if early else 1)
+                for k in pick([[k0], [k0], alike[kinds[k0]]]):
+                    p[k] += d
+            else:
+                for _ in range(pick([1, 1, 2, 3])):
+                    d = pick([-1, 1]) * pick([200, 500, 1000, 2000, 4000])
+                    for k in alike[pick(names)]:
+                        p[k] += d
+            for k in (reversed(text) if early else text):
+                for j, d in (nxt[k] if early else prv[k]):
+                    if early and p[j] <= p[k]:
+                        p[k] = p[j] - 0.001
+                    elif not early and p[j] >= p[k]:
+                        p[k] = p[j] + 0.001
+            slack = TUNE["slack"] * (1 - it / tries) * pick([0, 0.3, 1])
+            r = tried(sorted(win, key=lambda k: p[k]))
+            if r[0] > now[1] + slack + 300:
+                continue
+            r = whole(r)
+            if r[0] <= now[0] + slack:
+                now = r
+                if r[0] < best[0]:
+                    best = r
+        return seq[:a] + best[2] + seq[b:]
+
+    def timed(seq):
+        at = [0.0] * n; free = {}
+        for k in seq:
+            at[k] = max([free.get(eng[k], 0.0)] + [at[j] + cost0[j] + d for j, d in bw[k]]); free[eng[k]] = at[k] + cost0[k]
+        return at
+    tail = [0.0] * n
+    for k in range(n - 1, -1, -1):
+        tail[k] = cost0[k] + max([d + tail[j] for j, d in fw[k]] + [lat[k]])
+    seq = improve(sorted(every, key=lambda k: -tail[k]), 0, n, TUNE["first"])
+    for turn in range(TUNE["turns"]):
+        w = TUNE["width"]; a = -(w // 3) * (turn % 3)
+        while a < n:
+            seq = improve(seq, max(a, 0), min(a + w, n), TUNE["tries"]); at = timed(seq); seq.sort(key=lambda k: at[k]); a += w
+    at = timed(seq); best = (0, max(at[k] + cost0[k] + lat[k] for k in every), seq, at)
+    PLAN["bw"] = bw; PLAN["all"] = [best[1]] + [again(best[2], c) for c in others]
     end, seq, at = best[1:]
     seq.sort(key=lambda k: at[k])
     for k in range(n):
@@ -683,7 +809,6 @@ def rank_program(g, core, T, topo):
     for e in "vstp":
         if cnt[e]:
             g.sync.wait_ge(T.sem["e" + e], cnt[e])
-    for o in ops:
-        if o["sem"] in DMAS:
-            g.sync.wait_ge(T.sem[o["sem"]], o["n"])
+    for s, c in {o["sem"]: o["n"] for o in ops if o["sem"] in DMAS}.items():
+        g.sync.wait_ge(T.sem[s], c)
     g.wait_ge(T.sem["loc"], sent[0])

from concourse.bass import DstId, RemoteDMATransfer
from concourse.mybir import AluOpType as OP, ActivationFunctionType as AF

C, NV, LN, RO, N = 2048, 512, 128, 3, 8
B0 = C - LN * RO
MAGIC = 12582912.0
XD, XN = 2064, 2320
BF, F32, I32, U16, F16 = "bfloat16", "float32", "int32", "uint16", "float16"
SB = {
    "X0": (XN, BF), "X1": (XN, BF), "RI": (512, I32), "RW": (768, F32), "SW": (512, F32), "NT": (256, F32), "KI": (512, I32), "KF": (512, F32),
    "NI": (256, F32), "FNh": (8, F16), "RT": (16, I32), "FNi": (8, I32), "SNi": (8, I32), "FNu": (8, U16), "SNu": (8, U16), "FSu": (8, U16), "FSw": (128, F16),
    "CM0": (256, BF), "CM1": (256, BF), "CM2": (256, BF), "GO0": (128, BF), "GO1": (128, BF), "HL0": (128, BF), "HL1": (128, BF),
    "IOT": (144, BF), "X16": (256, BF), "PI": (8, I32), "PJ": (16, I32), "CF": (32, F32), "ID": (128, BF), "H5": (128, BF), "NG": (128, BF),
    "QI": (128, BF), "MI": (128, BF), "DP": (128, BF), "ID32": (128, F32), "BO": (128, BF), "G16": (128, BF), "S0": (144, BF), "S0N": (144, BF),
    "ONE": (512, BF), "BIG": (512, BF), "KC": (256, BF), "RB": (2048, BF), "MK": (2048, BF), "BC": (2048, BF), "SELW": (512, BF), "ZOFF": (512, BF),
    "RC": (256, BF), "WT": (32, F32), "Fc": (576, F16), "Fp": (576, F16), "THW": (256, BF), "RR": (256, BF), "M1K": (16, BF), "DUM": (64, F32), "DMX": (16, F32),
    "ZV": (4096, BF), "HV": (4096, F16), "ZU": (4096, BF), "HU": (4096, F16),
    "MXV": (4096, F16), "MNV": (4096, F16), "MXU": (4096, F16), "MNU": (4096, F16), "AB": (4096, BF),
    "RU": (512, U16), "WTT": (256, F16), "KS": (256, F32), "K1": (16, F32), "KB": (32, BF), "PRD": (256, F16), "CW": (256, F16), "CN": (32, F32),
    "CU": (16, U16), "DA": (16, F16), "DB": (16, BF), "Ec": (2176, BF), "SGc": (256, BF), "DL": (16, F32), "XU": (16, U16), "XC": (256, BF), "NW": (256, BF),
    "SV": (256, F32), "AW": (256, F16), "BON": (128, BF), "PW": (256, F16), "Ep": (2176, BF), "SGp": (256, BF),
    "EV": (256, BF), "EU": (256, BF), "LE": (256, BF), "SB_": (256, BF), "KP": (256, F16), "NS": (256, BF), "NP": (128, BF), "SP": (8, F32),
    "TT": (16, F32), "LF": (32, F32), "LP": (32, U16), "AC": (8, F32), "AP_": (16, F32), "OK": (8, F32),
    "BS": (32, F32), "DT": (32, F32), "EX": (32, BF), "LT": (64, F32), "LU": (32, U16), "RD": (256, F32), "AD": (256, F32), "KE": (144, BF),
    "S0Q": (144, BF), "NF": (128, F32), "N0": (128, F32), "N1": (128, F32), "JK": (16, F32), "VV": (32, F32),
    "RO_": (512, F32), "KO": (512, F32), "FU": (32, U16),
}
for _s in "EON":
    SB.update({"pr" + _s: (16, F32), "sg" + _s: (16, F32), "pu" + _s: (16, U16), "ac" + _s: (16, F32)})
PS = ["PD0", "PD1", "PK", "PV", "PM", "PX", "PA", "PB"]
OWN = ("X0", "X1", "RI", "KI", "RT", "FNi", "SNi", "SNu", "CM0", "CM1", "CM2", "GO0", "GO1", "HL0", "HL1", "RO_", "KO", "AC")
SCRATCH = {k: ("sbuf", [128, SB[k][0]], SB[k][1]) for k in OWN}
AT = {k: (k, 0) for k in list(OWN) + PS}
_fill = {}
for _k, (_w, _d) in SB.items():
    if _k not in OWN:
        AT[_k] = ("all_" + _d, _fill.get(_d, 0)); _fill[_d] = _fill.get(_d, 0) + (_w + 15) // 16 * 16
SCRATCH.update({"all_" + d: ("sbuf", [128, w], d) for d, w in _fill.items()})
SCRATCH.update({k: ("psum", [128, 512], F32) for k in PS})
DMAS = ["dx0", "dx1", "dring", "dkid", "drt", "dfn", "dsn", "dxl", "ox0", "ox1", "oyr0", "oyr1", "oyk", "dMK", "dRB"] + ["dc%d" % k for k in range(2 * RO)]
SEMAPHORES = ["ev", "es", "et", "ep", "arr0", "arr1", "hin0", "hin1", "loc"] + DMAS
TUNE = {
    "z": "vSsvvsvv", "u": ["SSsSsSsv", "SSsSssSs"], "zo": [[4, 5, 6, 7, 0, 1, 2, 3], [0, 1, 2, 3, 4, 5, 6, 7]], "cut": [8, 6], "wide": [0, 1],
    "span": 128, "share": {"c": [0, 32], "p": [0, 0, 128]}, "on_s": "KB DA DT CM1 CM2 KC RC WT DMX BON S0Q QI MI DP S0N H5 NG".split(),
    "F": 1.0, "G": 1.56, "S": 3.8, "PE": 0.45, "far": 4500, "same": 70, "cross": 140,
    "others": [(1.1, 1.15, 2.0, 0.5, 7000), (1.1, 2.0, 5.5, 0.45, 3500), (1.4, 1.6, 3.0, 0.6, 5500)],
    "seed": 1, "first": 40, "turns": 30, "tries": 200, "width": 200, "slack": 250, "ways": [0, 1, 1]}


def V(name, lo=0, hi=None, step=1):
    return (name, lo, (512 if name in PS else SB[name][0]) if hi is None else hi, step)


def IND(win, off):
    return ("@", win, off)


def cols(v):
    return 16 * cols(v[2]) if v[0] == "@" else (v[2] - v[1] + abs(v[3]) - 1) // abs(v[3])


def ap(T, v):
    if not isinstance(v, tuple):
        return v
    if v[0] == "@":
        return ap(T, v[1]).indirect(ap(T, v[2]))
    b, o = AT[v[0]]; p = slice(*v[4]) if len(v) > 4 else slice(None)
    if v[3] < 0:
        return T[b][p, o + v[2] - 1:(o + v[1] - 1 if o + v[1] else None):v[3]]
    return T[b][p, o + v[1]:o + v[2]:v[3]] if v[3] != 1 else T[b][p, o + v[1]:o + v[2]]


def build():
    ops = []; lv = [-1]

    def add(eng, fn, outs, ins, cost, grp=None, sem=None, n=1, lat=0, pre=None):
        R, W = [], []
        for v in ins:
            if isinstance(v, tuple):
                R += [v[1], v[2]] if v[0] == "@" else [v]
        for v in outs:
            if v[0] == "@":
                W.append(v[1]); R.append(v[2])
            else:
                W.append(v)
        ops.append({"e": eng, "f": fn, "R": R, "W": W, "c": cost, "g": grp, "sem": sem, "n": n, "lat": lat, "pre": pre, "x": [], "lv": lv[0]})
        return len(ops) - 1

    def two(*vs):
        return all(v[0] in SB and SB[v[0]][1] in (BF, U16, F16) for v in vs)

    def vc(o, a, f, fixed=50):
        return TUNE["F"] * (fixed + 0.83 * (TUNE["S"] * cols(o) if o[0] == "@" else TUNE["G"] * cols(a) if a[0] == "@" else f * cols(a)))

    def cp(o, a, pre=None):
        return add("v", lambda q, T, x: q.tensor_copy(ap(T, o), ap(T, a)), [o], [a], vc(o, a, 0.5 if "@" not in (o[0], a[0]) and two(o, a) else 1), pre=pre)

    def tt(o, a, b, op):
        add("v", lambda q, T, x: q.tensor_tensor(ap(T, o), ap(T, a), ap(T, b), op), [o], [a, b], vc(o, a, 1 if a[0] in PS or b[0] in PS else 2))

    def ts(o, a, s1, op0, s2=None, op1=None):
        def f(q, T, x):
            if op1 is None:
                return q.tensor_scalar(ap(T, o), ap(T, a), ap(T, s1), None, op0)
            return q.tensor_scalar(ap(T, o), ap(T, a), ap(T, s1), ap(T, s2), op0, op1)
        add("v", f, [o], [a, s1, s2], vc(o, a, 0.5 if two(o, a) else 1))

    def ms(o, c):
        add("v", lambda q, T, x: q.memset(ap(T, o), c), [o], [], vc(o, o, 0.5 if two(o) else 1))

    def scan(o, d0, d1, op0, op1, first=0.0):
        add("v", lambda q, T, x: q.tensor_tensor_scan(ap(T, o), ap(T, d0), ap(T, d1), first, op0, op1), [o], [d0, d1], vc(o, o, 0.5 if two(o, d0, d1) else 1))

    def act(o, a, fn=AF.Identity, bias=0.0, scale=1.0, total=None):
        add("s", lambda q, T, x: q.activation(ap(T, o), ap(T, a), fn) if o[0] == "@" else
            q.activation(ap(T, o), ap(T, a), fn, bias=ap(T, bias), scale=ap(T, scale), accum_out=ap(T, total)),
            [o] + ([total] if total else []), [a, bias, scale],
            vc(o, a, 1, 65) + (140 if total else 0))

    def lin(o, a, mul=1.0, plus=0.0):
        if o[0] in TUNE["on_s"]:
            act(o, a, bias=plus, scale=mul)
        else:
            ts(o, a, mul, OP.mult, plus, OP.add)

    def mm(ms_, grp=None):
        def f(q, T, x):
            for o, l, r, s0, s1 in ms_:
                i = q.matmul(ap(T, o), ap(T, l), ap(T, r), s0, s1)
            return i
        add("t", f, [m[0] for m in ms_], [m[1] for m in ms_] + [m[2] for m in ms_],
            60 + sum(TUNE["PE"] * max(64, cols(m[2])) * (4 if SB[m[1][0]][1] == F32 else 1) for m in ms_), grp)

    def acc(o, pairs, start=True, stop=True, grp=None):
        mm([(o, l, r, start and k == 0, stop and k == len(pairs) - 1) for k, (l, r) in enumerate(pairs)], grp)

    def sel(a, s="S0"):
        return V(s, 15 - a, 143 - a)

    def comb(f, lo=0, hi=256, s="S0"):
        return [(sel(a, s), V(f, lo + a, hi, 16)) for a in range(16)]

    def spread(bank, k, start, stop):
        return [(V(bank, 16 * q, 16 * q + 16), V("BC", 128 * q, 128 * q + 128), k, start and q == 0, stop and q == 15) for q in range(16)]

    def iota(o, pat, base, cm):
        small = SB[o[0]][1] != I32
        add("p", lambda q, T, x: q.iota(ap(T, o), pat, base, cm, allow_small_or_imprecise_dtypes=True) if small else q.iota(ap(T, o), pat, base, cm),
            [o], [], 130 + 2 * cols(o))

    def pick_(o, a, pat, op, base, cm):
        add("p", lambda q, T, x: q.affine_select(ap(T, o), ap(T, a), pat, op, 0.0, base, cm), [o], [a], 170 + 2 * cols(o))

    def dma(eng, sem, pairs, outs, ins, lat, n=16):
        def f(q, T, x):
            for o, a in pairs(T):
                q.dma_start(o, a).then_inc(T.sem[sem], 16)
        add(eng, f, outs, ins, 60 * n // 16, sem=sem, n=n, lat=lat)

    def col(k):
        return V("CF", k, k + 1)

    dma("y", "drt", lambda T: [(T.RT[:, :], T.rt[:, :])], [V("RT")], [], 2000)
    dma("y", "dring", lambda T: [(T.RI[:, :], T.ring[:, :])], [V("RI")], [], 2600)
    dma("s", "dx0", lambda T: [(T.X0[:, 0:1024], T.x[:, 0:1024])], [V("X0", 0, 1024)], [], 3500)
    dma("y", "dx1", lambda T: [(T.X0[:, 1024:2048], T.x[:, 1024:2048])], [V("X0", 1024, 2048)], [], 3700)
    dma("s", "dxl", lambda T: [(T.CM0[:, 0:128], T.xl[:, :])], [V("CM0", 0, 128)], [], 2500)
    dma("s", "dfn", lambda T: [(T.FNi[:, :], T.fn[:, :])], [V("FNi")], [], 2500)
    dma("y", "dsn", lambda T: [(T.SNi[:, :], T.snd[:, :])], [V("SNi")], [], 2500)
    iota(V("KI"), [[0, 512]], 0, 0)
    dma("y", "dkid", lambda T: [(T.KI[r:128:16, :], T.kid[r % 2:16:2, :]) for r in range(4)], [V("KI")], [], 3000, 64)
    iota(V("PI", 0, 2), [[0, 2]], 0, 1)
    iota(V("IOT"), [[1, 144]], 0, 0)
    iota(V("G16"), [[16, 8], [0, 16]], 0, 0)
    iota(V("X16"), [[0, 16], [1, 16]], 0, 0)
    iota(V("DUM"), [[128, 2], [256, 2], [16, 16]], 128, 1)
    iota(V("SELW"), [[1, 32], [0, 16]], 0, 0)
    iota(V("ZOFF"), [[0, 2], [256, 16], [0, 16]], -2048, 0)
    iota(V("NI", 0, 256), [[1, 256]], 0, 0)
    ms(V("ONE"), 1.0); ms(V("BIG"), 131072.0)
    act(V("SW", 0, 256), V("ONE", 0, 256), AF.Tanh, scale=16.0)
    ops[-1]["c"] += 1300
    act(V("NT"), V("ONE", 0, 256), scale=32.0 if TUNE["wide"][0] else -16.0)
    act(V("RW", 512, 768), V("ONE", 0, 256), scale=0.0)
    pick_(V("MK", 0, 512), V("ONE"), [[0, 32], [1, 16]], OP.not_equal, 0, 0)
    pick_(V("RB", 0, 512), V("BIG"), [[0, 32], [1, 16]], OP.is_equal, 0, 0)
    for nm in ("MK", "RB"):
        dma("y", "d" + nm, lambda T, nm=nm: [(ap(T, V(nm, b, b + 512)), ap(T, V(nm, 0, 512))) for b in (512, 1024, 1536)], [V(nm, 512, 2048)], [V(nm, 0, 512)], 2500, 48)
    for m in range(4):
        pick_(V("BC", 512 * m, 512 * m + 512), V("BIG"), [[-1, 4], [-16, 8], [0, 16]], OP.is_equal, -4 * m, 1)
    ts(V("PJ", 0, 1), V("PI", 0, 1), 15, OP.bitwise_and)
    ts(V("PJ", 1, 2), V("PI", 0, 1), 31, OP.bitwise_and)
    cp(V("CF", 0, 2), V("PJ", 0, 2))
    cp(col(3), V("PI", 0, 1))
    tt(col(4), col(3), col(0), OP.subtract)
    ts(col(5), col(4), 15.0, OP.add)
    ts(col(6), col(0), -8192.0, OP.mult, 61440.0, OP.add)
    ts(V("CF", 8, 10), V("IOT", 0, 2), col(0), OP.is_equal)
    tt(col(10), col(9), col(8), OP.subtract)
    ts(col(12), col(8), 7.5, OP.mult, 1.0, OP.add)
    ts(col(11), col(9), -9.5, OP.mult, col(12), OP.add)
    ts(col(13), col(9), -256.0, OP.mult)
    ts(col(15), col(8), -0.25, OP.mult)
    ts(col(14), col(9), 2048.0, OP.mult, col(15), OP.add)
    for h in range(2):
        ts(col(16 + h), col(0), 256.0, OP.mult, -2048.0, OP.add)
        for e in range(4):
            if TUNE["z"][4 * h + e] != "v":
                ms(col(16 + h) + ((32 * e, 32 * e + 32),), 0.0)
    ts(V("ID"), V("IOT", 0, 128), col(3), OP.is_equal)
    for nm, c in (("H5", 0.5), ("NG", -1.0), ("QI", -0.25), ("MI", MAGIC), ("DP", col(6)), ("ID32", float(C))):
        lin(V(nm), V("ID"), c)
    ts(V("BO"), V("G16"), col(4), OP.is_equal)
    lin(V("BON"), V("BO"), -1.0)
    ts(V("S0"), V("IOT"), col(5), OP.is_equal)
    lin(V("S0N"), V("S0"), -1.0)
    lin(V("KC"), V("X16"), 1.0 / 16, -15.0 / 32)
    lin(V("RC"), V("X16"), col(13), col(14))
    ts(V("SELW"), V("SELW"), col(1), OP.is_equal, -1.0, OP.mult)
    ts(V("DUM"), V("DUM"), col(4), OP.subtract, 1.0 / 256, OP.mult)
    ms(V("RR"), 0.5703125)
    scan(V("THW"), V("RR"), V("ONE", 0, 256), OP.mult, OP.mult, 1.5e28)
    acc(V("PA", 0, 16), comb("THW"))
    lin(V("WT", 0, 16), V("PA", 0, 16), 1.0 / (16 * 2.54)); lin(V("WT", 16, 32), V("PA", 0, 16), -16.0 / 2.54)
    ms(V("M1K"), -1024.0)
    lin(V("DMX"), V("DUM", 0, 16), 2.0, (XD - C - 128) / 128)
    ms(V("X0", 2048, XD), 0.0)
    ts(V("RW", 0, 512), V("RI"), 1.0 / C, OP.mult)
    ts(V("KE"), V("X16", 0, 144), col(0), OP.not_equal)
    cp(V("FNu"), V("FNi"))
    for k in range(2):
        add("v", lambda q, T, x, k=k: q.tensor_copy(T.SNu[:, x["runs"][k][0]], T.SNi[:, x["runs"][k][1]]), [V("SNu")], [V("SNi")], 64)
    cp(V("KF"), V("KI"))
    lin(V("S0Q"), V("S0"), 1.0 / 512)
    cp(V("FNh"), V("FNi"))

    def lowest(wide, key, s, bank, lo, span=256):
        gid = ("T", len(ops)); at = 0; ad = 0; part = [(V(bank, lo, lo + 256), V("NG"), V("THW"), True, False)]
        for i in range(16):
            end = (16 * i // span + 1) * span; w = end - 16 * i
            e = V("E" + s, at, at + w); at += w
            if w > TUNE["share"][s][2 if lv[0] < 0 else lv[0] % 2]:
                ts(e, V(wide, 16 * i, end), V(key, i, i + 1), OP.is_equal, V("WT", i, i + 1), OP.mult)
            else:
                d = V("F" + s, ad, ad + w); ad += w
                act(d, V(wide, 16 * i, end), AF.Abs, bias=V(key, i, i + 1), scale=-1.0)
                act(e, d, AF.Relu, bias=V("WT", i, i + 1), scale=V("WT", 16 + i, 17 + i))
            part.append((V(bank, lo + 16 * i, lo + end), V("BO"), e, False, i == 15))
            if i % 4 == 3:
                mm(part, gid); part = []
        act(V("SG" + s), V(bank, lo, lo + 256), AF.Sign)

    def nodes(s, v):
        ts(V("sg" + s), v, 1.0, OP.is_ge, -0.5, OP.add)
        tt(V("pr" + s), v, V("sg" + s), OP.subtract)
        ts(V("pu" + s), V("pr" + s), 256.0, OP.mult, -128.0, OP.add)

    def acting(s):
        act(V("PW"), IND(V("NI", 0, 256), V("pu" + s)), bias=0.5, scale=1.0 / 256)
        lowest("PW", "pr" + s, "p", "PA", 0)
        acc(V("PA", 256, 272), comb("SGp"))
        act(V("ac" + s), V("PA", 256, 272), AF.Relu, scale=0.25)

    def places(s, first):
        if first:
            ts(V("TT"), V("sg" + s), -1.0, OP.mult)
        else:
            acc(V("PX", 16, 32), comb("NS"))
            tt(V("TT"), V("PX", 16, 32), V("sg" + s), OP.mult)
        tt(V("LF", 0, 16), V("pr" + s), V("TT"), OP.subtract)
        tt(V("LF", 16, 32), V("pr" + s), V("TT"), OP.add)
        ts(V("LP"), V("LF"), 256.0, OP.mult)
        if s == "N":
            tt(V("OK"), V("PX", 24, 32), V("SP"), OP.mult)

    ts(V("VV", 0, 16), V("RT"), 1.0 / 256, OP.mult)
    nodes("E", V("VV", 0, 16)); places("E", True)
    cp(V("VV", 16, 24), V("VV", 8, 16)); cp(V("VV", 24, 32), V("VV", 0, 8))
    nodes("O", V("VV", 16, 32))
    ms(V("AC", 0, 1), 0.0); lin(V("DT", 0, 16), V("ONE", 0, 16), -4.0); lin(V("DT", 24, 32), V("ONE", 0, 8), 4.0)
    acting("E")
    mm([(V("PA", 272 + a, 400, 16), V("BC", 128 * a, 128 * a + 128), V("FNh"), a == 0, a == 15) for a in range(16)])
    act(V("NF"), V("PA", 272, 400), scale=1.0 / (131072 * C))
    act(V("FSw"), IND(V("NF"), V("SNu")), scale=128.0)

    def rings(r, e, engs, XA, use=None):
        lo, hi = 512 * e, 512 * e + 512; u = 256 * (r == "U") + 32 * e; eng = engs[e]
        src = IND(XA, V("RU", u, u + 32))
        z = ("H" if eng == "v" else "Z") + r
        if eng == "v":
            tt(V(z, lo, hi), src, V("ZOFF"), OP.add)
        else:
            act(V(z, lo, hi), src)
        if use:
            use(V(z, lo, hi))
        if eng == "S":
            return
        if eng == "s":
            lo -= 512 * (e - len(engs[:e].rstrip("S")))
            scan(V("MX" + r, lo, hi), V("MK", 0, hi - lo), V(z, lo, hi), OP.mult, OP.max)
            scan(V("MN" + r, lo, hi, -1), V("RB", 0, hi - lo), V(z, lo, hi, -1), OP.add, OP.min)
        else:
            for b in range(lo, hi, 256):
                scan(V("MX" + r, b + 1, b + 256, 2), V(z, b, b + 256, 2), V(z, b + 1, b + 256, 2), OP.max, OP.max, -4096.0)
                scan(V("MN" + r, b, b + 255, -2), V(z, b, b + 255, -2), V(z, b + 1, b + 256, -2), OP.min, OP.min, 4096.0)

    def middle(r, e0, e1, bank, engs, cm):
        lo, hi = 32 * e0, 32 * e1; o = V(bank, lo, hi)
        part = []
        for kinds_, lhs, rhs in (("sv", "NG", cm), ("s", "QI", "ONE"), ("v", "BO", "RC")):
            e = e0
            while e < e1:
                f = e
                while f < e1 and engs[f].lower() in kinds_:
                    f += 1
                if f > e:
                    part.append((V(bank, 32 * e, 32 * f), V(lhs), V(rhs, 32 * e, 32 * f), not part, False))
                e = f + 1
        gid = ("M", len(ops)); mm(part, gid)
        mm([(o, V("H5"), V("MX" + r, 16 * lo + 15, 16 * hi, 16), False, False), (o, V("H5"), V("MN" + r, 16 * lo, 16 * hi, 16), False, False),
            (o, V("MI"), V("ONE", lo, hi), False, True)], gid)

    send = None
    for t in range(RO):
        p0 = B0 + LN * t
        cm = "CM%d" % t
        for l in range(2):
            s = "N" if l else "EO"[t & 1]
            last = t == RO - 1 and l == 1
            lv[0] = 2 * t + l
            xa, xb = "X%d" % l, "X%d" % (1 - l)
            XA, XB, RA = V(xa, 0, XD), V(xb), V("RW")
            for lo, hi in ((8, 16), (0, 8), (16, 32)) if TUNE["zo"][l][0] >= 4 else ((0, 8), (8, 16), (16, 32)):
                if lv[0]:
                    ts(V("RU", 16 * lo, 16 * hi), IND(RA, V("LP", lo, hi)), float(C), OP.mult)
                else:
                    cp(V("RU", 16 * lo, 16 * hi), IND(V("RI"), V("LP", lo, hi)))
            if l == 0:
                k = cp(V(xa, p0, p0 + LN), V(cm, 0, LN), pre=("arr%d" % (t - 1) if t else None))
                if t:
                    ops[k]["x"].append(send); ops[k]["W"].append(V(cm, 16, LN))
                else:
                    cp(V(cm, 128, 256), IND(XA, V("FNu")))
                for h in (1, 0):
                    acc(V("PB", 128 * h, 128 * h + 128), [(V(cm, 128 * h, 128 * h + 128), V("ID"))])
                    act(V("WTT", 128 * h, 128 * h + 128), V("PB", 128 * h, 128 * h + 128), bias=col(16 + h))
            dma("y", "dc%d" % (2 * t + l), lambda T, xa=xa, xb=xb: [(T[xb][:, 0:XD], T[xa][:, 0:XD])], [V(xb, 0, XD)], [V(xa, 0, XD)], 5000)
            act(V("RD"), IND(RA, V("LP", 0, 16)))
            vid = ("V", t, l)
            mm([(V("PV", 0, 256), V("ID32"), V("RD"), True, False), (V("PV", 0, 256), V("DP"), V("ONE", 0, 256), False, False)], vid)
            kid = ("K", t, l)
            mm([(V("PK", 0, 256), V("ID"), V("KC"), True, False)], kid)
            zs = TUNE["z"]
            for n_, e in enumerate(TUNE["zo"][l]):
                pd = V(("PD0", "PD1", "PB")[n_ % 3]); pp = ((32 * (e % 4), 32 * (e % 4) + 32),); gid = ("P", t, l, e)
                minus_w = (V("WTT", 128 * (e // 4), 128 * (e // 4) + 128) + pp, V("SELW") + pp)
                if n_ < 3:
                    acc(pd, [minus_w], True, False, gid)
                    rings("V", e, zs, XA, lambda z: acc(pd, [(V("ID"), z)], False, True, gid))
                else:
                    rings("V", e, zs, XA, lambda z: acc(pd, [(V("ID"), z), minus_w]))
                act(V("AB", 512 * e, 512 * e + 512), pd, AF.Abs)
                mm([(V("PK", 0, 256), sel(q), V("AB", 256 * q, 256 * q + 256), False, n_ == 7 and q % 2 == 1) for q in (2 * e, 2 * e + 1)], kid)
            if l == 0:
                if t < RO - 1:
                    act(V("N%d" % t), V("NI", 0, LN), bias=p0 / C, scale=1.0 / C)
                acc(V("PM", 0, 128), [(V("MI"), V("KE", t, t + 128)), (V("NG"), V("IOT", 0, 128))])
                act(V("AD", 0, 128), V("PM", 0, 128), bias=p0 / C, scale=-1.0 / C)
                nf = V("N%d" % (t - 1)) if t else V("NF")
            middle("V", 0, 8, "PM", zs, cm)
            act(V("EV"), V("PM", 0, 256), AF.Abs, bias=-MAGIC)
            if l == 0:
                ts(V("LE"), V("PM", 0, 256), MAGIC, OP.is_le)
                acc(V("PM", 256, 512), [(V("BO"), V("LE"))])
                act(V("SB_"), V("PM", 256, 512), AF.Sign, bias=col(11), scale=col(10))
                tt(V("KP"), IND(V("KI"), V("LP", 0, 16)), V("SB_"), OP.mult)
                acc(V("PM", 0, 16), comb("KP", s="S0Q"))
                nodes("N", V("PM", 0, 16))
                act(V("NP"), IND(V("SW", 0, 256), V("puN", 8, 16)), scale=-1.0 / 16)
                acc(V("PM", 16, 24), comb("NP", 0, 128))
                act(V("SP"), V("PM", 16, 24), scale=-4.0)
            scan(V("KS"), V("RB", 0, 256), V("PK", 0, 256), OP.add, OP.min)
            ts(V("K1"), V("KS", 15, 256, 16), MAGIC, OP.add, MAGIC, OP.subtract)
            tt(V("KB", 0, 16), V("KS", 15, 256, 16), V("K1"), OP.subtract)
            lin(V("KB", 16, 32), V("KB", 0, 16), -0.5)
            mm(spread("PV", V("KB", 0, 16), False, True), vid)
            cid = ("C", t, l)
            mm(spread("PK", V("KB", 16, 32), True, False), cid)
            ts(V("PRD"), V("PV", 0, 256), 0.0, OP.max, 4096.0, OP.min)
            acc(V("PK", 0, 256), [(V("BO"), V("PRD"))], False, True, cid)
            acc(V("PV", 256, 272), [(V("ID"), V("M1K"))] + comb("PRD"))
            act(V("CW"), V("PK", 0, 256), bias=-31744.0)
            ts(V("CN", 16, 32), V("PV", 256, 272), 4096 * MAGIC, OP.add, 4096 * MAGIC, OP.subtract)
            tt(V("CN", 0, 16), V("PV", 256, 272), V("CN", 16, 32), OP.subtract)
            ts(V("CU"), V("CN", 0, 16), 1024.0, OP.add)
            lin(V("DA"), V("CN", 0, 16), 1.0 / 128, 8.0)
            act(V("DB"), V("CN", 0, 16), AF.Relu, bias=-16.0 * 1023, scale=16.0)
            lowest("CW", "CN", "c", "PK", 256, TUNE["span"])
            act(V("XC"), IND(XA, V("CU")))
            acc(V("PD0", 0, 256), [(V("H5"), V(cm)), (V("QI"), V("ONE", 0, 256)), (V("H5"), V("XC")), (V("MI"), V("ONE", 0, 256))])
            act(V("NW"), V("PD0", 0, 256), bias=-MAGIC)
            acc(V("PV", 272, 288), [(V("ID"), V("DA")), (V("ID"), V("DB"))] + comb("SGc"))
            tt(V("DL"), V("PV", 272, 288), V("DMX"), OP.min)
            ts(V("XU"), V("DL"), 128.0, OP.mult, float(C), OP.add)
            idle = V("ac" + s)
            act(V("AP_"), idle, bias=V("AC", 0, 1), scale=-2048.0)
            wide = TUNE["wide"][l]
            if lv[0]:
                act(V("NT"), V("NS"), scale=-512.0 if wide else 256.0)
            tt(V("AD", 128, 256), V("RD", 128, 256), nf, OP.is_equal)
            tt(V("BS", 16, 32), V("LF", 0, 16), idle, OP.add)
            if l == 1:
                tt(V("BS", 24, 32), V("BS", 24, 32), V("OK"), OP.max)
            act(V("DT", 16, 24), V("TT", 0, 8), scale=2.0)
            if wide:
                tt(V("LT", 32, 48), V("pr" + s), idle, OP.add)
                tt(V("LT", 0, 16), V("LT", 32, 48), V("DUM", 16, 32), OP.min)
                ts(V("LU", 0, 16), V("LT", 0, 16), 256.0, OP.mult, -128.0, OP.add)
                act(V("AW"), V("ONE", 0, 256), bias=-0.5, scale=V("AC", 0, 1))
            else:
                act(V("BS", 0, 16), V("pr" + s), bias=3.5)

            def signs(lo, hi):
                wid = ("W", t, l, lo)
                acc(V("PD1", lo, hi), [(V("BON"), V("EV", lo, hi)), (V("NG"), V("AW", lo, hi))], True, False, wid)
                acc(V("PD1", lo, hi), [(V("BO"), V("EU", lo, hi))], False, True, wid)
                tt(V("SV", lo, hi), V("PD1", lo, hi), V("NT", lo, hi), OP.mult)
                act(IND(V("SW"), V("LU", lo // 16, hi // 16)), V("SV", lo, hi), AF.Tanh)

            m0 = 0; did = ("D", t, l)
            acc(V("PX", 0, 16), comb("EV", s="S0N"), True, False, did)
            for e in range(8):
                rings("U", e, TUNE["u"][l], XA)
                if e + 1 in (TUNE["cut"][l], 8):
                    lo, hi = 32 * m0, 32 * e + 32
                    middle("U", m0, e + 1, "PB", TUNE["u"][l], cm)
                    act(V("EU", lo, hi), V("PB", lo, hi), AF.Abs, bias=-MAGIC)
                    if wide:
                        signs(lo, hi)
                    m0 = e + 1
            acc(V("PX", 0, 16), comb("EU"), False, True, did)
            r0 = 16 * wide
            for r in range(r0, 32, 16):
                tt(V("EX", r, r + 16), V("PX", 0, 16), V("AP_"), OP.is_lt)
            tt(V("LT", r0, 32), V("EX", r0, 32), V("DT", r0, 32), OP.mult)
            tt(V("LT", 32 + r0, 64), V("LT", r0, 32), V("BS", r0, 32), OP.add)
            tt(V("LT", r0, 32), V("LT", 32 + r0, 64), V("DUM", 32 + r0, 64), OP.min)
            ts(V("LU", r0, 32), V("LT", r0, 32), 256.0, OP.mult)
            if not wide:
                act(IND(V("SW"), V("LU", 0, 16)), V("NT"), AF.Tanh)
            tt(V("RD", 0, 128), IND(RA, V("LU", 16, 24)), V("KE", t, t + 128), OP.mult)
            tt(IND(RA, V("LU", 16, 32)), V("RD"), V("AD"), OP.max)
            for b in range(256, 0, -TUNE["span"]):
                cp(IND(XB, V("XU", (b - TUNE["span"]) // 16, b // 16)), V("NW", b - TUNE["span"], b))
            if l == 1 and not last:
                go = "GO%d" % t; nm = "CM%d" % (t + 1)
                act(V(go), IND(V(xb, p0 - LN, p0), V("SNu")) if t else IND(V(xb, 0, XD), V("FSu")))
                send = ops[add("p", lambda q, T, x, t=t: x["send"](t), [], [V(go)], 1500, sem="loc", n=0, lat=TUNE["far"])]
                lin(V(nm, 0, 16), V(go, 0, 16))
                lin(V(nm, 128, 256), V(xb, p0, p0 + LN))
            if last:
                dma("y", "ox0", lambda T: [(T.yx[:, 0:1024], T.X0[:, 0:1024])], [], [V("X0", 0, 1024)], 3000)
                dma("y", "ox1", lambda T: [(T.yx[:, 1024:2048], T.X0[:, 1024:2048])], [], [V("X0", 1024, 2048)], 3000)
            nx = "N" if l == 0 else "EO"[(t + 1) & 1]
            if not last:
                act(V("NS"), IND(V("SW", 0, 256), V("pu" + nx)), scale=-1.0 / 16)
                lv[0] += 1
                if l == 0 or t == 0:
                    acting(nx)
                places(nx, False)
                acc(V("PM", 32, 48), [(V("BO"), V("EX", 16, 32))])
                act(V("JK"), V("PM", 32, 48), scale=-1.0, total=V("AC", 0, 1))
                if lv[0] == 1:
                    acc(V("PM", 48, 56), comb("FSw", 0, 128))
                    cp(V("FSu"), V("PM", 48, 56))
    act(V("NS"), V("SW", 0, 256), scale=-1.0 / 32)
    acc(V("PX", 16, 32), comb("NS"))
    tt(V("LF", 0, 16), V("PX", 16, 32), V("DUM", 0, 16), OP.add)
    tt(V("LF", 16, 32), V("DUM", 0, 16), V("PX", 16, 32), OP.subtract)
    for h in range(2):
        ts(V("FU", 16 * h, 16 * h + 16), V("LF", 16 * h, 16 * h + 16), 256.0, OP.mult)
        fu = V("FU", 16 * h, 16 * h + 16)
        if h:
            act(V("RO_", 256, 512), IND(V("RW"), fu), scale=float(C))
            act(V("KO", 256, 512), IND(V("KF"), fu))
        else:
            ts(V("RO_", 0, 256), IND(V("RW"), fu), float(C), OP.mult)
            cp(V("KO", 0, 256), IND(V("KF"), fu))
        dma("y", "oyr%d" % h, lambda T, h=h: [(T.yr[:, 256 * h:256 * h + 256], T.RO_[:, 256 * h:256 * h + 256])], [], [V("RO_", 256 * h, 256 * h + 256)], 2300)
    dma("y", "oyk", lambda T: [(T.yk[r:16:2, :], T.KO[r:128:16, :]) for r in range(2)], [], [V("KO")], 2500, 32)
    return ops


PLAN = {}


def kind(o):
    w = o["W"][0] if o["W"] else ("", 0)
    return w[0] + ("b" if w[0] in ("RU", "LF", "LT", "AD", "RD", "DT", "EU", "KB", "CN", "WTT") and w[1] > 0 else "") + ("s" if o["lv"] < 0 else str(o["lv"] % 2))


def schedule(ops):
    n = len(ops); others = []; named = ("F", "G", "S", "PE", "far"); mid = [TUNE[k] for k in named]
    for rates in TUNE["others"] + [mid]:
        TUNE.update(zip(named, rates))
        others.append([(o["c"], o["lat"]) for o in build()])
    others.pop()
    for k, o in enumerate(ops):
        o["k"] = k
    pred = [set() for _ in range(n)]; soft = [set() for _ in range(n)]
    hist = {}
    for k, o in enumerate(ops):
        for x in o["x"]:
            soft[k].add(x["k"])
        for w, vs in ((False, o["R"]), (True, o["W"])):
            for v in vs:
                h = hist.setdefault(v[0], [])
                for (j, lo, hi, wj) in h:
                    if j == k:
                        continue
                    clash = lo < v[2] and v[1] < hi and (w or wj)
                    if v[0] in PS:
                        if ops[j]["e"] != o["e"]:
                            clash = True
                        elif o["e"] == "t":
                            soft[k].add(j)
                            clash = clash and not (o["g"] is not None and o["g"] == ops[j]["g"])
                    if clash:
                        pred[k].add(j)
        for w, vs in ((False, o["R"]), (True, o["W"])):
            for v in vs:
                h = hist[v[0]]
                if w and abs(v[3]) == 1 and len(v) == 4 and v[0] not in PS:
                    h[:] = [e for e in h if not (v[1] <= e[1] and e[2] <= v[2])]
                if v[0] in PS and o["e"] == "t":
                    h[:] = [e for e in h if ops[e[0]]["e"] == "t"][-40:]
                if (k, v[1], v[2], w) not in h[-20:]:
                    h.append((k, v[1], v[2], w))
    allp = [pred[k] | soft[k] for k in range(n)]
    succ = [[] for _ in range(n)]
    for k in range(n):
        for j in allp[k]:
            succ[j].append(k)

    def gap(j, k):
        return ops[j]["lat"] + (TUNE["same"] if ops[j]["e"] == ops[k]["e"] else TUNE["cross"]) * (0 if j not in pred[k] and not ops[j]["lat"] else 1)
    fw = [[(j, gap(k, j)) for j in succ[k]] for k in range(n)]
    eng = [o["e"] for o in ops]; cost0 = [o["c"] for o in ops]; lat = [o["lat"] for o in ops]

    def again(seq, cost):
        ready = [0.0] * n; free = {e: 0.0 for e in "vstpy"}; end = 0.0
        for k in seq:
            e = eng[k]; c, late = cost[k]; f = free[e] = max(ready[k], free[e]) + c; end = max(end, f + late); f += late - lat[k]
            for j, d in fw[k]:
                if f + d > ready[j]:
                    ready[j] = f + d
        return end
    bw = [[(j, gap(j, k)) for j in allp[k]] for k in range(n)]
    z = [TUNE["seed"]]

    def pick(xs):
        z[0] = (z[0] * 6364136223846793005 + 1442695040888963407) % 2 ** 64
        return xs[(z[0] >> 33) % len(xs)]

    every = list(range(n)); worlds = [list(zip(cost0, lat))] + others; kinds = [kind(o) for o in ops]

    def place(order, prv, first):
        fin = {}; used = {e: ([], []) for e in "vstpy"}
        for k in order:
            t = first[k]
            for j, d in prv[k]:
                d += fin[j]
                if d > t:
                    t = d
            s0, s1 = used[eng[k]]; c = cost0[k]; i = m = len(s0)
            while i and s1[i - 1] > t:
                i -= 1
            while i < m and s0[i] < t + c:
                t = s1[i]; i += 1
            s0.insert(i, t); s1.insert(i, t + c); fin[k] = t + c
        return fin

    def improve(seq, a, b, tries):
        win = seq[a:b]; inside = set(win); frames = []
        prv = {k: [e for e in bw[k] if e[0] in inside] for k in win}; nxt = {k: [e for e in fw[k] if e[0] in inside] for k in win}
        for w in worlds:
            fin = {}; free = {}; rest = {}; head = {}; fixed = 0.0
            for k in seq[:a]:
                fin[k] = free[eng[k]] = max([free.get(eng[k], 0.0)] + [fin[j] + d + w[j][1] - lat[j] for j, d in bw[k]]) + w[k][0]
            for k in reversed(seq[b:]):
                rest[k] = head[eng[k]] = max([head.get(eng[k], 0.0), w[k][1]] + [rest[j] + d + w[k][1] - lat[k] for j, d in fw[k]]) + w[k][0]
                fixed = max([fixed] + [fin[j] + d + w[j][1] - lat[j] + rest[k] for j, d in bw[k] if j in fin])
            frames.append(({k: max([free.get(eng[k], 0.0)] + [fin[j] + d + w[j][1] - lat[j] for j, d in bw[k] if j in fin]) for k in win},
                           {k: max([head.get(eng[k], 0.0), w[k][1]] + [rest[j] + d + w[k][1] - lat[k] for j, d in fw[k] if j in rest]) for k in win}, fixed))
        first, after, fixed = frames[0]

        def tried(order):
            fin = place(order, prv, first)
            fin = place(sorted(win, key=lambda k: -fin[k]), nxt, after)
            fin = place(sorted(win, key=lambda k: -fin[k]), prv, first)
            return max(fixed, max(fin[k] + after[k] for k in win)), fin

        def whole(r):
            fin = r[1]; order = sorted(win, key=lambda k: fin[k] - cost0[k]); total = r[0]
            for w, (f0, a0, end) in zip(others, frames[1:]):
                f = {}; free = {}
                for k in order:
                    t = max(f0[k], free.get(eng[k], 0.0))
                    for j, d in prv[k]:
                        d += f[j] + w[j][1] - lat[j]
                        if d > t:
                            t = d
                    f[k] = free[eng[k]] = t = t + w[k][0]
                    if t + a0[k] > end:
                        end = t + a0[k]
                total += end
            before = {}; last = {}
            for k in order:
                before[k] = last.get(eng[k]); last[eng[k]] = k
            k = max(win, key=lambda k: fin[k] + after[k]); held = []
            while True:
                j = before[k]; t = fin[k] - cost0[k] - 0.01
                if j is not None and fin[j] >= t:
                    held.append((j, k))
                else:
                    j = [j for j, d in prv[k] if fin[j] + d >= t]
                    if not j:
                        break
                    j = j[0]
                k = j
            return total, r[0], order, fin, held
        fin = place(win, prv, first)
        best = now = whole((max(fixed, max(fin[k] + after[k] for k in win)), fin)); alike = {}
        for k in win:
            alike.setdefault(kinds[k], []).append(k)
        names = sorted(alike); text = sorted(win)
        for it in range(tries):
            p = {k: now[3][k] - cost0[k] for k in win}; early = pick([0, 1])
            if now[4] and pick(TUNE["ways"]):
                x, y = pick(now[4]); k0 = y if early else x
                d = (p[y] - p[x] + pick([10, 10, 300, 1000, 2000])) * (-1 if early else 1)
                for k in pick([[k0], [k0], alike[kinds[k0]]]):
                    p[k] += d
            else:
                for _ in range(pick([1, 1, 2, 3])):
                    d = pick([-1, 1]) * pick([200, 500, 1000, 2000, 4000])
                    for k in alike[pick(names)]:
                        p[k] += d
            for k in (reversed(text) if early else text):
                for j, d in (nxt[k] if early else prv[k]):
                    if early and p[j] <= p[k]:
                        p[k] = p[j] - 0.001
                    elif not early and p[j] >= p[k]:
                        p[k] = p[j] + 0.001
            slack = TUNE["slack"] * (1 - it / tries) * pick([0, 0.3, 1])
            r = tried(sorted(win, key=lambda k: p[k]))
            if r[0] > now[1] + slack + 300:
                continue
            r = whole(r)
            if r[0] <= now[0] + slack:
                now = r
                if r[0] < best[0]:
                    best = r
        return seq[:a] + best[2] + seq[b:]

    def timed(seq):
        at = [0.0] * n; free = {}
        for k in seq:
            at[k] = max([free.get(eng[k], 0.0)] + [at[j] + cost0[j] + d for j, d in bw[k]]); free[eng[k]] = at[k] + cost0[k]
        return at
    tail = [0.0] * n
    for k in range(n - 1, -1, -1):
        tail[k] = cost0[k] + max([d + tail[j] for j, d in fw[k]] + [lat[k]])
    seq = improve(sorted(every, key=lambda k: -tail[k]), 0, n, TUNE["first"])
    for turn in range(TUNE["turns"]):
        w = TUNE["width"]; a = -(w // 3) * (turn % 3)
        while a < n:
            seq = improve(seq, max(a, 0), min(a + w, n), TUNE["tries"]); at = timed(seq); seq.sort(key=lambda k: at[k]); a += w
    at = timed(seq); best = (0, max(at[k] + cost0[k] + lat[k] for k in every), seq, at)
    PLAN["bw"] = bw; PLAN["all"] = [best[1]] + [again(best[2], c) for c in others]
    end, seq, at = best[1:]
    seq.sort(key=lambda k: at[k])
    for k in range(n):
        ops[k]["t"] = at[k]
    need = set()
    for k in range(n):
        need |= pred[k]
    cnt = {e: 0 for e in "vstpy"}
    for k in seq:
        o = ops[k]
        if o["sem"] is None and k in need:
            cnt[o["e"]] += 1; o["mark"] = ("e" + o["e"], cnt[o["e"]])
        elif o["sem"] in DMAS:
            o["mark"] = (o["sem"], o["n"])
        else:
            o["mark"] = None
    known = {e: {} for e in "vstpy"}; clock = {}
    for k in seq:
        o = ops[k]; kn = known[o["e"]]; waits = []
        for j in sorted(pred[k], key=lambda j: -ops[j]["t"]):
            m = ops[j]["mark"]
            if m is not None and kn.get(m[0], 0) < m[1]:
                waits.append(m)
                for s, c in clock[j].items():
                    kn[s] = max(kn.get(s, 0), c)
        o["waits"] = waits
        clock[k] = dict(kn)
        if o["mark"]:
            clock[k][o["mark"][0]] = o["mark"][1]
    return seq, cnt, end


def bits(es):
    return sum(1 << e for e in es)


def routes(T, topo, r):
    me = T.cores[r]
    near = [d for d in range(1, N) if topo.may_write(me, T.cores[(r + d) % N])]
    far = [d for d in range(1, N) if d not in near]
    able = [c for c in topo.cores_of(me) if c not in T.cores and all(topo.may_write(c, T.cores[(r + d) % N]) for d in far)]
    able.sort(key=lambda c: topo.die(c) != topo.die(me))
    h = (len(far) + 1) // 2
    return near, [(able[0], far[:h]), (able[1], far[h:])]


def shares(es, k):
    out = [es]
    while len(out) < k:
        out.sort(key=len); a = out.pop()
        out += [a[:len(a) // 2], a[len(a) // 2:]]
    return out


def arrivals(T, topo, r):
    tot = 0
    for q in range(N):
        near, helpers = routes(T, topo, q)
        for src, ds in [(T.cores[q], near)] + helpers:
            sh = shares(topo.engines(src, T.cores[(q + ds[0]) % N]), len(ds))
            tot += sum(len(e) for d, e in zip(ds, sh) if (q + d) % N == r)
    return tot


def on_chip(T, topo, r):
    me = T.cores[r]; near, helpers = routes(T, topo, r)
    off = topo.engines(me, T.cores[(r + near[0]) % N])
    return shares([e for e in topo.engines(me, helpers[0][0]) if e not in off], len(helpers))


def forward(g, T, topo, src, r, ds, buf, lo, t):
    sh = shares(topo.engines(src, T.cores[(r + ds[0]) % N]), len(ds)); trs = []
    for k, d in enumerate(ds):
        rid, pid = topo.addr(T.cores[(r + d) % N], src)
        trs.append(RemoteDMATransfer(dst_ids=[DstId(rid=rid, pnc=pid)], dma_engine_mask=bits(sh[k]), remote_sem=T.sem["arr%d" % t],
                                     src=buf[:, lo + 16 * k:lo + 16 * k + 16], dst=T["CM%d" % (t + 1)][:, 16 * d:16 * d + 16]))
    g.remote_dma_fused(trs, local_sem=T.sem["loc"])
    return sum(len(e) for e in sh)


def even_run(ds):
    step = ds[1] - ds[0]
    assert all(b - a == step for a, b in zip(ds, ds[1:]))
    return slice(ds[0], ds[-1] + 1, step)


def rank_program(g, core, T, topo):
    rank = T.rank_of(core)
    if rank is None:
        for r in range(N):
            for k, (h, ds) in enumerate(routes(T, topo, r)[1]):
                if h == core:
                    tot = 0
                    for t in range(RO - 1):
                        g.wait_ge(T.sem["hin%d" % t], len(on_chip(T, topo, r)[k]))
                        tot += forward(g, T, topo, core, r, ds, T["HL%d" % t], 0, t)
                    g.wait_ge(T.sem["loc"], tot)
        return
    if "ops" not in PLAN:
        ops = build()
        PLAN["ops"] = ops; PLAN["s"] = schedule(ops)
    ops = PLAN["ops"]; seq, cnt, end = PLAN["s"]
    near, helpers = routes(T, topo, rank)
    sent = [0]

    def send(t):
        go = T["GO%d" % t]; lo = 16 * (1 + len(near)); trs = []
        for (h, ds), es in zip(helpers, on_chip(T, topo, rank)):
            rid, pid = topo.addr(h, core); w = 16 * len(ds)
            trs.append(RemoteDMATransfer(dst_ids=[DstId(rid=rid, pnc=pid)], dma_engine_mask=bits(es), remote_sem=T.sem["hin%d" % t],
                                         src=go[:, lo:lo + w], dst=T["HL%d" % t][:, 0:w]))
            lo += w; sent[0] += len(es)
        g.remote_dma_fused(trs, local_sem=T.sem["loc"])
        sent[0] += forward(g, T, topo, core, rank, near, go, 16, t)

    k0 = 1 + len(near)
    x = {"runs": [(slice(0, k0), even_run([0] + near)), (slice(k0, N), even_run([d for h, ds in helpers for d in ds]))], "send": send}
    qs = {"v": g.vector, "s": g.scalar, "t": g.tensor, "p": g, "y": g.sync}
    come = arrivals(T, topo, rank); seen = set()
    for k in seq:
        o = ops[k]; q = qs[o["e"]]
        if o["pre"] and o["pre"] not in seen:
            seen.add(o["pre"]); q.wait_ge(T.sem[o["pre"]], come)
        for s, c in o["waits"]:
            q.wait_ge(T.sem[s], c)
        i = o["f"](q, T, x)
        if o["sem"] is None and o["mark"]:
            i.then_inc(T.sem[o["mark"][0]], 1)
    for e in "vstp":
        if cnt[e]:
            g.sync.wait_ge(T.sem["e" + e], cnt[e])
    for s, c in {o["sem"]: o["n"] for o in ops if o["sem"] in DMAS}.items():
        g.sync.wait_ge(T.sem[s], c)
    g.wait_ge(T.sem["loc"], sent[0])
